import numpy as np, ml_dtypes
CORES = [16,18,20,22]
N = 4
BF = ml_dtypes.bfloat16
W, P, RO, L = 3072, 1, 6, 256
Q = 1.0
def parts(rng):
    share = rng.choice(np.array([0.015, 0.025, 0.04]), (N, 8, 1, 1)) * Q
    r = np.where(rng.random((N, 8, 16, W)) < share, rng.integers(5, 16, (N, 8, 16, W)), rng.integers(0, 5, (N, 8, 16, W)))
    hot = (rng.random((N, 8, 1, W)) < 0.004 * Q) & (rng.random((N, 8, 16, W)) < 0.7)
    r = np.where(hot, 15, r)
    return r, rng.integers(0, 256, (N, 8, 16, W)), rng.integers(0, W, (N, 8, 16, W)), rng.integers(0, W, (N, 8, 16, L))
def pack(r, x, k, s):
    return {"rec": np.ascontiguousarray(r.reshape(N, 128, W)).astype(np.float32).astype(BF), "wealth": np.ascontiguousarray(x.reshape(N, 128, W)).astype(np.float32).astype(BF),
            "kin": np.ascontiguousarray(k.reshape(N, 128, W)).astype(np.int32), "slips": np.ascontiguousarray(s.reshape(N, 128, L)).astype(np.int32)}
def setup_inputs(rng):
    r, x, k, s = parts(rng)
    return pack(r, x, k, s)
def setup_inputs_spread(rng):
    e = np.exp2(4.3 + 3.9 * rng.random((N, 8, 16, 1))) / Q
    r = np.minimum((16 * rng.random((N, 8, 16, W)) ** e).astype(np.int64), 15)
    x = np.minimum((np.exp2(8 * rng.random((N, 8, 1, W))) * rng.random((N, 8, 16, W))).astype(np.int64), 255)
    k = np.minimum((W * rng.random((N, 8, 16, W)) ** 2).astype(np.int64), W - 1)
    s = np.minimum((W * rng.random((N, 8, 16, L)) ** (1 + rng.random((N, 8, 1, L)))).astype(np.int64), W - 1)
    return pack(r, x, k, s)
def setup_inputs_ends(rng):
    r = 15 * (rng.random((N, 8, 16, W)) < 0.02 * Q)
    r = np.where(rng.random((N, 8, 1, W)) < 0.004 * Q, 15, r)
    w = rng.random((N, 8, 1, W)); x = 255 * np.where(w < 0.4, 0, np.where(w < 0.7, 1, rng.integers(0, 2, (N, 8, 16, W))))
    u = rng.random((N, 8, 16, W))
    k = np.where(u < 0.36, 0, np.where(u < 0.72, W - 1, np.where(u < 0.78, W - 2, rng.integers(0, W, (N, 8, 16, W)))))
    for first, places in ((1, ((2, W - 2), (15, W - 1))), (3, ((4, W - 1), (9, 5), (12, 5))), (6, ((4, 5), (9, W - 1)))):
        c = np.zeros((16, 1), np.int64)
        for m, v in places: c[m, 0] = v
        k[:, :, :, first::8] = c; x[:, :, :, first::8] = 0
    m = (np.arange(W) & 4) == 4
    k[:, 7] = np.where(m & (k[:, 7] == W - 1), 0, k[:, 7])
    a, b = W - 600, W - 344
    k[:, :, :, a:b] = 0; r[:, :, :, a:b] = 0; x[:, :, :, a:b] = 0
    k[:, :, :, W - 40:W - 24] = 0; r[:, :, :, W - 40:W - 24] = 0; x[:, :, :, W - 40:W - 24] = 0; k[:, :, 15, W - 32:W - 24] = W - 1
    r[:, :, :, 0] = 0; r[:, :, :, W - 1] = 15 * (rng.random((N, 8, 16)) < rng.choice(np.array([0.05, 0.15, 0.3]), (N, 8, 1))); r[:, 7, :, W - 1] = 15
    r[:, :, :, W - 2] = 0; r[:, :, :, 5] = 0
    x[:, :, :, 0] = 0; x[:, :, :, W - 1] = 255; x[:, :, :, 5] = 255; x[:, :, :, W - 2] = 255; x[:, :, 15, W - 2] = 254
    u = rng.random((N, 8, 16, L)); s = np.where(u < 0.35, 0, np.where(u < 0.7, W - 1, rng.integers(1, W - 600, (N, 8, 16, L))))
    s[:, :, :, 112:128] = W - 1
    for q in range(2):
        for g in range(8): s[q, g, :, 240:] = a + rng.permutation(256).reshape(16, 16)
    p = np.arange(16); s[N - 1, 7, :, 255] = np.where((p & 1) == 0, W - 40 + (p >> 1), W - 32 + (p >> 1))
    return pack(r, x, k, s)
def setup_inputs_corners(rng):
    r, x, k, s = parts(rng); own = np.arange(W); lane = np.arange(L)
    k[:, :4] = own
    n = rng.choice(np.array([0, 1, 3, 7, 8, 9, 11, 12, 13, 16]), (1, 4, 1, W)); order = np.argsort(rng.random((1, 4, 16, W)), axis=2)
    high = np.where(rng.random((N, 4, 16, W)) < 0.7, 15, rng.integers(6, 16, (N, 4, 16, W)))
    low = np.where(rng.random((N, 4, 16, W)) < 0.15, 5, rng.integers(0, 5, (N, 4, 16, W)))
    high[:, 1] = 6; low[:, 1] = 5; high[:, 2] = 6 + (own & 7); low[:, 2] = 5 + (own & 7)
    r[:, :4] = np.where(order < n, high, low)
    s[:, :2] = lane + 256 * rng.integers(0, W // 256, (N, 2, 16, L))
    s[:, 4] = np.repeat(rng.integers(0, W, (N, 1, 16)), 16, axis=2)
    for q in range(N):
        if (q & 1) == 0: s[q, 5] = rng.integers(0, W)
        else: s[q, 5] = lane + 256 * rng.integers(0, W // 256, (16, L))
    k[:, 6] = rng.choice(np.array([0, W - 1, W // 2]), (N, 1, W))
    z = rng.integers(0, 3, (N, 16, W)); k[:, 7] = np.where(z == 0, 0, np.where(z == 1, W - 1, own))
    r[:, 6:, :, [0, W - 1, W // 2]] = np.where(rng.random((N, 2, 16, 3)) < 0.2, 15, rng.integers(0, 5, (N, 2, 16, 3)))
    s[:, 7] = np.where(rng.random((N, 16, L)) < 0.1, rng.choice(np.array([0, W - 1]), (N, 16, L)), s[:, 7])
    x[:, 1] = 255; x[:, 2] = 255 * rng.integers(0, 2, (N, 1, W))
    return pack(r, x, k, s)
def setup_inputs_alike(rng):
    r, x, k, s = parts(rng)
    pool = np.repeat(rng.integers(0, W, (N, 8, 16, 6)), 16, axis=2)
    few = np.take_along_axis(pool, rng.integers(0, 6, (N, 8, L, 16)), 3).transpose(0, 1, 3, 2)
    s[:, ::2] = few[:, ::2]
    s[:, 1::4, :, 1::2] = np.roll(s[:, 1::4, :, 0::2], 5, axis=2)
    s[:, 3] = W - 1 - rng.integers(0, 40, (N, 16, L))
    k[:, 1::2, 8:] = k[:, 1::2, :8]
    x = np.take_along_axis(rng.choice(np.array([0, 128, 255]), (N, 8, 16, 5)), rng.integers(0, 5, (N, 8, 1, W)), 3)
    return pack(r, x, k, s)
def setup_inputs_full(rng):
    r, x, k, s = parts(rng); own = np.arange(W); lane = np.arange(L); bag = (own >> 4) & 15
    z = 2 * rng.integers(0, 8, N) + 1
    r[:, :3] = rng.integers(0, 5, (N, 3, 16, W))
    even = own[(own & 16) == 0]; r[:, 1, bag[even], even] = 15; k[:, 1] = k[:, 1] | 16
    hot = np.repeat((bag[None, :] == z[:, None])[:, None, :], 8, axis=1)
    hot[:, :2, :256] = False; hot[:, 2, :256:2] = False
    r = np.where(hot[:, :, None, :], 15, r)
    named = np.take_along_axis(hot, k.reshape(N, 8, 16 * W), 2).reshape(N, 8, 16, W); k = np.where(named, k ^ 32, k)
    s[:, :3] = lane + 256 * rng.integers(0, W // 256, (N, 3, 16, L))
    inbag = (lane >> 4)[None, :] == z[:, None]
    first = np.arange(16)[:, None] == ((5 * (lane & 15)) & 15)[None, :]
    s = np.where(inbag[:, None, None, :], lane + 256 * np.where(first, 0, rng.integers(1, W // 256, (N, 8, 16, L))), s)
    return pack(r, x, k, s)
def check_inputs(d):
    bad = []
    for k, lo, hi in (("rec", 0, 15), ("wealth", 0, 255), ("kin", 0, W - 1), ("slips", 0, W - 1)):
        v = np.asarray(d[k]).astype(np.float64)
        if not (np.min(v) >= lo and np.max(v) <= hi): bad.append("range of " + k)
        elif np.any(v != np.floor(v)): bad.append("whole numbers of " + k)
    return bad
def reference(rec, wealth, kin, slips):
    R = rec.astype(np.float32).astype(np.int64).reshape(N, 8, 16, W); X = wealth.astype(np.float32).astype(np.int64).reshape(N, 8, 16, W)
    K = kin.astype(np.int64).reshape(N, 8, 16, W); S = slips.astype(np.int64).reshape(N, 8, 16, L)
    lane = np.arange(L); b = lane >> 4; j = lane & 15; a = np.zeros((N, 16), np.int64)
    lower = lane[None, :] < lane[:, None]
    def picks(tab, ks):
        return np.take_along_axis(tab, ks.reshape(8, 1, 16 * L), 2).reshape(8, 16, 16, L)
    for t in range(RO):
        T = 8 + t; later = []
        for r in range(N):
            o = (a[r][b] + 5 * j + t) & 15
            c = S[r][:, o, lane]
            ci = c[:, None, :]
            counts = ~np.any((c[:, :, None] == c[:, None, :]) & lower[None], axis=2)
            kc = np.take_along_axis(K[r], ci, 2)
            M = np.maximum(np.take_along_axis(R[r], ci, 2), np.max(picks(R[r], kc), axis=2))
            for u in range(P):
                q = (r + 1 + (P * t + u) % (N - 1)) % N
                M = np.maximum(M, np.max(picks(R[q], np.take_along_axis(K[q], ci, 2)), axis=2))
            f = np.sum(M >= T - 2, axis=1)
            bar = (M[:, b, lane] >= T - 3) | (f >= 8)
            barred = counts & bar; inst = counts & ~bar
            torn = inst | (barred & (f >= 12))
            nxt = np.zeros((8, L), bool); nxt[:, :L - 16] = torn[:, 16:]
            moved = barred & (f < 12) & ((f & 1) == 1) & nxt
            sc = np.sum(np.maximum(picks(X[r], kc) - np.take_along_axis(X[r], ci, 2)[:, :, None, :], 0), axis=1)
            best = np.take_along_axis(kc, np.argmax(sc, axis=1)[:, None, :], 1)[:, 0]
            new = np.where(torn | moved, best, c)
            new[:, 16:] = np.where(moved[:, :L - 16], c[:, :L - 16], new[:, 16:])
            later.append((o, c, inst, new))
        for r in range(N):
            o, c, inst, new = later[r]
            S[r][:, o, lane] = new
            gi, li = np.nonzero(inst)
            R[r][gi, b[li], c[gi, li]] = T
            K[r][gi, t, c[gi, li]] = c[gi, li ^ 1]
            a[r] = np.sum(inst.reshape(8, 16, 16), axis=(0, 2))
    return {"yr": R.reshape(N, 128, W).astype(np.float32).astype(BF), "ys": S.reshape(N, 128, L).astype(np.float32)}

@@ -1,0 +1,454 @@
+import math
+from concourse.mybir import AluOpType as A
+from concourse.mybir import ActivationFunctionType as F
+from concourse.mybir import AxisListType
+
+RO = 6
+WV = 4
+KS = 2
+EQ1 = 4
+NV = 32
+W = 3072
+WD = W + 256
+BASE = 1.75
+XB = [256 * b - 8 * b * (b - 1) for b in range(17)]
+
+SCRATCH = {}
+
+
+def _bufs(where, n, dtype, names):
+    for k in names.split():
+        SCRATCH[k] = (where, [128, n], dtype)
+
+
+_bufs("sbuf", W, "bfloat16", "recs Wt")
+_bufs("sbuf", W, "int32", "kinI")
+_bufs("sbuf", W, "float32", "IOTA")
+_bufs("sbuf", WD, "bfloat16", "E")
+_bufs("sbuf", WD, "float32", "K")
+_bufs("sbuf", 4096, "bfloat16", "GE FE X")
+_bufs("sbuf", XB[16], "bfloat16", "EQT")
+_bufs("sbuf", 512, "float32", "Z ZT kc2 kTr")
+_bufs("sbuf", 256, "int32", "slI rI rJ rB")
+_bufs("sbuf", 256, "uint16", "kcu fku kTu cbu")
+_bufs("sbuf", 256, "float32", "kcf kcm cXm Pm DB THR riF tq")
+_bufs("sbuf", 512, "bfloat16", "wc DT DBt")
+_bufs("sbuf", 128, "float32", "S1s t1 IDf NEG PX SW")
+_bufs("sbuf", 256, "bfloat16", "Ec X1 X2 TIE cb")
+_bufs("sbuf", 16, "int32", "bI bI2 z4 zy od")
+_bufs("sbuf", 16, "uint16", "mu SL cTs LQ LP")
+_bufs("sbuf", 16, "float32", "cs cTf cTg m1 m2 zc b3 tn mv0 mv tm u1 v1 nT lane dm wcol Dg OH")
+_bufs("sbuf", 16, "bfloat16", "a1")
+_bufs("sbuf", 32, "uint16", "L1 L2 LZ")
+_bufs("sbuf", 32, "int32", "rH")
+_bufs("sbuf", 64, "float32", "t2")
+_bufs("sbuf", 32 * RO, "float32", "um")
+_bufs("sbuf", 128, "bfloat16", "BO ID ON")
+_bufs("sbuf", 144, "bfloat16", "Q16 Q1 Q32 QS")
+_bufs("sbuf", 144, "float32", "Q1f")
+_bufs("sbuf", 1, "int32", "pI xI gI hI oI uk")
+_bufs("sbuf", 1, "float32", "pF xF gF hF oF colA colB colC colD colE colF colG")
+_bufs("sbuf", 8, "float32", "eb Ne Nn")
+_bufs("sbuf", 2, "uint16", "of0 of1")
+_bufs("psum", 512, "float32", "pES pFS pEQ pS1 pZ pU pB pX")
+_bufs("sbuf", 16 * RO, "uint16", "cTu ql")
+_bufs("sbuf", 256 * RO, "bfloat16", "fs rl")
+SEMAPHORES = ["sv", "ss", "sp", "sg", "ls", "dsl", "dsh", "dun", "dys", "dw"] + ["dk%d" % i for i in range(4)] + ["dr%d" % i for i in range(2)] + ["dy%d" % i for i in range(4)] \
+    + ["qa%d" % t for t in range(RO)] + ["ra%d" % t for t in range(RO)]
+
+
+def rank_program(g, core, T, topo):
+    rank = T.rank_of(core)
+    if rank is None:
+        return
+    sem = T.sem
+    ENG = {"V": g.vector, "S": g.scalar, "P": g.tensor, "G": g, "Y": g.sync}
+    SEM = {"V": "sv", "S": "ss", "P": "sp", "G": "sg"}
+    cnt = {}
+    clock = {"V": {}, "S": {}, "P": {}, "G": {}, "Y": {}}
+    snap = {}
+    lastw = {}
+    lastr = {}
+
+    def dep(q, r, w):
+        need = {}
+
+        def add(tok, war):
+            s, n = tok
+            if war and q == "P" and s == "sp":
+                return
+            if need.get(s, 0) < n:
+                need[s] = n
+        for k in r:
+            if k in lastw:
+                add(lastw[k], False)
+        for k in w:
+            if k in lastw:
+                add(lastw[k], True)
+            for s, n in lastr.get(k, {}).items():
+                add((s, n), True)
+        ck = clock[q]
+        for s in sorted(need, key=lambda s: -len(snap.get((s, need[s]), {}))):
+            n = need[s]
+            if ck.get(s, 0) < n:
+                ENG[q].wait_ge(sem[s], n)
+                ck[s] = n
+                for s2, n2 in snap.get((s, n), {}).items():
+                    if ck.get(s2, 0) < n2:
+                        ck[s2] = n2
+
+    def mark(q, tok, r, w):
+        snap[tok] = dict(clock[q])
+        for k in w:
+            lastw[k] = tok
+            lastr[k] = {}
+        for k in r:
+            d = lastr.setdefault(k, {})
+            if d.get(tok[0], 0) < tok[1]:
+                d[tok[0]] = tok[1]
+
+    def op(q, fn, w, r):
+        w, r = w.split(), r.split()
+        dep(q, r, w)
+        s = SEM[q]
+        fn().then_inc(sem[s], 1)
+        cnt[s] = cnt.get(s, 0) + 1
+        mark(q, (s, cnt[s]), r, w)
+
+    def dmas(q, pairs, s, w, r):
+        w, r = w.split(), r.split()
+        dep(q, r, w)
+        for o, i in pairs:
+            ENG[q].dma_start(o, i).then_inc(sem[s], 16)
+            cnt[s] = cnt.get(s, 0) + 16
+        mark(q, (s, cnt[s]), r, w)
+
+    def ts(w, r, out, in0, s1, s2, op0, op1=None):
+        if op1 is None:
+            op("V", lambda: g.vector.tensor_scalar(out, in0, s1, None, op0), w, r)
+        else:
+            op("V", lambda: g.vector.tensor_scalar(out, in0, s1, s2, op0, op1), w, r)
+
+    def tt(w, r, out, a, b, o):
+        op("V", lambda: g.vector.tensor_tensor(out, a, b, o), w, r)
+
+    def cp(w, r, out, in_):
+        op("V", lambda: g.vector.tensor_copy(out, in_), w, r)
+
+    def fill(w, ap, v):
+        op("V", lambda: g.vector.memset(ap, v), w, "")
+
+    def vtr(w, r, out, in_):
+        op("V", lambda: g.vector.transpose(out, in_), w, r)
+
+    def act(w, r, out, in_, f=F.Copy, bias=0.0, scale=1.0):
+        op("S", lambda: g.scalar.activation(out, in_, f, bias=bias, scale=scale), w, r)
+
+    def mm(w, r, out, l, x, st, sp):
+        op("P", lambda: g.tensor.matmul(out, l, x, st, sp), w, r)
+
+    dmas("Y", [(T.slI[:], T.slips[:])], "dsl", "slI", "")
+    for i in range(4):
+        a, b = 768 * i, 768 * (i + 1)
+        dmas("Y" if i < 2 else "S", [(T.kinI[:, a:b], T.kin[:, a:b])], "dk%d" % i, "kinI%d" % i, "")
+
+    op("G", lambda: g.iota(T.pI[:], [[0, 1]], 0, 1), "pI", "")
+    op("G", lambda: g.iota(T.rI[:], [[1, 256]], 0, 0), "rI", "")
+    op("G", lambda: g.iota(T.IOTA[:], [[1, W]], 0, 0, allow_small_or_imprecise_dtypes=True), "IOTA", "")
+    SH, AND = A.arith_shift_right, A.bitwise_and
+    fill("eb", T.eb[:, 2:3], -48.0 * math.log(2.0))
+    ts("xI", "pI", T.xI[:], T.pI[:], 15, None, AND)
+    ts("hI", "pI", T.hI[:], T.pI[:], 16, None, AND)
+    ts("rH", "rI", T.rH[:], T.rI[:, 0:32], 1, None, SH)
+    ts("rJ", "rI", T.rJ[:], T.rI[:], 15, None, AND)
+    cp("xF", "xI", T.xF[:], T.xI[:])
+    cp("hF", "hI", T.hF[:], T.hI[:])
+    ts("colA", "xF hF", T.colA[:], T.xF[:], 32.0, T.hF[:], A.mult, A.add)
+    ts("L1", "rH xF", T.L1[:], T.rH[:], 16.0, T.xF[:], A.mult, A.add)
+    ts("LZ", "rJ colA", T.LZ[:], T.rJ[:, 0:32], T.colA[:], None, A.add)
+    cp("of0", "xF", T.of0[:, 0:1], T.xF[:])
+    cp("kc2", "slI L1", T.kc2[:], T.slI[:].indirect(T.L1[:, 0:32]))
+    vtr("kTa kTb", "kc2", T.kTr[:], T.kc2[:])
+    cp("ZT", "kTa kTb LZ", T.ZT[:], T.kTr[:].indirect(T.LZ[:, 0:32]))
+    dmas("Y", [(T.Z[j::16, 0:256], T.ZT[j::16, 16 * (5 * j % 16):16 * (5 * j % 16) + 256]) for j in range(16)], "dsh", "Z", "ZT")
+    for i in range(2):
+        a, b = 1536 * i, 1536 * (i + 1)
+        dmas("Y", [(T.recs[:, a:b], T.rec[:, a:b])], "dr%d" % i, "recs%d" % i, "")
+    dmas("Y", [(T.Wt[:], T.wealth[:])], "dw", "Wt", "")
+    fill("Ed", T.E[:, W:WD], 0.0)
+    fill("Kd", T.K[:, W:WD], 0.0)
+    ts("rB", "rI", T.rB[:], T.rI[:], 4, None, SH)
+    ts("gI", "pI", T.gI[:], T.pI[:], 4, None, SH)
+    cp("pF", "pI", T.pF[:], T.pI[:])
+    cp("gF", "gI", T.gF[:], T.gI[:])
+    ts("ID", "rI pF", T.ID[:], T.rI[:, 0:128], T.pF[:], None, A.is_equal)
+    ts("colG", "hF pF", T.colG[:], T.hF[:], -2.0, T.pF[:], A.mult, A.add)
+    ts("colG", "colG", T.colG[:], T.colG[:], 16.0, None, A.add)
+    ts("SW", "rI colG", T.SW[:], T.rI[:, 0:128], T.colG[:], None, A.is_equal)
+    ts("oI", "pI", T.oI[:], T.pI[:], 1, None, AND)
+    cp("oF", "oI", T.oF[:], T.oI[:])
+    ts("gI", "hI", T.gI[:], T.hI[:], 4, None, SH)
+    tt("colF", "oF gI", T.colF[:], T.oF[:], T.gI[:], A.not_equal)
+    ts("xI", "xI", T.xI[:], T.xI[:], 1, None, SH)
+    ts("colE", "xI hF", T.colE[:], T.xI[:], 32.0, T.hF[:], A.mult, A.add)
+    ts("colF", "colF colE", T.colF[:], T.colF[:], 256.0, T.colE[:], A.mult, A.add)
+    ts("LP", "rI colF", T.LP[:], T.rI[:, 0:16], T.colF[:], None, A.add)
+    LB = math.log(BASE)
+    ts("colC", "xF", T.colC[:], T.xF[:], 16.0, None, A.mult)
+    ts("colD", "gF", T.colD[:], T.gF[:], 16.0, 15.0, A.mult, A.add)
+    tt("colB", "xF hF", T.colB[:], T.xF[:], T.hF[:], A.add)
+    ts("lane", "rI xF", T.lane[:], T.rI[:, 0:16], 16.0, T.xF[:], A.mult, A.add)
+    fill("eb0", T.eb[:, 0:1], 71.0)
+    fill("eb1", T.eb[:, 1:2], 71.0 + math.log(2.53))
+    cp("riF", "rI", T.riF[:], T.rI[:])
+    act("wcol", "lane eb0", T.wcol[:], T.lane[:], F.Exp, bias=T.eb[:, 0:1], scale=-LB)
+    act("THR", "riF eb1", T.THR[:], T.riF[:], F.Exp, bias=T.eb[:, 1:2], scale=-LB)
+    ts("Q16", "rI colD", T.Q16[:], T.rI[:, 0:144], T.colD[:], 16.0, A.is_equal, A.mult)
+    ts("Q1", "rI colD", T.Q1[:], T.rI[:, 0:144], T.colD[:], None, A.is_equal)
+    ts("Q32", "rI colD", T.Q32[:], T.rI[:, 0:144], T.colD[:], 32.0, A.is_equal, A.mult)
+    ts("QS", "rI colD", T.QS[:], T.rI[:, 0:144], T.colD[:], 1.0 / 16.0, A.is_equal, A.mult)
+    ts("Q1f", "rI colD", T.Q1f[:], T.rI[:, 0:144], T.colD[:], None, A.is_equal)
+    ts("BO", "rB gF", T.BO[:], T.rB[:, 0:128], T.gF[:], None, A.is_equal)
+    ts("TIE", "rB", T.TIE[:], T.rB[:], -1.0, 15.0, A.mult, A.add)
+    ts("DB", "rB xF", T.DB[:], T.rB[:], T.xF[:], None, A.is_equal)
+    for i in range(4):
+        a, b = 768 * i, 768 * (i + 1)
+        cp("K%d" % i, "kinI%d" % i, T.K[:, a:b], T.kinI[:, a:b])
+    KK = "K0 K1 K2 K3 Kd"
+
+    def records():
+        for i in range(2):
+            a, b = 1536 * i, 1536 * (i + 1)
+            act("E", "recs%d eb" % i, T.E[:, a:b], T.recs[:, a:b], F.Exp, bias=T.eb[:, 2:3], scale=6.0 * math.log(2.0))
+
+    def later_constants():
+        ts("dm", "lane", T.dm[:], T.lane[:], float(W), None, A.add)
+        ts("IDf", "rI pF", T.IDf[:], T.rI[:, 0:128], T.pF[:], None, A.is_equal)
+        ts("NEG", "rI pF", T.NEG[:], T.rI[:, 0:128], T.pF[:], -1.0, A.is_equal, A.mult)
+        for t in range(1, RO):
+            ts("um1", "colC", T.um[:, 32 * t + 16:32 * t + 17], T.colC[:], 1.0 / 16.0, 16.0 * t, A.mult, A.add)
+        ts("riF", "DB", T.riF[:], T.DB[:], -1e20, 1e20, A.mult, A.add)
+        ts("tq", "DB", T.tq[:], T.DB[:], 0.9 * 64.0 ** -3, None, A.mult)
+        ts("colE", "xF", T.colE[:], T.xF[:], -1.0, 15.0, A.mult, A.add)
+        ts("colF", "oF pF", T.colF[:], T.oF[:], -2.0, T.pF[:], A.mult, A.add)
+        tt("DT0", "tq riF", T.DT[:, 0:256], T.tq[:], T.riF[:], A.max)
+        ts("OH", "rI colE", T.OH[:], T.rI[:, 0:16], T.colE[:], None, A.is_equal)
+        ts("colF", "colF", T.colF[:], T.colF[:], 1.0, None, A.add)
+        ts("Dg", "rI xF", T.Dg[:], T.rI[:, 0:16], T.xF[:], 16.0, A.is_equal, A.mult)
+        ts("PX", "rI colF", T.PX[:], T.rI[:, 0:128], T.colF[:], None, A.is_equal)
+        ts("Ne", "rI xF", T.Ne[:, 0:RO], T.rI[:, 0:RO], T.xF[:], None, A.is_equal)
+        ts("Nn", "rI xF", T.Nn[:, 0:RO], T.rI[:, 0:RO], T.xF[:], None, A.not_equal)
+        ts("LQ", "rI colB", T.LQ[:], T.rI[:, 0:16], 32.0, T.colB[:], A.mult, A.add)
+        ts("L2", "rH colC", T.L2[:], T.rH[:], T.colC[:], None, A.add)
+        fill("ON", T.ON[:], 1.0)
+        fill("mv", T.mv[:], 0.0)
+
+    def remote(dst, out, in_, rs, r):
+        eng = topo.engines(core, dst)[::2]
+        m = 0
+        for e in eng:
+            m |= 1 << e
+        rid, pid, _ = topo.addr(dst)
+        dep("G", r.split(), [])
+        g.remote_dma(out, in_, sem[rs], sem.ls, pid, rid, m)
+        cnt["ls"] = cnt.get("ls", 0) + len(eng)
+        return len(eng)
+
+    OF = (T.of0, T.of1)
+
+    def draw(t):
+        cp("cTu%d" % t, "Z of%d" % (t % 2), T.cTu[:, 16 * t:16 * t + 16], T.Z[:, 0:256].indirect(OF[t % 2][:, 0:1]))
+
+    ident = T.ID[:]
+    Ew, Kw, Ww, Iw = T.E[:, 0:W], T.K[:, 0:W], T.Wt[:], T.IOTA[:]
+
+    def gather_e(eng, dst, dk, lst, lk, a, n):
+        out, in_ = dst[:, 16 * a:16 * (a + n)], Ew.indirect(lst[:, a:a + n])
+        if eng == "S":
+            act(dk, "E " + lk, out, in_)
+        else:
+            cp(dk, "E " + lk, out, in_)
+
+    def sum_e(ps, pk, dst, dk, a, n, st, sp):
+        for m in range(16):
+            mm(pk, dk + " ID", ps[:, a:a + n], ident, dst[:, 16 * a + m:16 * (a + n):16], st and m == 0, sp and m == 15)
+
+    draw(0)
+    for t in range(RO):
+        asked = T.cores[(rank + 1 + t % 3) % 4]
+        asker = T.cores[(rank - 1 - t % 3) % 4]
+        cu = T.cTu[:, 16 * t:16 * t + 16]
+        cuk = "cTu%d" % t
+        cfk, cf = ("cTf", T.cTf) if t % 2 == 0 else ("cTg", T.cTg)
+        last = t == RO - 1
+        u = 32 * (t + 1)
+        dtk, dt_ = "DT%d" % (t % 2), T.DT[:, 256 * (t % 2):256 * (t % 2) + 256]
+        ne = remote(asked, T.ql[:, 16 * t:16 * t + 16], cu, "qa%d" % t, cuk)
+        lastw["ql%d" % t] = ("qa%d" % t, ne)
+        lastw["rl%d" % t] = ("ra%d" % t, ne)
+        act(cfk, "Z of%d" % (t % 2), cf[:], T.Z[:, 0:256].indirect(OF[t % 2][:, 0:1]))
+        act("kcf", KK + " " + cuk, T.kcf[:], Kw.indirect(cu))
+
+        def own_wealth():
+            act("wc", "Wt " + cuk, T.wc[:, 0:256], Ww.indirect(cu))
+            act("wcb", "Wt " + cuk, T.wc[:, 256:512], Ww.indirect(cu))
+        if t == 0:
+            records()
+        else:
+            own_wealth()
+            tt("E Ed", "Ec DBt SL", T.E[:].indirect(T.SL[:]), T.Ec[:], T.DBt[:, 0:256], A.add)
+        cp("kcu", "kcf", T.kcu[:], T.kcf[:])
+        act("Ec", "E " + cuk, T.Ec[:], Ew.indirect(cu))
+        vtr("kTa", "kcf", T.kTr[:, 0:256], T.kcf[:])
+        mm("pX", "kTa SW", T.pX[:, 0:256], T.SW[:], T.kTr[:, 0:256], True, True)
+        act("kTb", "pX", T.kTr[:, 256:512], T.pX[:, 0:256])
+        cp("cbu", "IOTA " + cuk, T.cbu[:], Iw.indirect(cu))
+        gather_e("S", T.GE, "GE0", T.kcu, "kcu", 0, 64)
+        if t == 0:
+            own_wealth()
+            later_constants()
+        mm("pES", "Ec ID", T.pES[:, 0:256], ident, T.Ec[:], True, False)
+        sum_e(T.pES, "pES", T.GE, "GE0", 0, 64, False, False)
+
+        def equal(b):
+            o, n = XB[b], 256 - 16 * b
+            ts("EQT%d" % b, "cbu wcol " + cfk, T.EQT[:, o:o + n], T.cbu[:, 16 * b:256], cf[:, b:b + 1], T.wcol[:, b:b + 1], A.is_equal, A.mult)
+
+        def equal_sum(b):
+            o, n = XB[b], 256 - 16 * b
+            mm("pEQ", "EQT%d BO" % b, T.pEQ[:, 16 * b:256], T.BO[:], T.EQT[:, o:o + n], b == 0, b == 15)
+
+        def wealth(m):
+            tt("X%d" % m, "Wt kTu wc wcb", T.X[:, 512 * m:512 * m + 512], Ww.indirect(T.kTu[:, 32 * m:32 * m + 32]), T.wc[:], A.max)
+
+        def score(h):
+            mm("pS1", "TIE ID", T.pS1[:, 128 * h:128 * h + 128], ident, T.TIE[:, 128 * h:128 * h + 128], True, False)
+            xs = " ".join("X%d" % m for m in range(4 * h, 4 * h + 4))
+            for j in range(16):
+                mm("pS1", xs + " Q16", T.pS1[:, 128 * h:128 * h + 128], T.Q16[:, 15 - j:143 - j], T.X[:, 2048 * h + j:2048 * h + 2048:16], False, j == 15)
+        for b in range(EQ1):
+            equal(b)
+        cp("kTu", "kTa kTb LP", T.kTu[:], T.kTr[:].indirect(T.LP[:]))
+        cp("fku", KK + " ql%d" % t, T.fku[:], Kw.indirect(T.ql[:, 16 * t:16 * t + 16]))
+        for m in range(WV):
+            wealth(m)
+        gather_e("V", T.FE, "FE3", T.fku, "fku", 192, 64)
+        for m in range(WV, 8):
+            wealth(m)
+        for b in range(EQ1):
+            equal_sum(b)
+        for k in range(3):
+            gather_e("S", T.FE, "FE%d" % k, T.fku, "fku", 64 * k, 64)
+        for k in range(4):
+            if k == KS:
+                score(0)
+            p = (0, 1, 3, 2)[k]
+            sum_e(T.pFS, "pFS", T.FE, "FE%d" % p, 64 * p, 64, True, True)
+        gather_e("S", T.GE, "GE1", T.kcu, "kcu", 64, 32)
+        fs = T.fs[:, 256 * t:256 * t + 256]
+        act("fs%d" % t, "pFS", fs, T.pFS[:, 0:256])
+        remote(asker, T.rl[:, 256 * t:256 * t + 256], fs, "ra%d" % t, "fs%d" % t)
+        score(1)
+        gather_e("S", T.GE, "GE1b", T.kcu, "kcu", 96, 32)
+        gather_e("S", T.GE, "GE2", T.kcu, "kcu", 128, 64)
+        act("S1s", "pS1", T.S1s[:], T.pS1[:, 128:256])
+        if NV < 64:
+            gather_e("S", T.GE, "GE3", T.kcu, "kcu", 192, 64 - NV)
+        for b in range(EQ1, 16):
+            equal(b)
+            equal_sum(b)
+        sum_e(T.pES, "pES", T.GE, "GE1 GE1b", 64, 64, False, False)
+        if not last:
+            mm("pX", "PX " + cfk, T.pX[:, 0:16], T.PX[:], cf[:], True, True)
+        mm("pX", "IDf " + cfk, T.pX[:, 16:32], T.IDf[:], cf[:], True, False)
+        mm("pX", "NEG dm", T.pX[:, 16:32], T.NEG[:], T.dm[:], False, True)
+        if NV:
+            gather_e("V", T.GE, "GE4", T.kcu, "kcu", 256 - NV, NV)
+        tt("cb", "pEQ THR", T.cb[:], T.pEQ[:, 0:256], T.THR[:], A.is_lt)
+        if not last:
+            cp("cTs", "pX", T.cTs[:], T.pX[:, 0:16])
+        sum_e(T.pES, "pES", T.GE, "GE2", 128, 64, False, False)
+        tt("t1", "pS1 S1s", T.t1[:], T.pS1[:, 0:128], T.S1s[:], A.max)
+        sum_e(T.pES, "pES", T.GE, "GE3 GE4", 192, 64, False, False)
+        mm("pES", "rl%d ID" % t, T.pES[:, 0:256], ident, T.rl[:, 256 * t:256 * t + 256], False, True)
+        for j in range(16):
+            mm("pX", "cb QS", T.pX[:, 32:48], T.QS[:, 15 - j:143 - j], T.cb[:, j::16], j == 0, j == 15)
+        act("cs", "pX", T.cs[:], T.pX[:, 32:48])
+        tt("t2", "t1", T.t2[:], T.t1[:, 0:64], T.t1[:, 64:128], A.max)
+        mm("pB", "IDf " + cfk, T.pB[:, 32:47], T.IDf[:], cf[:, 0:15], True, False)
+        mm("pB", "NEG " + cfk, T.pB[:, 32:47], T.NEG[:], cf[:, 1:16], False, True)
+        tt("t3", "t2", T.t1[:, 0:32], T.t2[:, 0:32], T.t2[:, 32:64], A.max)
+        if not last:
+            act("kcm", "kcf Nn", T.kcm[:], T.kcf[:], F.Copy, scale=T.Nn[:, t:t + 1])
+            act("cXm", "IOTA Ne cTs", T.cXm[:], Iw.indirect(T.cTs[:]), F.Copy, scale=T.Ne[:, t:t + 1])
+        act("DBt", "DB", T.DBt[:, 0:256], T.DB[:], F.Copy, scale=64.0 ** t)
+        if not last:
+            o = 256 * ((t + 1) % 2)
+            act("DT%d" % ((t + 1) % 2), dtk, T.DT[:, o:o + 256], dt_, F.Copy, scale=64.0)
+        ts("X1", "pES", T.X1[:], T.pES[:, 0:256], 0.9 * 64.0 ** (t - 2), 0.5, A.is_ge, A.subtract)
+        for j in range(16):
+            mm("pZ", "X1 Q1", T.pZ[:, 0:16], T.Q1[:, 15 - j:143 - j], T.X1[:, j::16], j == 0, False)
+        tt("X2", "pES " + dtk, T.X2[:], T.pES[:, 0:256], dt_, A.is_ge)
+        for j in range(16):
+            mm("pZ", "X2 Q32", T.pZ[:, 0:16], T.Q32[:, 15 - j:143 - j], T.X2[:, j::16], False, j == 15)
+        tt("bI", "t3", T.bI[:], T.t1[:, 0:16], T.t1[:, 16:32], A.max)
+        ts("bI2", "bI", T.bI2[:], T.bI[:], 15, None, AND)
+        cp("mu", "bI2", T.mu[:], T.bI2[:])
+        tt("Pm", "OH mu kcf", T.Pm[:], T.OH[:].indirect(T.mu[:]), T.kcf[:], A.mult)
+        tt("zc", "pZ cs", T.zc[:], T.pZ[:, 0:16], T.cs[:], A.mult)
+        ts("a1", "zc", T.a1[:], T.zc[:], 0.0, None, A.is_lt)
+        ts("z4", "zc", T.z4[:], T.zc[:], -4.0, None, A.add)
+        if not last:
+            mm("pU", "a1 ON", T.pU[:, 0:16], T.ON[:], T.a1[:], True, True)
+        mm("pB", "NEG " + cfk, T.pB[:, 0:16], T.NEG[:], cf[:], True, False)
+        for j in range(16):
+            mm("pB", "Pm Q1f", T.pB[:, 0:16], T.Q1f[:, 15 - j:143 - j], T.Pm[:, j::16], False, j == 15)
+        tt("m1", "pX a1", T.m1[:], T.pX[:, 16:32], T.a1[:], A.mult)
+        ts("zy", "z4", T.zy[:], T.z4[:], 31, None, AND)
+        ts("od", "z4", T.od[:], T.z4[:], 1, None, AND)
+        tt("m2", "m1 dm", T.m2[:], T.m1[:], T.dm[:], A.add)
+        ts("b3", "zy", T.b3[:], T.zy[:], 5.0, None, A.is_lt)
+        if not last:
+            tt("um0", "pU Dg", T.um[:, u:u + 16], T.pU[:, 0:16], T.Dg[:], A.mult)
+        tt("tn", "a1 b3", T.tn[:], T.a1[:], T.b3[:], A.add)
+        cp("SL", "m2", T.SL[:], T.m2[:])
+        if not last:
+            op("V", lambda: g.vector.tensor_reduce(T.um[:, u + 17:u + 18], T.um[:, u:u + 17], AxisListType.X, A.add), "um2", "um0 um1")
+        tt("mv0", "od tn", T.mv0[:], T.od[:], T.tn[:], A.is_gt)
+        if not last:
+            ts("uk", "um2", T.uk[:], T.um[:, u + 17:u + 18], 1.0 / 256.0, -127.5 / 256.0, A.mult, A.add)
+        tt("mv", "mv0 tn", T.mv[:, 0:15], T.mv0[:, 0:15], T.tn[:, 1:16], A.mult)
+        if not last:
+            ts("of%d" % ((t + 1) % 2), "uk um2", OF[(t + 1) % 2][:, 0:1], T.uk[:], -256.0, T.um[:, u + 17:u + 18], A.mult, A.add)
+        tt("tm", "mv tn", T.tm[:], T.tn[:], T.mv[:], A.add)
+        if not last:
+            tt(KK, "kcm cXm SL", T.K[:].indirect(T.SL[:]), T.kcm[:], T.cXm[:], A.add)
+        else:
+            tt("E Ed", "Ec DBt SL", T.E[:].indirect(T.SL[:]), T.Ec[:], T.DBt[:, 0:256], A.add)
+        tt("tm", "tm mv", T.tm[:, 1:16], T.tm[:, 1:16], T.mv[:, 0:15], A.subtract)
+        tt("v1", "mv pB", T.v1[:, 0:15], T.mv[:, 0:15], T.pB[:, 32:47], A.mult)
+        tt("u1", "tm pB", T.u1[:], T.tm[:], T.pB[:, 0:16], A.mult)
+        tt("nT", "u1 " + cfk, T.nT[:], T.u1[:], cf[:], A.add)
+        tt("nT", "nT v1", T.nT[:, 1:16], T.nT[:, 1:16], T.v1[:, 0:15], A.add)
+        cp("Z", "nT of%d" % (t % 2), T.Z[:, 0:256].indirect(OF[t % 2][:, 0:1]), T.nT[:])
+        if not last:
+            draw(t + 1)
+
+    cp("Z2", "Z", T.Z[:, 256:512], T.Z[:, 0:256])
+    dmas("Y", [(T.ZT[j::16, 0:256], T.Z[j::16, 16 * (-5 * j % 16):16 * (-5 * j % 16) + 256]) for j in range(16)], "dun", "ZT", "Z Z2")
+    for i in range(4):
+        a, b = 768 * i, 768 * (i + 1)
+        act("LN%d IOTA" % i, "E", T.IOTA[:, a:b], T.E[:, a:b], F.Ln)
+        if i == 3:
+            act("YR3", "LN3", T.Wt[:, a:b], T.IOTA[:, a:b], F.Identity, bias=136.0, scale=1.0 / (6.0 * math.log(2.0)))
+        else:
+            ts("YR%d" % i + ("" if i else " Wt"), "LN%d" % i, T.Wt[:, a:b], T.IOTA[:, a:b], 1.0 / (6.0 * math.log(2.0)), 136.0, A.mult, A.add)
+        ts("YQ%d" % i, "YR%d" % i, T.recs[:, a:b], T.Wt[:, a:b], -128.0, None, A.add)
+        dmas("Y", [(T.yr[:, a:b], T.recs[:, a:b])], "dy%d" % i, "", "YQ%d" % i)
+    cp("kc2", "ZT L2", T.kc2[:], T.ZT[:, 0:256].indirect(T.L2[:, 0:32]))
+    vtr("kTa kTb", "kc2", T.kTr[:], T.kc2[:])
+    cp("Pm", "kTa kTb LQ", T.Pm[:], T.kTr[:].indirect(T.LQ[:]))
+    dmas("Y", [(T.ys[:], T.Pm[:])], "dys", "", "Pm")
+    for s in cnt:
+        if clock["G"].get(s, 0) < cnt[s]:
+            g.wait_ge(sem[s], cnt[s])

@@ -4,14 +4,23 @@ from concourse.mybir import ActivationFunctionType as F
 from concourse.mybir import AxisListType
 
 RO = 6
-WV = 4
-KS = 2
-EQ1 = 4
-NV = 32
 W = 3072
 WD = W + 256
+NA = 192
 BASE = 1.75
 XB = [256 * b - 8 * b * (b - 1) for b in range(17)]
+KO = 64.0
+HO = 1536.0
+BIG = 4096.0
+FIRST = ("ask cbu eq:0:4 eq+:0:4 K:0:1 eq:4:4 eq+:4:4 K:1:1 eq:8:8 eq+:8:8 csw cb K:2:2 kcf kcu kTa SW kTb fku kTu starts cb+ "
+         "Ec fV:128:64 fS:0:64 fV:192:64 fS:64:64 wc Ec+ f+:128:64 f+:0:64 f+:192:64 f+:64:64 Rn gS:0:32 answer w:0:1 w:1:1 w:2:2 w:4:4 Kn gS:32:32 "
+         "gS:64:64 g+:0:64 w+:0:4 w:8:4 w+:4:4 g+:64:64 gS:128:64 S1s w:12:4 w+:8:4 g+:128:64 rl+ lS:0:12 lS:12:4 w+:12:4 X1a X2a t1 t2 t3 t4 t5 mu Pm "
+         "l+:0:12 l.:12:4 X1b X2b z+ Pm+ ")
+LATER = ("ask kcf cf wc R kcu kTa SW Ec cbu kTb gS:0:48 eq:0:4 -csw kTu fku Ec+ starts eq+:0:4 fV:192:64 fS:0:64 fS:64:64 fS:128:64 *mark "
+         "w:0:1 w:1:1 w:2:2 eq:4:12 w:4:4 f+:192:64 f+:0:64 f+:64:64 eq+:4:12 w+:0:4 f+:128:64 gS:48:16 answer -Kn *unroll cb w:8:4 w+:4:4 cb+ g+:0:64 "
+         "gS:64:64 w:12:4 w+:8:4 S1s gS:128:64 g+:64:64 w+:12:4 lV:0:2 t1 *zA t2 t3 lS:2:10 g+:128:64 rl+ t4 t5 X1a mu X2a Pm *zB lS:12:4 *marks "
+         "l+:0:12 l.:12:4 X1b X2b Pm+ Rn z+ ")
+FATES = "best zz nb3 a1 od a+ ntn D1 D2 m1 -um sn SL *R *yr -K -uk mv aa -of ww vv ub sm -Z -draw"
 
 SCRATCH = {}
 
@@ -21,39 +30,44 @@ def _bufs(where, n, dtype, names):
         SCRATCH[k] = (where, [128, n], dtype)
 
 
-_bufs("sbuf", W, "bfloat16", "recs Wt")
+_bufs("sbuf", W, "bfloat16", "Wt")
 _bufs("sbuf", W, "int32", "kinI")
 _bufs("sbuf", W, "float32", "IOTA")
-_bufs("sbuf", WD, "bfloat16", "E")
+_bufs("sbuf", WD, "bfloat16", "R")
 _bufs("sbuf", WD, "float32", "K")
 _bufs("sbuf", 4096, "bfloat16", "GE FE X")
 _bufs("sbuf", XB[16], "bfloat16", "EQT")
-_bufs("sbuf", 512, "float32", "Z ZT kc2 kTr")
+_bufs("sbuf", 512, "float32", "Z ZT zA zB kTr")
 _bufs("sbuf", 256, "int32", "slI rI rJ rB")
-_bufs("sbuf", 256, "uint16", "kcu fku kTu cbu")
-_bufs("sbuf", 256, "float32", "kcf kcm cXm Pm DB THR riF tq")
-_bufs("sbuf", 512, "bfloat16", "wc DT DBt")
-_bufs("sbuf", 128, "float32", "S1s t1 IDf NEG PX SW")
-_bufs("sbuf", 256, "bfloat16", "Ec X1 X2 TIE cb")
-_bufs("sbuf", 16, "int32", "bI bI2 z4 zy od")
-_bufs("sbuf", 16, "uint16", "mu SL cTs LQ LP")
-_bufs("sbuf", 16, "float32", "cs cTf cTg m1 m2 zc b3 tn mv0 mv tm u1 v1 nT lane dm wcol Dg OH")
+_bufs("sbuf", 256, "uint16", "kcu fku cbu")
+_bufs("sbuf", 320, "uint16", "kTu")
+_bufs("sbuf", 256, "float32", "kcf Kn csw THR DT riF SN MK")
+_bufs("sbuf", 256, "float16", "Pm slH M0")
+_bufs("sbuf", 1024, "bfloat16", "wc")
+_bufs("sbuf", 512, "bfloat16", "XX")
+_bufs("sbuf", 256 * RO, "bfloat16", "DBt")
+_bufs("sbuf", 128, "float32", "S1s t1 IDf SW")
+_bufs("sbuf", 256, "bfloat16", "Ec Rn TIE cb DB")
+_bufs("sbuf", 16, "int32", "bI bI2 od best")
+_bufs("sbuf", 32, "int32", "zz rH")
+_bufs("sbuf", 16, "uint16", "mu SL LQ")
+_bufs("sbuf", 16, "float32", "m1 nb3 sn mv aa ub ww vv sm D1 D2 lane dm wcol OH MRK CU")
+_bufs("sbuf", 32, "float32", "ntn")
 _bufs("sbuf", 16, "bfloat16", "a1")
-_bufs("sbuf", 32, "uint16", "L1 L2 LZ")
-_bufs("sbuf", 32, "int32", "rH")
+_bufs("sbuf", 32, "bfloat16", "CZ")
+_bufs("sbuf", 32, "uint16", "L1 L2 LZ LP")
 _bufs("sbuf", 64, "float32", "t2")
-_bufs("sbuf", 32 * RO, "float32", "um")
-_bufs("sbuf", 128, "bfloat16", "BO ID ON")
-_bufs("sbuf", 144, "bfloat16", "Q16 Q1 Q32 QS")
-_bufs("sbuf", 144, "float32", "Q1f")
-_bufs("sbuf", 1, "int32", "pI xI gI hI oI uk")
-_bufs("sbuf", 1, "float32", "pF xF gF hF oF colA colB colC colD colE colF colG")
-_bufs("sbuf", 8, "float32", "eb Ne Nn")
+_bufs("sbuf", 32 * RO, "float32", "CC")
+_bufs("sbuf", 128, "bfloat16", "BO ID ON NEG")
+_bufs("sbuf", 144, "bfloat16", "Q16 Q1 QF QL")
+_bufs("sbuf", 144, "float16", "Qh")
+_bufs("sbuf", 1, "int32", "pI xI gI hI oI uk cI dI")
+_bufs("sbuf", 1, "float32", "pF xF gF hF um colA colB colC colD colE colF colG colH colI")
 _bufs("sbuf", 2, "uint16", "of0 of1")
-_bufs("psum", 512, "float32", "pES pFS pEQ pS1 pZ pU pB pX")
+_bufs("psum", 512, "float32", "pA pL pFS pEQ pS0 pS1 pZ pX")
 _bufs("sbuf", 16 * RO, "uint16", "cTu ql")
 _bufs("sbuf", 256 * RO, "bfloat16", "fs rl")
-SEMAPHORES = ["sv", "ss", "sp", "sg", "ls", "dsl", "dsh", "dun", "dys", "dw"] + ["dk%d" % i for i in range(4)] + ["dr%d" % i for i in range(2)] + ["dy%d" % i for i in range(4)] \
+SEMAPHORES = ["sv", "ss", "sp", "sg", "ls", "dsl", "dsh", "dun", "dys", "dyr", "dw", "dr", "dwc", "dkn"] + ["dk%d" % i for i in range(4)] \
     + ["qa%d" % t for t in range(RO)] + ["ra%d" % t for t in range(RO)]
 
 
@@ -64,6 +78,7 @@ def rank_program(g, core, T, topo):
     sem = T.sem
     ENG = {"V": g.vector, "S": g.scalar, "P": g.tensor, "G": g, "Y": g.sync}
     SEM = {"V": "sv", "S": "ss", "P": "sp", "G": "sg"}
+    BANKS = [k for k in SCRATCH if SCRATCH[k][0] == "psum"]
     cnt = {}
     clock = {"V": {}, "S": {}, "P": {}, "G": {}, "Y": {}}
     snap = {}
@@ -82,6 +97,10 @@ def rank_program(g, core, T, topo):
         for k in r:
             if k in lastw:
                 add(lastw[k], False)
+            if k in BANKS:
+                for s, n in lastr.get(k, {}).items():
+                    if s != SEM[q]:
+                        add((s, n), False)
         for k in w:
             if k in lastw:
                 add(lastw[k], True)
@@ -141,107 +160,113 @@ def rank_program(g, core, T, topo):
     def vtr(w, r, out, in_):
         op("V", lambda: g.vector.transpose(out, in_), w, r)
 
-    def act(w, r, out, in_, f=F.Copy, bias=0.0, scale=1.0):
-        op("S", lambda: g.scalar.activation(out, in_, f, bias=bias, scale=scale), w, r)
+    def act(w, r, out, in_, f=F.Copy, **k):
+        op("S", lambda: g.scalar.activation(out, in_, f, **k), w, r)
 
     def mm(w, r, out, l, x, st, sp):
         op("P", lambda: g.tensor.matmul(out, l, x, st, sp), w, r)
+
+    def iota(w, out, pat, cm=0, **k):
+        op("G", lambda: g.iota(out, pat, 0, cm, **k), w, "")
+
+    def by_lanes(w, r, out, sel, x, st, sp):
+        for j in range(16):
+            mm(w, r, out, sel[:, 15 - j:143 - j], x[:, j::16], st and j == 0, sp and j == 15)
 
     dmas("Y", [(T.slI[:], T.slips[:])], "dsl", "slI", "")
     for i in range(4):
         a, b = 768 * i, 768 * (i + 1)
         dmas("Y" if i < 2 else "S", [(T.kinI[:, a:b], T.kin[:, a:b])], "dk%d" % i, "kinI%d" % i, "")
+    dmas("Y", [(T.R[:, 0:W], T.rec[:])], "dr", "R", "")
+    dmas("Y", [(T.Wt[:], T.wealth[:])], "dw", "Wt", "")
 
-    op("G", lambda: g.iota(T.pI[:], [[0, 1]], 0, 1), "pI", "")
-    op("G", lambda: g.iota(T.rI[:], [[1, 256]], 0, 0), "rI", "")
-    op("G", lambda: g.iota(T.IOTA[:], [[1, W]], 0, 0, allow_small_or_imprecise_dtypes=True), "IOTA", "")
     SH, AND = A.arith_shift_right, A.bitwise_and
-    fill("eb", T.eb[:, 2:3], -48.0 * math.log(2.0))
+    iota("pI", T.pI[:], [[0, 1]], 1)
+    iota("rJ", T.rJ[:], [[0, 16], [1, 16]])
+    iota("rI", T.rI[:], [[1, 256]])
+    iota("IO0", T.IOTA[:, 0:1024], [[1, 1024]], allow_small_or_imprecise_dtypes=True)
+    iota("rB", T.rB[:], [[1, 16], [0, 16]])
     ts("xI", "pI", T.xI[:], T.pI[:], 15, None, AND)
     ts("hI", "pI", T.hI[:], T.pI[:], 16, None, AND)
-    ts("rH", "rI", T.rH[:], T.rI[:, 0:32], 1, None, SH)
-    ts("rJ", "rI", T.rJ[:], T.rI[:], 15, None, AND)
+    ts("gI", "pI", T.gI[:], T.pI[:], 4, None, SH)
+    ts("cI", "pI", T.cI[:], T.pI[:], 13.0, None, A.mult)
     cp("xF", "xI", T.xF[:], T.xI[:])
     cp("hF", "hI", T.hF[:], T.hI[:])
-    ts("colA", "xF hF", T.colA[:], T.xF[:], 32.0, T.hF[:], A.mult, A.add)
-    ts("L1", "rH xF", T.L1[:], T.rH[:], 16.0, T.xF[:], A.mult, A.add)
-    ts("LZ", "rJ colA", T.LZ[:], T.rJ[:, 0:32], T.colA[:], None, A.add)
-    cp("of0", "xF", T.of0[:, 0:1], T.xF[:])
-    cp("kc2", "slI L1", T.kc2[:], T.slI[:].indirect(T.L1[:, 0:32]))
-    vtr("kTa kTb", "kc2", T.kTr[:], T.kc2[:])
-    cp("ZT", "kTa kTb LZ", T.ZT[:], T.kTr[:].indirect(T.LZ[:, 0:32]))
-    dmas("Y", [(T.Z[j::16, 0:256], T.ZT[j::16, 16 * (5 * j % 16):16 * (5 * j % 16) + 256]) for j in range(16)], "dsh", "Z", "ZT")
-    for i in range(2):
-        a, b = 1536 * i, 1536 * (i + 1)
-        dmas("Y", [(T.recs[:, a:b], T.rec[:, a:b])], "dr%d" % i, "recs%d" % i, "")
-    dmas("Y", [(T.Wt[:], T.wealth[:])], "dw", "Wt", "")
-    fill("Ed", T.E[:, W:WD], 0.0)
-    fill("Kd", T.K[:, W:WD], 0.0)
-    ts("rB", "rI", T.rB[:], T.rI[:], 4, None, SH)
-    ts("gI", "pI", T.gI[:], T.pI[:], 4, None, SH)
+    ts("colD", "gI", T.colD[:], T.gI[:], 16.0, 15.0, A.mult, A.add)
+    ts("dI", "cI", T.dI[:], T.cI[:], 15, None, AND)
     cp("pF", "pI", T.pF[:], T.pI[:])
     cp("gF", "gI", T.gF[:], T.gI[:])
+    cp("colH", "dI", T.colH[:], T.dI[:])
+    ts("colA", "xF hF", T.colA[:], T.xF[:], 32.0, T.hF[:], A.mult, A.add)
+    cp("of0", "xF", T.of0[:, 0:1], T.xF[:])
+    ts("M0", "rJ colH", T.M0[:], T.rJ[:], T.colH[:], None, A.is_equal)
+    ts("LZ", "rJ colA", T.LZ[:], T.rJ[:, 0:32], T.colA[:], None, A.add)
+    ts("Qh", "rI colD", T.Qh[:], T.rI[:, 0:144], T.colD[:], None, A.is_equal)
+    ts("rH", "rI", T.rH[:], T.rI[:, 0:32], 1, None, SH)
+    ts("lane", "rI xF", T.lane[:], T.rI[:, 0:16], 16.0, T.xF[:], A.mult, A.add)
+    cp("riF", "rI", T.riF[:], T.rI[:])
+    ts("L1", "rH xF", T.L1[:], T.rH[:], 16.0, T.xF[:], A.mult, A.add)
+    LB = math.log(BASE)
+    act("wcol", "lane", T.wcol[:], T.lane[:], F.Exp, bias=71.0, scale=-LB)
+    act("THR", "riF", T.THR[:], T.riF[:], F.Exp, bias=71.0 + math.log(2.53), scale=-LB)
+    act("Kd", "riF", T.K[:, W:WD], T.riF[:], F.Silu)
+    act("IO1", "IO0", T.IOTA[:, 1024:2048], T.IOTA[:, 0:1024], F.Identity, bias=1024.0)
+    act("IO2", "IO0", T.IOTA[:, 2048:3072], T.IOTA[:, 0:1024], F.Identity, bias=2048.0)
+    IOTA = "IO0 IO1 IO2"
+    ts("slH", "slI", T.slH[:], T.slI[:], -HO, None, A.add)
+    ts("Q1", "rI colD", T.Q1[:], T.rI[:, 0:144], T.colD[:], None, A.is_equal)
+    tt("Pm", "slH M0", T.Pm[:], T.slH[:], T.M0[:], A.mult)
+    by_lanes("pEQ", "Pm Qh", T.pEQ[:, 0:16], T.Qh, T.Pm, True, True)
+    cp("zA", "slI L1", T.zA[:], T.slI[:].indirect(T.L1[:, 0:32]))
+    ts("cTu0", "pEQ", T.cTu[:, 0:16], T.pEQ[:, 0:16], HO, None, A.add)
+    ts("cf0", "pEQ", T.CC[:, 16:32], T.pEQ[:, 0:16], HO, None, A.add)
+    vtr("zB", "zA", T.zB[:], T.zA[:])
+    act("ZT", "zB LZ", T.ZT[:], T.zB[:].indirect(T.LZ[:, 0:32]))
+    dmas("Y", [(T.Z[j::16, 0:256], T.ZT[j::16, 16 * (5 * j % 16):16 * (5 * j % 16) + 256]) for j in range(16)], "dsh", "Z", "ZT")
     ts("ID", "rI pF", T.ID[:], T.rI[:, 0:128], T.pF[:], None, A.is_equal)
     ts("colG", "hF pF", T.colG[:], T.hF[:], -2.0, T.pF[:], A.mult, A.add)
-    ts("colG", "colG", T.colG[:], T.colG[:], 16.0, None, A.add)
-    ts("SW", "rI colG", T.SW[:], T.rI[:, 0:128], T.colG[:], None, A.is_equal)
     ts("oI", "pI", T.oI[:], T.pI[:], 1, None, AND)
-    cp("oF", "oI", T.oF[:], T.oI[:])
     ts("gI", "hI", T.gI[:], T.hI[:], 4, None, SH)
-    tt("colF", "oF gI", T.colF[:], T.oF[:], T.gI[:], A.not_equal)
-    ts("xI", "xI", T.xI[:], T.xI[:], 1, None, SH)
-    ts("colE", "xI hF", T.colE[:], T.xI[:], 32.0, T.hF[:], A.mult, A.add)
-    ts("colF", "colF colE", T.colF[:], T.colF[:], 256.0, T.colE[:], A.mult, A.add)
-    ts("LP", "rI colF", T.LP[:], T.rI[:, 0:16], T.colF[:], None, A.add)
-    LB = math.log(BASE)
-    ts("colC", "xF", T.colC[:], T.xF[:], 16.0, None, A.mult)
-    ts("colD", "gF", T.colD[:], T.gF[:], 16.0, 15.0, A.mult, A.add)
-    tt("colB", "xF hF", T.colB[:], T.xF[:], T.hF[:], A.add)
-    ts("lane", "rI xF", T.lane[:], T.rI[:, 0:16], 16.0, T.xF[:], A.mult, A.add)
-    fill("eb0", T.eb[:, 0:1], 71.0)
-    fill("eb1", T.eb[:, 1:2], 71.0 + math.log(2.53))
-    cp("riF", "rI", T.riF[:], T.rI[:])
-    act("wcol", "lane eb0", T.wcol[:], T.lane[:], F.Exp, bias=T.eb[:, 0:1], scale=-LB)
-    act("THR", "riF eb1", T.THR[:], T.riF[:], F.Exp, bias=T.eb[:, 1:2], scale=-LB)
-    ts("Q16", "rI colD", T.Q16[:], T.rI[:, 0:144], T.colD[:], 16.0, A.is_equal, A.mult)
-    ts("Q1", "rI colD", T.Q1[:], T.rI[:, 0:144], T.colD[:], None, A.is_equal)
-    ts("Q32", "rI colD", T.Q32[:], T.rI[:, 0:144], T.colD[:], 32.0, A.is_equal, A.mult)
-    ts("QS", "rI colD", T.QS[:], T.rI[:, 0:144], T.colD[:], 1.0 / 16.0, A.is_equal, A.mult)
-    ts("Q1f", "rI colD", T.Q1f[:], T.rI[:, 0:144], T.colD[:], None, A.is_equal)
+    ts("colG", "colG", T.colG[:], T.colG[:], 16.0, None, A.add)
+    ts("cI", "xI", T.cI[:], T.xI[:], 1, None, SH)
+    ts("dI", "xI", T.dI[:], T.xI[:], 2, None, SH)
+    tt("colF", "oI gI", T.colF[:], T.oI[:], T.gI[:], A.not_equal)
+    ts("SW", "rI colG", T.SW[:], T.rI[:, 0:128], T.colG[:], None, A.is_equal)
+    ts("colF", "colF hF", T.colF[:], T.colF[:], 256.0, T.hF[:], A.mult, A.add)
+    ts("oI", "cI", T.oI[:], T.cI[:], 1, None, AND)
+    ts("colE", "cI colF", T.colE[:], T.cI[:], 32.0, T.colF[:], A.mult, A.add)
+    ts("colI", "oI colF", T.colI[:], T.oI[:], 32.0, T.colF[:], A.mult, A.add)
+    ts("LP", "rI colE", T.LP[:, 0:16], T.rI[:, 0:16], T.colE[:], None, A.add)
+    ts("colI", "dI colI", T.colI[:], T.dI[:], 192.0, T.colI[:], A.add, A.add)
     ts("BO", "rB gF", T.BO[:], T.rB[:, 0:128], T.gF[:], None, A.is_equal)
-    ts("TIE", "rB", T.TIE[:], T.rB[:], -1.0, 15.0, A.mult, A.add)
+    ts("LP2", "rI colI", T.LP[:, 16:20], T.rI[:, 0:4], 4.0, T.colI[:], A.mult, A.add)
     ts("DB", "rB xF", T.DB[:], T.rB[:], T.xF[:], None, A.is_equal)
-    for i in range(4):
-        a, b = 768 * i, 768 * (i + 1)
-        cp("K%d" % i, "kinI%d" % i, T.K[:, a:b], T.kinI[:, a:b])
-    KK = "K0 K1 K2 K3 Kd"
-
-    def records():
-        for i in range(2):
-            a, b = 1536 * i, 1536 * (i + 1)
-            act("E", "recs%d eb" % i, T.E[:, a:b], T.recs[:, a:b], F.Exp, bias=T.eb[:, 2:3], scale=6.0 * math.log(2.0))
-
-    def later_constants():
-        ts("dm", "lane", T.dm[:], T.lane[:], float(W), None, A.add)
-        ts("IDf", "rI pF", T.IDf[:], T.rI[:, 0:128], T.pF[:], None, A.is_equal)
-        ts("NEG", "rI pF", T.NEG[:], T.rI[:, 0:128], T.pF[:], -1.0, A.is_equal, A.mult)
-        for t in range(1, RO):
-            ts("um1", "colC", T.um[:, 32 * t + 16:32 * t + 17], T.colC[:], 1.0 / 16.0, 16.0 * t, A.mult, A.add)
-        ts("riF", "DB", T.riF[:], T.DB[:], -1e20, 1e20, A.mult, A.add)
-        ts("tq", "DB", T.tq[:], T.DB[:], 0.9 * 64.0 ** -3, None, A.mult)
-        ts("colE", "xF", T.colE[:], T.xF[:], -1.0, 15.0, A.mult, A.add)
-        ts("colF", "oF pF", T.colF[:], T.oF[:], -2.0, T.pF[:], A.mult, A.add)
-        tt("DT0", "tq riF", T.DT[:, 0:256], T.tq[:], T.riF[:], A.max)
-        ts("OH", "rI colE", T.OH[:], T.rI[:, 0:16], T.colE[:], None, A.is_equal)
-        ts("colF", "colF", T.colF[:], T.colF[:], 1.0, None, A.add)
-        ts("Dg", "rI xF", T.Dg[:], T.rI[:, 0:16], T.xF[:], 16.0, A.is_equal, A.mult)
-        ts("PX", "rI colF", T.PX[:], T.rI[:, 0:128], T.colF[:], None, A.is_equal)
-        ts("Ne", "rI xF", T.Ne[:, 0:RO], T.rI[:, 0:RO], T.xF[:], None, A.is_equal)
-        ts("Nn", "rI xF", T.Nn[:, 0:RO], T.rI[:, 0:RO], T.xF[:], None, A.not_equal)
-        ts("LQ", "rI colB", T.LQ[:], T.rI[:, 0:16], 32.0, T.colB[:], A.mult, A.add)
-        ts("L2", "rH colC", T.L2[:], T.rH[:], T.colC[:], None, A.add)
-        fill("ON", T.ON[:], 1.0)
-        fill("mv", T.mv[:], 0.0)
+    ts("TIE", "rB", T.TIE[:], T.rB[:], -1.0, 15.0, A.mult, A.add)
+    fill("Rd", T.R[:, W:WD], 0.0)
+    ts("colE", "xF", T.colE[:], T.xF[:], -1.0, 15.0, A.mult, A.add)
+    ts("colI", "xF", T.colI[:], T.xF[:], 2 * BIG, None, A.add)
+    ts("dm", "lane", T.dm[:], T.lane[:], W - BIG, None, A.add)
+    ts("OH", "rI colE", T.OH[:], T.rI[:, 0:16], T.colE[:], None, A.is_equal)
+    ts("CU", "rI xF colI", T.CU[:], T.rI[:, 0:16], T.xF[:], T.colI[:], A.is_equal, A.mult)
+    fill("CZ", T.CZ[:, 0:16], -0.5)
+    fill("CZ2", T.CZ[:, 16:32], -1.875)
+    fill("ON", T.ON[:], 16.0)
+    fill("vv0", T.vv[:, 0:1], 0.0)
+    fill("ntn1", T.ntn[:, 16:17], 1.0)
+    fill("MRK", T.MRK[:], -1.0)
+    ts("colC", "xF", T.colC[:], T.xF[:], 16.0, None, A.mult)
+    tt("colB", "xF hF", T.colB[:], T.xF[:], T.hF[:], A.add)
+    ts("L2", "rH colC", T.L2[:], T.rH[:], T.colC[:], None, A.add)
+    ts("LQ", "rI colB", T.LQ[:], T.rI[:, 0:16], 32.0, T.colB[:], A.mult, A.add)
+    act("IDf", "ID", T.IDf[:], T.ID[:])
+    act("NEG", "ID", T.NEG[:], T.ID[:], scale=-BIG)
+    act("Q16", "Q1", T.Q16[:], T.Q1[:], scale=16.0)
+    act("QF", "Q1", T.QF[:], T.Q1[:], scale=1.0 / 32.0)
+    act("QL", "Q1", T.QL[:], T.Q1[:], scale=1.0 / 16.0)
+    act("DT", "DB", T.DT[:], T.DB[:], F.Identity, bias=-1.0, scale=1.0 + 1.0 / 128.0)
+    for t in range(RO):
+        act("DBt", "DB", T.DBt[:, 256 * t:256 * t + 256], T.DB[:], scale=8.0 + t)
+        act("CC%d" % t, "CU", T.CC[:, 32 * t:32 * t + 16], T.CU[:], F.Identity, bias=16.0 * (t + 1) - 2 * BIG)
 
     def remote(dst, out, in_, rs, r):
         eng = topo.engines(core, dst)[::2]
@@ -255,200 +280,200 @@ def rank_program(g, core, T, topo):
         return len(eng)
 
     OF = (T.of0, T.of1)
-
-    def draw(t):
-        cp("cTu%d" % t, "Z of%d" % (t % 2), T.cTu[:, 16 * t:16 * t + 16], T.Z[:, 0:256].indirect(OF[t % 2][:, 0:1]))
-
     ident = T.ID[:]
-    Ew, Kw, Ww, Iw = T.E[:, 0:W], T.K[:, 0:W], T.Wt[:], T.IOTA[:]
+    Rw, Kw, Ww, Iw, Zw = T.R[:, 0:W], T.K[:, 0:W], T.Wt[:], T.IOTA[:], T.Z[:, 0:256]
+    KK = "K0 K1 K2 K3"
 
-    def gather_e(eng, dst, dk, lst, lk, a, n):
-        out, in_ = dst[:, 16 * a:16 * (a + n)], Ew.indirect(lst[:, a:a + n])
-        if eng == "S":
-            act(dk, "E " + lk, out, in_)
-        else:
-            cp(dk, "E " + lk, out, in_)
-
-    def sum_e(ps, pk, dst, dk, a, n, st, sp):
-        for m in range(16):
-            mm(pk, dk + " ID", ps[:, a:a + n], ident, dst[:, 16 * a + m:16 * (a + n):16], st and m == 0, sp and m == 15)
-
-    draw(0)
     for t in range(RO):
         asked = T.cores[(rank + 1 + t % 3) % 4]
         asker = T.cores[(rank - 1 - t % 3) % 4]
-        cu = T.cTu[:, 16 * t:16 * t + 16]
-        cuk = "cTu%d" % t
-        cfk, cf = ("cTf", T.cTf) if t % 2 == 0 else ("cTg", T.cTg)
+        cu, cuk = T.cTu[:, 16 * t:16 * t + 16], "cTu%d" % t
+        cf, cfk = T.CC[:, 32 * t + 16:32 * t + 32], "cf%d" % t
+        of, ofk = OF[t % 2][:, 0:1], "of%d" % (t % 2)
+        of2, of2k = OF[(t + 1) % 2][:, 0:1], "of%d" % ((t + 1) % 2)
+        fs = T.fs[:, 256 * t:256 * t + 256]
         last = t == RO - 1
-        u = 32 * (t + 1)
-        dtk, dt_ = "DT%d" % (t % 2), T.DT[:, 256 * (t % 2):256 * (t % 2) + 256]
-        ne = remote(asked, T.ql[:, 16 * t:16 * t + 16], cu, "qa%d" % t, cuk)
-        lastw["ql%d" % t] = ("qa%d" % t, ne)
-        lastw["rl%d" % t] = ("ra%d" % t, ne)
-        act(cfk, "Z of%d" % (t % 2), cf[:], T.Z[:, 0:256].indirect(OF[t % 2][:, 0:1]))
-        act("kcf", KK + " " + cuk, T.kcf[:], Kw.indirect(cu))
+        bar = -(8.0 + t - 3) + 1.0 / 64.0
+        done = {}
+
+        def pieces(pre, a, n):
+            return " ".join(k for k, (x, y) in done.items() if k.startswith(pre) and x < a + n and y > a)
+
+        def levels(eng, out, key, lst, lk):
+            if eng == "S":
+                act(key, "R " + lk, out, Rw.indirect(lst), F.Relu, bias=bar)
+            else:
+                ts(key, "R " + lk, out, Rw.indirect(lst), bar, 0.0, A.add, A.max)
+
+        def sum_kin(ps, pk, src, keys, a, n, whole):
+            for m in range(16):
+                mm(pk, keys + " ID", ps[:, a:a + n], ident, src[:, 16 * a + m:16 * (a + n):16], whole and m == 0, whole and m == 15)
+
+        def piece(k, a, n):
+            if k[0] in "gfl" and k[1] in "SV":
+                key = "%sE%d" % (k[0], a)
+                done[key] = (a, a + n)
+                if k[0] == "g":
+                    levels(k[1], T.GE[:, 16 * a:16 * (a + n)], key, T.kcu[:, a:a + n], "kcu")
+                elif k[0] == "f":
+                    levels(k[1], T.FE[:, 16 * a:16 * (a + n)], key, T.fku[:, a:a + n], "fku")
+                else:
+                    levels(k[1], T.GE[:, 16 * NA + 64 * a:16 * NA + 64 * (a + n)], key, T.kTu[:, 256 + 4 * a:256 + 4 * (a + n)], "kTu")
+            elif k == "g+":
+                sum_kin(T.pA, "pA", T.GE, pieces("gE", a, n), a, n, False)
+            elif k == "f+":
+                sum_kin(T.pFS, "pFS", T.FE, pieces("fE", a, n), a, n, True)
+            elif k in ("l+", "l."):
+                for m in range(a, a + n):
+                    o = 16 * NA + 64 * m
+                    mm("pL", pieces("lE", m, 1) + " ID", T.pL[:, 0:64], ident, T.GE[:, o:o + 64], False, k == "l." and m == a + n - 1)
+            elif k == "w":
+                done["X%d" % a] = (a, a + n)
+                tt("X%d" % a, "Wt kTu wc" + (" wcb" if n > 1 else ""), T.X[:, 256 * a:256 * (a + n)], Ww.indirect(T.kTu[:, 16 * a:16 * (a + n)]),
+                   T.wc[:, 0:256 * n], A.max)
+            elif k == "w+":
+                h = a // 8
+                o = 16 * (a - 8 * h)
+                for j in range(16):
+                    mm("pS%d" % h, pieces("X", a, n) + " Q16", (T.pS0, T.pS1)[h][:, o:o + 16 * n], T.Q16[:, 15 - j:143 - j],
+                       T.X[:, 256 * a + j:256 * (a + n):16], False, j == 15 and (a + n) % 8 == 0)
+            else:
+                for b in range(a, a + n):
+                    o, w = XB[b], 256 - 16 * b
+                    if k == "eq":
+                        ts("EQT%d" % b, "cbu wcol " + cfk, T.EQT[:, o:o + w], T.cbu[:, 16 * b:256], T.CC[:, 32 * t + 16 + b:32 * t + 17 + b],
+                           T.wcol[:, b:b + 1], A.is_equal, A.mult)
+                    elif k == "eq+":
+                        mm("pEQ", "EQT%d BO" % b, T.pEQ[:, 16 * b:256], T.BO[:], T.EQT[:, o:o + w], b == 0, b == 15)
+                    else:
+                        ts("K%d" % b, "kinI%d" % b, T.K[:, 768 * b:768 * b + 768], T.kinI[:, 768 * b:768 * b + 768], KO, None, A.add)
+
+        def ask():
+            ne = remote(asked, T.ql[:, 16 * t:16 * t + 16], cu, "qa%d" % t, cuk)
+            lastw["ql%d" % t] = ("qa%d" % t, ne)
+            lastw["rl%d" % t] = ("ra%d" % t, ne)
+
+        def answer():
+            act("fs%d" % t, "pFS", fs, T.pFS[:, 0:256])
+            remote(asker, T.rl[:, 256 * t:256 * t + 256], fs, "ra%d" % t, "fs%d" % t)
+
+        def neighbours():
+            ts("csw0", "cbu", T.csw[:, 0::2], T.cbu[:, 1::2], KO, None, A.add)
+            ts("csw1", "cbu", T.csw[:, 1::2], T.cbu[:, 0::2], KO, None, A.add)
 
         def own_wealth():
             act("wc", "Wt " + cuk, T.wc[:, 0:256], Ww.indirect(cu))
-            act("wcb", "Wt " + cuk, T.wc[:, 256:512], Ww.indirect(cu))
-        if t == 0:
-            records()
-        else:
-            own_wealth()
-            tt("E Ed", "Ec DBt SL", T.E[:].indirect(T.SL[:]), T.Ec[:], T.DBt[:, 0:256], A.add)
-        cp("kcu", "kcf", T.kcu[:], T.kcf[:])
-        act("Ec", "E " + cuk, T.Ec[:], Ew.indirect(cu))
-        vtr("kTa", "kcf", T.kTr[:, 0:256], T.kcf[:])
-        mm("pX", "kTa SW", T.pX[:, 0:256], T.SW[:], T.kTr[:, 0:256], True, True)
-        act("kTb", "pX", T.kTr[:, 256:512], T.pX[:, 0:256])
-        cp("cbu", "IOTA " + cuk, T.cbu[:], Iw.indirect(cu))
-        gather_e("S", T.GE, "GE0", T.kcu, "kcu", 0, 64)
-        if t == 0:
-            own_wealth()
-            later_constants()
-        mm("pES", "Ec ID", T.pES[:, 0:256], ident, T.Ec[:], True, False)
-        sum_e(T.pES, "pES", T.GE, "GE0", 0, 64, False, False)
+            dmas("Y", [(T.wc[:, 256 * i:256 * i + 256], T.wc[:, 0:256]) for i in range(1, 4)], "dwc", "wcb", "wc")
 
-        def equal(b):
-            o, n = XB[b], 256 - 16 * b
-            ts("EQT%d" % b, "cbu wcol " + cfk, T.EQT[:, o:o + n], T.cbu[:, 16 * b:256], cf[:, b:b + 1], T.wcol[:, b:b + 1], A.is_equal, A.mult)
+        def starts():
+            mm("pZ", "CZ CZ2 ID", T.pZ[:, 0:32], ident, T.CZ[:], True, False)
+            mm("pX", "CC%d IDf %s" % (t, cfk), T.pX[:, 0:32], T.IDf[:], T.CC[:, 32 * t:32 * t + 32], True, False)
+            for h in range(2):
+                mm("pS%d" % h, "TIE ID", (T.pS0, T.pS1)[h][:, 0:128], ident, T.TIE[:, 128 * h:128 * h + 128], True, False)
 
-        def equal_sum(b):
-            o, n = XB[b], 256 - 16 * b
-            mm("pEQ", "EQT%d BO" % b, T.pEQ[:, 16 * b:256], T.BO[:], T.EQT[:, o:o + n], b == 0, b == 15)
+        def own_sum():
+            mm("pA", "Ec ID", T.pA[:, 0:NA], ident, T.Ec[:, 0:NA], True, False)
+            mm("pL", "Ec ID", T.pL[:, 0:64], ident, T.Ec[:, NA:256], True, False)
 
-        def wealth(m):
-            tt("X%d" % m, "Wt kTu wc wcb", T.X[:, 512 * m:512 * m + 512], Ww.indirect(T.kTu[:, 32 * m:32 * m + 32]), T.wc[:], A.max)
+        def answer_sum():
+            mm("pA", "rl%d ID" % t, T.pA[:, 0:NA], ident, T.rl[:, 256 * t:256 * t + NA], False, True)
+            mm("pL", "rl%d ID" % t, T.pL[:, 0:64], ident, T.rl[:, 256 * t + NA:256 * t + 256], False, False)
 
-        def score(h):
-            mm("pS1", "TIE ID", T.pS1[:, 128 * h:128 * h + 128], ident, T.TIE[:, 128 * h:128 * h + 128], True, False)
-            xs = " ".join("X%d" % m for m in range(4 * h, 4 * h + 4))
-            for j in range(16):
-                mm("pS1", xs + " Q16", T.pS1[:, 128 * h:128 * h + 128], T.Q16[:, 15 - j:143 - j], T.X[:, 2048 * h + j:2048 * h + 2048:16], False, j == 15)
-        for b in range(EQ1):
-            equal(b)
-        cp("kTu", "kTa kTb LP", T.kTu[:], T.kTr[:].indirect(T.LP[:]))
-        cp("fku", KK + " ql%d" % t, T.fku[:], Kw.indirect(T.ql[:, 16 * t:16 * t + 16]))
-        for m in range(WV):
-            wealth(m)
-        gather_e("V", T.FE, "FE3", T.fku, "fku", 192, 64)
-        for m in range(WV, 8):
-            wealth(m)
-        for b in range(EQ1):
-            equal_sum(b)
-        for k in range(3):
-            gather_e("S", T.FE, "FE%d" % k, T.fku, "fku", 64 * k, 64)
-        for k in range(4):
-            if k == KS:
-                score(0)
-            p = (0, 1, 3, 2)[k]
-            sum_e(T.pFS, "pFS", T.FE, "FE%d" % p, 64 * p, 64, True, True)
-        gather_e("S", T.GE, "GE1", T.kcu, "kcu", 64, 32)
-        fs = T.fs[:, 256 * t:256 * t + 256]
-        act("fs%d" % t, "pFS", fs, T.pFS[:, 0:256])
-        remote(asker, T.rl[:, 256 * t:256 * t + 256], fs, "ra%d" % t, "fs%d" % t)
-        score(1)
-        gather_e("S", T.GE, "GE1b", T.kcu, "kcu", 96, 32)
-        gather_e("S", T.GE, "GE2", T.kcu, "kcu", 128, 64)
-        act("S1s", "pS1", T.S1s[:], T.pS1[:, 128:256])
-        if NV < 64:
-            gather_e("S", T.GE, "GE3", T.kcu, "kcu", 192, 64 - NV)
-        for b in range(EQ1, 16):
-            equal(b)
-            equal_sum(b)
-        sum_e(T.pES, "pES", T.GE, "GE1 GE1b", 64, 64, False, False)
-        if not last:
-            mm("pX", "PX " + cfk, T.pX[:, 0:16], T.PX[:], cf[:], True, True)
-        mm("pX", "IDf " + cfk, T.pX[:, 16:32], T.IDf[:], cf[:], True, False)
-        mm("pX", "NEG dm", T.pX[:, 16:32], T.NEG[:], T.dm[:], False, True)
-        if NV:
-            gather_e("V", T.GE, "GE4", T.kcu, "kcu", 256 - NV, NV)
-        tt("cb", "pEQ THR", T.cb[:], T.pEQ[:, 0:256], T.THR[:], A.is_lt)
-        if not last:
-            cp("cTs", "pX", T.cTs[:], T.pX[:, 0:16])
-        sum_e(T.pES, "pES", T.GE, "GE2", 128, 64, False, False)
-        tt("t1", "pS1 S1s", T.t1[:], T.pS1[:, 0:128], T.S1s[:], A.max)
-        sum_e(T.pES, "pES", T.GE, "GE3 GE4", 192, 64, False, False)
-        mm("pES", "rl%d ID" % t, T.pES[:, 0:256], ident, T.rl[:, 256 * t:256 * t + 256], False, True)
-        for j in range(16):
-            mm("pX", "cb QS", T.pX[:, 32:48], T.QS[:, 15 - j:143 - j], T.cb[:, j::16], j == 0, j == 15)
-        act("cs", "pX", T.cs[:], T.pX[:, 32:48])
-        tt("t2", "t1", T.t2[:], T.t1[:, 0:64], T.t1[:, 64:128], A.max)
-        mm("pB", "IDf " + cfk, T.pB[:, 32:47], T.IDf[:], cf[:, 0:15], True, False)
-        mm("pB", "NEG " + cfk, T.pB[:, 32:47], T.NEG[:], cf[:, 1:16], False, True)
-        tt("t3", "t2", T.t1[:, 0:32], T.t2[:, 0:32], T.t2[:, 32:64], A.max)
-        if not last:
-            act("kcm", "kcf Nn", T.kcm[:], T.kcf[:], F.Copy, scale=T.Nn[:, t:t + 1])
-            act("cXm", "IOTA Ne cTs", T.cXm[:], Iw.indirect(T.cTs[:]), F.Copy, scale=T.Ne[:, t:t + 1])
-        act("DBt", "DB", T.DBt[:, 0:256], T.DB[:], F.Copy, scale=64.0 ** t)
-        if not last:
-            o = 256 * ((t + 1) % 2)
-            act("DT%d" % ((t + 1) % 2), dtk, T.DT[:, o:o + 256], dt_, F.Copy, scale=64.0)
-        ts("X1", "pES", T.X1[:], T.pES[:, 0:256], 0.9 * 64.0 ** (t - 2), 0.5, A.is_ge, A.subtract)
-        for j in range(16):
-            mm("pZ", "X1 Q1", T.pZ[:, 0:16], T.Q1[:, 15 - j:143 - j], T.X1[:, j::16], j == 0, False)
-        tt("X2", "pES " + dtk, T.X2[:], T.pES[:, 0:256], dt_, A.is_ge)
-        for j in range(16):
-            mm("pZ", "X2 Q32", T.pZ[:, 0:16], T.Q32[:, 15 - j:143 - j], T.X2[:, j::16], False, j == 15)
-        tt("bI", "t3", T.bI[:], T.t1[:, 0:16], T.t1[:, 16:32], A.max)
-        ts("bI2", "bI", T.bI2[:], T.bI[:], 15, None, AND)
-        cp("mu", "bI2", T.mu[:], T.bI2[:])
-        tt("Pm", "OH mu kcf", T.Pm[:], T.OH[:].indirect(T.mu[:]), T.kcf[:], A.mult)
-        tt("zc", "pZ cs", T.zc[:], T.pZ[:, 0:16], T.cs[:], A.mult)
-        ts("a1", "zc", T.a1[:], T.zc[:], 0.0, None, A.is_lt)
-        ts("z4", "zc", T.z4[:], T.zc[:], -4.0, None, A.add)
-        if not last:
-            mm("pU", "a1 ON", T.pU[:, 0:16], T.ON[:], T.a1[:], True, True)
-        mm("pB", "NEG " + cfk, T.pB[:, 0:16], T.NEG[:], cf[:], True, False)
-        for j in range(16):
-            mm("pB", "Pm Q1f", T.pB[:, 0:16], T.Q1f[:, 15 - j:143 - j], T.Pm[:, j::16], False, j == 15)
-        tt("m1", "pX a1", T.m1[:], T.pX[:, 16:32], T.a1[:], A.mult)
-        ts("zy", "z4", T.zy[:], T.z4[:], 31, None, AND)
-        ts("od", "z4", T.od[:], T.z4[:], 1, None, AND)
-        tt("m2", "m1 dm", T.m2[:], T.m1[:], T.dm[:], A.add)
-        ts("b3", "zy", T.b3[:], T.zy[:], 5.0, None, A.is_lt)
-        if not last:
-            tt("um0", "pU Dg", T.um[:, u:u + 16], T.pU[:, 0:16], T.Dg[:], A.mult)
-        tt("tn", "a1 b3", T.tn[:], T.a1[:], T.b3[:], A.add)
-        cp("SL", "m2", T.SL[:], T.m2[:])
-        if not last:
-            op("V", lambda: g.vector.tensor_reduce(T.um[:, u + 17:u + 18], T.um[:, u:u + 17], AxisListType.X, A.add), "um2", "um0 um1")
-        tt("mv0", "od tn", T.mv0[:], T.od[:], T.tn[:], A.is_gt)
-        if not last:
-            ts("uk", "um2", T.uk[:], T.um[:, u + 17:u + 18], 1.0 / 256.0, -127.5 / 256.0, A.mult, A.add)
-        tt("mv", "mv0 tn", T.mv[:, 0:15], T.mv0[:, 0:15], T.tn[:, 1:16], A.mult)
-        if not last:
-            ts("of%d" % ((t + 1) % 2), "uk um2", OF[(t + 1) % 2][:, 0:1], T.uk[:], -256.0, T.um[:, u + 17:u + 18], A.mult, A.add)
-        tt("tm", "mv tn", T.tm[:], T.tn[:], T.mv[:], A.add)
-        if not last:
-            tt(KK, "kcm cXm SL", T.K[:].indirect(T.SL[:]), T.kcm[:], T.cXm[:], A.add)
-        else:
-            tt("E Ed", "Ec DBt SL", T.E[:].indirect(T.SL[:]), T.Ec[:], T.DBt[:, 0:256], A.add)
-        tt("tm", "tm mv", T.tm[:, 1:16], T.tm[:, 1:16], T.mv[:, 0:15], A.subtract)
-        tt("v1", "mv pB", T.v1[:, 0:15], T.mv[:, 0:15], T.pB[:, 32:47], A.mult)
-        tt("u1", "tm pB", T.u1[:], T.tm[:], T.pB[:, 0:16], A.mult)
-        tt("nT", "u1 " + cfk, T.nT[:], T.u1[:], cf[:], A.add)
-        tt("nT", "nT v1", T.nT[:, 1:16], T.nT[:, 1:16], T.v1[:, 0:15], A.add)
-        cp("Z", "nT of%d" % (t % 2), T.Z[:, 0:256].indirect(OF[t % 2][:, 0:1]), T.nT[:])
-        if not last:
-            draw(t + 1)
+        def new_kin():
+            act("Kn", "kcf", T.Kn[:], T.kcf[:], F.Identity, bias=KO + HO)
+            dmas("Y", [(T.Kn[t::16, :], T.csw[t::16, :])], "dkn", "Kn", "csw0 csw1")
 
-    cp("Z2", "Z", T.Z[:, 256:512], T.Z[:, 0:256])
-    dmas("Y", [(T.ZT[j::16, 0:256], T.Z[j::16, 16 * (-5 * j % 16):16 * (-5 * j % 16) + 256]) for j in range(16)], "dun", "ZT", "Z Z2")
-    for i in range(4):
-        a, b = 768 * i, 768 * (i + 1)
-        act("LN%d IOTA" % i, "E", T.IOTA[:, a:b], T.E[:, a:b], F.Ln)
-        if i == 3:
-            act("YR3", "LN3", T.Wt[:, a:b], T.IOTA[:, a:b], F.Identity, bias=136.0, scale=1.0 / (6.0 * math.log(2.0)))
-        else:
-            ts("YR%d" % i + ("" if i else " Wt"), "LN%d" % i, T.Wt[:, a:b], T.IOTA[:, a:b], 1.0 / (6.0 * math.log(2.0)), 136.0, A.mult, A.add)
-        ts("YQ%d" % i, "YR%d" % i, T.recs[:, a:b], T.Wt[:, a:b], -128.0, None, A.add)
-        dmas("Y", [(T.yr[:, a:b], T.recs[:, a:b])], "dy%d" % i, "", "YQ%d" % i)
-    cp("kc2", "ZT L2", T.kc2[:], T.ZT[:, 0:256].indirect(T.L2[:, 0:32]))
-    vtr("kTa kTb", "kc2", T.kTr[:], T.kc2[:])
-    cp("Pm", "kTa kTb LQ", T.Pm[:], T.kTr[:].indirect(T.LQ[:]))
-    dmas("Y", [(T.ys[:], T.Pm[:])], "dys", "", "Pm")
+        def counts():
+            by_lanes("pZ", "cb QF", T.pZ[:, 0:16], T.QF, T.cb, False, False)
+            by_lanes("pZ", "cb QL", T.pZ[:, 16:32], T.QL, T.cb, False, False)
+
+        def installed():
+            mm("pX", "a1 NEG", T.pX[:, 16:32], T.NEG[:], T.a1[:], False, last)
+            if not last:
+                mm("pX", "a1 ON", T.pX[:, 0:16], T.ON[:], T.a1[:], False, True)
+
+        def unroll():
+            act("Z2", "Z", T.Z[:, 256:512], T.Z[:, 0:256])
+            dmas("Y", [(T.ZT[j::16, 0:256], T.Z[j::16, 16 * (-5 * j % 16):16 * (-5 * j % 16) + 256]) for j in range(16)], "dun", "ZT", "Z Z2")
+
+        def marks():
+            act("MK", "zB LQ", T.MK[:], T.zB[:].indirect(T.LQ[:]), F.Relu, scale=-1.0)
+            act("SN", "zB LQ", T.SN[:], T.zB[:].indirect(T.LQ[:]), F.Relu)
+
+        STEP = {
+            "ask": ask, "answer": answer, "starts": starts, "Ec+": own_sum, "rl+": answer_sum, "Kn": new_kin, "cb+": counts,
+            "csw": neighbours, "wc": own_wealth, "a+": installed, "unroll": unroll, "marks": marks,
+            "cbu": lambda: cp("cbu", IOTA + " " + cuk, T.cbu[:], Iw.indirect(cu)),
+            "kcf": lambda: act("kcf", KK + " " + cuk, T.kcf[:], Kw.indirect(cu), F.Identity, bias=-(KO + HO)),
+            "cf": lambda: act(cfk, "Z " + ofk, cf, Zw.indirect(of)),
+            "R": lambda: cp("R Rd", "Rn SL", T.R[:].indirect(T.SL[:]), T.Rn[:]),
+            "K": lambda: act(KK + " Kd", "Kn SL", T.K[:].indirect(T.SL[:]), T.Kn[:], F.Silu),
+            "kcu": lambda: ts("kcu", "kcf", T.kcu[:, 0:NA], T.kcf[:, 0:NA], HO + 0.25, None, A.add),
+            "kTa": lambda: vtr("kTa", "kcf", T.kTr[:, 0:256], T.kcf[:]),
+            "SW": lambda: mm("pX", "kTa SW", T.pX[:, 0:256], T.SW[:], T.kTr[:, 0:256], True, True),
+            "kTb": lambda: act("kTb", "pX", T.kTr[:, 256:512], T.pX[:, 0:256]),
+            "kTu": lambda: ts("kTu", "kTa kTb LP LP2", T.kTu[:], T.kTr[:].indirect(T.LP[:, 0:20]), HO + 0.25, None, A.add),
+            "fku": lambda: ts("fku", KK + " ql%d" % t, T.fku[:], Kw.indirect(T.ql[:, 16 * t:16 * t + 16]), 0.25 - KO, None, A.add),
+            "Ec": lambda: levels("S", T.Ec[:], "Ec", cu, cuk),
+            "Rn": lambda: tt("Rn", "R DBt " + cuk, T.Rn[:], Rw.indirect(cu), T.DBt[:, 256 * t:256 * t + 256], A.max),
+            "cb": lambda: tt("cb", "pEQ THR", T.cb[:], T.pEQ[:, 0:256], T.THR[:], A.is_lt),
+            "S1s": lambda: act("S1s", "pS0", T.S1s[:], T.pS0[:, 0:128]),
+            "t1": lambda: tt("t1", "pS1 S1s", T.t1[:], T.pS1[:, 0:128], T.S1s[:], A.max),
+            "t2": lambda: tt("t2", "t1", T.t2[:], T.t1[:, 0:64], T.t1[:, 64:128], A.max),
+            "t3": lambda: tt("t3", "t2", T.t1[:, 0:32], T.t2[:, 0:32], T.t2[:, 32:64], A.max),
+            "t4": lambda: tt("bI", "t3", T.bI[:], T.t1[:, 0:16], T.t1[:, 16:32], A.max),
+            "t5": lambda: ts("bI2", "bI", T.bI2[:], T.bI[:], 15, None, AND),
+            "mu": lambda: cp("mu", "bI2", T.mu[:], T.bI2[:]),
+            "Pm": lambda: tt("Pm", "OH mu kcf", T.Pm[:], T.OH[:].indirect(T.mu[:]), T.kcf[:], A.mult),
+            "Pm+": lambda: by_lanes("pEQ", "Pm Qh", T.pEQ[:, 0:16], T.Qh, T.Pm, True, True),
+            "best": lambda: ts("best", "pEQ", T.best[:], T.pEQ[:, 0:16], HO, None, A.add),
+            "D1": lambda: tt("D1", "best " + cfk, T.D1[:], T.best[:], cf, A.subtract),
+            "D2": lambda: tt("D2", "best " + cfk, T.D2[:, 1:16], T.CC[:, 32 * t + 16:32 * t + 31], T.best[:, 1:16], A.subtract),
+            "X1a": lambda: ts("X1a", "pA", T.XX[:, 0:NA], T.pA[:, 0:NA], 0.75, 1.0 / 64.0, A.is_ge, A.mult),
+            "X2a": lambda: tt("X2a", "pA DT", T.XX[:, 256:256 + NA], T.pA[:, 0:NA], T.DT[:, 0:NA], A.is_lt),
+            "X1b": lambda: ts("X1b", "pL", T.XX[:, NA:256], T.pL[:, 0:64], 0.75, 1.0 / 64.0, A.is_ge, A.mult),
+            "X2b": lambda: tt("X2b", "pL DT", T.XX[:, 256 + NA:512], T.pL[:, 0:64], T.DT[:, NA:256], A.is_lt),
+            "z+": lambda: by_lanes("pZ", "X1a X2a X1b X2b Q1", T.pZ[:, 0:32], T.Q1, T.XX, False, True),
+            "zz": lambda: ts("zz", "pZ", T.zz[:], T.pZ[:, 0:32], 64.0, 1.0, A.mult, A.add),
+            "nb3": lambda: ts("nb3", "pZ", T.nb3[:], T.pZ[:, 0:16], 11.5 / 64.0, None, A.is_lt),
+            "a1": lambda: tt("a1", "zz", T.a1[:], T.zz[:, 0:16], T.zz[:, 16:32], A.is_lt),
+            "od": lambda: ts("od", "zz", T.od[:], T.zz[:, 0:16], 33, None, AND),
+            "ntn": lambda: tt("ntn", "a1 nb3", T.ntn[:, 0:16], T.nb3[:], T.a1[:], A.subtract),
+            "m1": lambda: tt("m1", "pX dm", T.m1[:], T.pX[:, 16:32], T.dm[:], A.min),
+            "SL": lambda: ts("SL", "m1", T.SL[:], T.m1[:], BIG, None, A.add),
+            "um": lambda: op("V", lambda: g.vector.tensor_reduce(T.um[:], T.pX[:, 0:16], AxisListType.X, A.max), "um", "pX"),
+            "uk": lambda: ts("uk", "um", T.uk[:], T.um[:], 1.0 / 256.0, -127.5 / 256.0, A.mult, A.add),
+            "of": lambda: ts(of2k, "uk um", of2, T.uk[:], -256.0, T.um[:], A.mult, A.add),
+            "sn": lambda: tt("sn", "ntn ntn1", T.sn[:], T.ntn[:, 0:16], T.ntn[:, 1:17], A.subtract),
+            "mv": lambda: tt("mv", "od sn", T.mv[:], T.od[:], T.sn[:], A.is_lt),
+            "aa": lambda: tt("aa", "ntn D1", T.aa[:], T.ntn[:, 0:16], T.D1[:], A.mult),
+            "ww": lambda: tt("ww", "mv D1", T.ww[:], T.mv[:], T.D1[:], A.mult),
+            "vv": lambda: tt("vv", "mv D2", T.vv[:, 1:16], T.mv[:, 0:15], T.D2[:, 1:16], A.mult),
+            "ub": lambda: tt("ub", "best aa", T.ub[:], T.best[:], T.aa[:], A.subtract),
+            "sm": lambda: tt("sm", "ww vv vv0", T.sm[:], T.ww[:], T.vv[:], A.add),
+            "Z": lambda: tt("Z", "sm ub " + ofk, Zw.indirect(of), T.sm[:], T.ub[:], A.add),
+            "draw": lambda: cp("cTu%d" % (t + 1), "Z " + of2k, T.cTu[:, 16 * t + 16:16 * t + 32], Zw.indirect(of2)),
+            "mark": lambda: cp("Z", "MRK " + ofk, Zw.indirect(of), T.MRK[:]),
+            "zA": lambda: act("zA", "ZT L2", T.zA[:], T.ZT[:, 0:256].indirect(T.L2[:, 0:32])),
+            "zB": lambda: vtr("zB", "zA", T.zB[:], T.zA[:]),
+            "yr": lambda: dmas("Y", [(T.yr[:], T.R[:, 0:W])], "dyr", "", "R"),
+        }
+        for name in ((LATER if t else FIRST) + FATES).split():
+            if name[0] in "*-":
+                if last != (name[0] == "*"):
+                    continue
+                name = name[1:]
+            if name in STEP:
+                STEP[name]()
+            else:
+                k, a, n = name.split(":")
+                piece(k, int(a), int(n))
+
+    tt("aa", "sm ub", T.aa[:], T.sm[:], T.ub[:], A.add)
+    cp("mu", "aa", T.mu[:], T.aa[:])
+    tt("Kn", IOTA + " mu MK", T.Kn[:], Iw.indirect(T.mu[:]), T.MK[:], A.mult)
+    tt("csw0 csw1", "Kn SN", T.csw[:], T.Kn[:], T.SN[:], A.add)
+    dmas("S", [(T.ys[:], T.csw[:])], "dys", "", "csw0 csw1")
     for s in cnt:
         if clock["G"].get(s, 0) < cnt[s]:
             g.wait_ge(sem[s], cnt[s])

@@ -12,15 +12,18 @@ XB = [256 * b - 8 * b * (b - 1) for b in range(17)]
 KO = 64.0
 HO = 1536.0
 BIG = 4096.0
-FIRST = ("ask cbu eq:0:4 eq+:0:4 K:0:1 eq:4:4 eq+:4:4 K:1:1 eq:8:8 eq+:8:8 csw cb K:2:2 kcf kcu kTa SW kTb fku kTu starts cb+ "
-         "Ec fV:128:64 fS:0:64 fV:192:64 fS:64:64 wc Ec+ f+:128:64 f+:0:64 f+:192:64 f+:64:64 Rn gS:0:32 answer w:0:1 w:1:1 w:2:2 w:4:4 Kn gS:32:32 "
-         "gS:64:64 g+:0:64 w+:0:4 w:8:4 w+:4:4 g+:64:64 gS:128:64 S1s w:12:4 w+:8:4 g+:128:64 rl+ lS:0:12 lS:12:4 w+:12:4 X1a X2a t1 t2 t3 t4 t5 mu Pm "
-         "l+:0:12 l.:12:4 X1b X2b z+ Pm+ ")
-LATER = ("ask kcf cf wc R kcu kTa SW Ec cbu kTb gS:0:48 eq:0:4 -csw kTu fku Ec+ starts eq+:0:4 fV:192:64 fS:0:64 fS:64:64 fS:128:64 *mark "
-         "w:0:1 w:1:1 w:2:2 eq:4:12 w:4:4 f+:192:64 f+:0:64 f+:64:64 eq+:4:12 w+:0:4 f+:128:64 gS:48:16 answer -Kn *unroll cb w:8:4 w+:4:4 cb+ g+:0:64 "
-         "gS:64:64 w:12:4 w+:8:4 S1s gS:128:64 g+:64:64 w+:12:4 lV:0:2 t1 *zA t2 t3 lS:2:10 g+:128:64 rl+ t4 t5 X1a mu X2a Pm *zB lS:12:4 *marks "
-         "l+:0:12 l.:12:4 X1b X2b Pm+ Rn z+ ")
-FATES = "best zz nb3 a1 od a+ ntn D1 D2 m1 -um sn SL *R *yr -K -uk mv aa -of ww vv ub sm -Z -draw"
+RND = 1.5 * 2.0 ** 23
+WL = 14
+KP = 512
+FIRST = ("ask c_eq c_kin cbh eq:0:16 c_z eq+:0:16 c_late kcf cb kTa Kn+ SW kcu fku K:0:3 kTb kTu K:3:3 dc starts Rc fS:0:64 fV:176:80 Ec fS:64:112 "
+         "cb+ Rn+ f+:0:64 f+:192:64 f+:64:64 f+:128:64 gS:0:40 wcV w:0:4 answer gS:40:32 w+:0:4 w:4:4 gS:72:56 Ec+ g+:0:64 g+:64:64 w:8:3 gS:128:64 "
+         "w+:4:4 g+:128:64 lS:0:13 rl+ S1s lS:13:3 w+:8:3 l+:0:13 w:11:3 l.:13:3 Kn Rn next X1a X2a X1b X2b w+:11:3 z+ w:14:2 "
+         "t1 zz t2 w+:14:2 a1 yy t3 a+ od tn t4 m1 um t5 SL K sn t6 uk mv t7 of mu tm vv Pm Pm+ qq ub sm Z draw")
+LATER = ("ask R0 kcf cf wc Rc kTa SW kcu cbh gS:0:16 kTb Ec Rn+ gS:16:48 dc eq:0:6 starts eq+:0:6 fku fS:0:80 eq:6:10 fS:80:48 Ec+ kTu -Kn+ "
+         "fV:192:64 *mark eq+:6:10 w:0:2 cb fS:128:64 f+:0:64 w:4:4 g+:0:64 f+:192:64 cb+ gS:64:32 f+:64:64 f+:128:64 w:2:2 w:8:3 w:11:3 answer "
+         "gS:96:32 gS:128:40 gV:168:24 w+:0:4 w+:4:4 w+:8:3 g+:64:64 *unroll w+:11:3 g+:128:64 w:14:1 lS:0:10 S1s rl+ l+:0:6 t1 w:15:1 lS:10:5 "
+         "l+:6:6 t2 lS:15:1 *zA X1a l.:12:4 t3 -next X2a Rn w+:14:2 -Kn t4 X1b X2b z+ t5 t6 t7 mu "
+         "zz a1 a+ yy Pm m1 tn od SL *R *yr sn -um -K mv -uk tm Pm+ -of vv qq ub *zB *marks sm -Z -draw")
 
 SCRATCH = {}
 
@@ -38,36 +41,37 @@ _bufs("sbuf", WD, "float32", "K")
 _bufs("sbuf", 4096, "bfloat16", "GE FE X")
 _bufs("sbuf", XB[16], "bfloat16", "EQT")
 _bufs("sbuf", 512, "float32", "Z ZT zA zB kTr")
-_bufs("sbuf", 256, "int32", "slI rI rJ rB")
-_bufs("sbuf", 256, "uint16", "kcu fku cbu")
+_bufs("sbuf", 256, "int32", "slI rJ rB")
+_bufs("sbuf", 256, "uint16", "kcu fku")
 _bufs("sbuf", 320, "uint16", "kTu")
-_bufs("sbuf", 256, "float32", "kcf Kn csw THR DT riF SN MK")
-_bufs("sbuf", 256, "float16", "Pm slH M0")
+_bufs("sbuf", 256, "float32", "kcf Kn THR DT rI SN MK")
+_bufs("sbuf", 256, "float16", "Pm slH M0 cbh")
 _bufs("sbuf", 1024, "bfloat16", "wc")
 _bufs("sbuf", 512, "bfloat16", "XX")
 _bufs("sbuf", 256 * RO, "bfloat16", "DBt")
-_bufs("sbuf", 128, "float32", "S1s t1 IDf SW")
-_bufs("sbuf", 256, "bfloat16", "Ec Rn TIE cb DB")
-_bufs("sbuf", 16, "int32", "bI bI2 od best")
+_bufs("sbuf", 128, "float32", "S1s t1 IDf NEGf SW")
+_bufs("sbuf", 128 * (RO - 1), "float32", "NN")
+_bufs("sbuf", 256, "bfloat16", "Ec Rc Rn TIE cb DB")
+_bufs("sbuf", 16, "int32", "bI bI2 od yy")
 _bufs("sbuf", 32, "int32", "zz rH")
 _bufs("sbuf", 16, "uint16", "mu SL LQ")
-_bufs("sbuf", 16, "float32", "m1 nb3 sn mv aa ub ww vv sm D1 D2 lane dm wcol OH MRK CU")
-_bufs("sbuf", 32, "float32", "ntn")
+_bufs("sbuf", 16, "float32", "m1 sn tm qq aa ub vv sm dc lane dm wcol OH MRK CU Nc")
+_bufs("sbuf", 32, "float32", "tn mv")
 _bufs("sbuf", 16, "bfloat16", "a1")
 _bufs("sbuf", 32, "bfloat16", "CZ")
 _bufs("sbuf", 32, "uint16", "L1 L2 LZ LP")
 _bufs("sbuf", 64, "float32", "t2")
 _bufs("sbuf", 32 * RO, "float32", "CC")
 _bufs("sbuf", 128, "bfloat16", "BO ID ON NEG")
-_bufs("sbuf", 144, "bfloat16", "Q16 Q1 QF QL")
-_bufs("sbuf", 144, "float16", "Qh")
+_bufs("sbuf", 144, "bfloat16", "Q16 Q1 QF")
+_bufs("sbuf", 144, "float16", "Qh QL")
 _bufs("sbuf", 1, "int32", "pI xI gI hI oI uk cI dI")
 _bufs("sbuf", 1, "float32", "pF xF gF hF um colA colB colC colD colE colF colG colH colI")
 _bufs("sbuf", 2, "uint16", "of0 of1")
 _bufs("psum", 512, "float32", "pA pL pFS pEQ pS0 pS1 pZ pX")
 _bufs("sbuf", 16 * RO, "uint16", "cTu ql")
 _bufs("sbuf", 256 * RO, "bfloat16", "fs rl")
-SEMAPHORES = ["sv", "ss", "sp", "sg", "ls", "dsl", "dsh", "dun", "dys", "dyr", "dw", "dr", "dwc", "dkn"] + ["dk%d" % i for i in range(4)] \
+SEMAPHORES = ["sv", "ss", "sp", "sg", "ls", "dsl", "dsh", "dun", "dys", "dyr", "dw", "dr", "dk", "dwc"] \
     + ["qa%d" % t for t in range(RO)] + ["ra%d" % t for t in range(RO)]
 
 
@@ -166,107 +170,120 @@ def rank_program(g, core, T, topo):
     def mm(w, r, out, l, x, st, sp):
         op("P", lambda: g.tensor.matmul(out, l, x, st, sp), w, r)
 
-    def iota(w, out, pat, cm=0, **k):
-        op("G", lambda: g.iota(out, pat, 0, cm, **k), w, "")
+    def iota(w, out, pat, base=0, cm=0, **k):
+        op("G", lambda: g.iota(out, pat, base, cm, **k), w, "")
 
     def by_lanes(w, r, out, sel, x, st, sp):
         for j in range(16):
             mm(w, r, out, sel[:, 15 - j:143 - j], x[:, j::16], st and j == 0, sp and j == 15)
 
     dmas("Y", [(T.slI[:], T.slips[:])], "dsl", "slI", "")
-    for i in range(4):
-        a, b = 768 * i, 768 * (i + 1)
-        dmas("Y" if i < 2 else "S", [(T.kinI[:, a:b], T.kin[:, a:b])], "dk%d" % i, "kinI%d" % i, "")
+    dmas("Y", [(T.kinI[:], T.kin[:])], "dk", "kinI", "")
     dmas("Y", [(T.R[:, 0:W], T.rec[:])], "dr", "R", "")
     dmas("Y", [(T.Wt[:], T.wealth[:])], "dw", "Wt", "")
 
     SH, AND = A.arith_shift_right, A.bitwise_and
-    iota("pI", T.pI[:], [[0, 1]], 1)
+    FL = dict(allow_small_or_imprecise_dtypes=True)
+    iota("pI", T.pI[:], [[0, 1]], 0, 1)
+    iota("rI", T.rI[:], [[1, 256]], **FL)
     iota("rJ", T.rJ[:], [[0, 16], [1, 16]])
-    iota("rI", T.rI[:], [[1, 256]])
-    iota("IO0", T.IOTA[:, 0:1024], [[1, 1024]], allow_small_or_imprecise_dtypes=True)
+    iota("IO0", T.IOTA[:, 0:1024], [[1, 1024]], -int(HO), **FL)
     iota("rB", T.rB[:], [[1, 16], [0, 16]])
     ts("xI", "pI", T.xI[:], T.pI[:], 15, None, AND)
-    ts("hI", "pI", T.hI[:], T.pI[:], 16, None, AND)
     ts("gI", "pI", T.gI[:], T.pI[:], 4, None, SH)
     ts("cI", "pI", T.cI[:], T.pI[:], 13.0, None, A.mult)
+    ts("hI", "pI", T.hI[:], T.pI[:], 16, None, AND)
     cp("xF", "xI", T.xF[:], T.xI[:])
-    cp("hF", "hI", T.hF[:], T.hI[:])
     ts("colD", "gI", T.colD[:], T.gI[:], 16.0, 15.0, A.mult, A.add)
     ts("dI", "cI", T.dI[:], T.cI[:], 15, None, AND)
+    cp("hF", "hI", T.hF[:], T.hI[:])
     cp("pF", "pI", T.pF[:], T.pI[:])
     cp("gF", "gI", T.gF[:], T.gI[:])
     cp("colH", "dI", T.colH[:], T.dI[:])
-    ts("colA", "xF hF", T.colA[:], T.xF[:], 32.0, T.hF[:], A.mult, A.add)
-    cp("of0", "xF", T.of0[:, 0:1], T.xF[:])
-    ts("M0", "rJ colH", T.M0[:], T.rJ[:], T.colH[:], None, A.is_equal)
-    ts("LZ", "rJ colA", T.LZ[:], T.rJ[:, 0:32], T.colA[:], None, A.add)
-    ts("Qh", "rI colD", T.Qh[:], T.rI[:, 0:144], T.colD[:], None, A.is_equal)
-    ts("rH", "rI", T.rH[:], T.rI[:, 0:32], 1, None, SH)
     ts("lane", "rI xF", T.lane[:], T.rI[:, 0:16], 16.0, T.xF[:], A.mult, A.add)
-    cp("riF", "rI", T.riF[:], T.rI[:])
-    ts("L1", "rH xF", T.L1[:], T.rH[:], 16.0, T.xF[:], A.mult, A.add)
+    ts("Qh", "rI colD", T.Qh[:], T.rI[:, 0:144], T.colD[:], None, A.is_equal)
+    ts("ID", "rI pF", T.ID[:], T.rI[:, 0:128], T.pF[:], None, A.is_equal)
+    ts("Q1", "rI colD", T.Q1[:], T.rI[:, 0:144], T.colD[:], None, A.is_equal)
+    ts("M0", "rJ colH", T.M0[:], T.rJ[:], T.colH[:], None, A.is_equal)
     LB = math.log(BASE)
     act("wcol", "lane", T.wcol[:], T.lane[:], F.Exp, bias=71.0, scale=-LB)
-    act("THR", "riF", T.THR[:], T.riF[:], F.Exp, bias=71.0 + math.log(2.53), scale=-LB)
-    act("Kd", "riF", T.K[:, W:WD], T.riF[:], F.Silu)
+    act("THR", "rI", T.THR[:], T.rI[:], F.Exp, bias=71.0 + math.log(2.53), scale=-LB)
     act("IO1", "IO0", T.IOTA[:, 1024:2048], T.IOTA[:, 0:1024], F.Identity, bias=1024.0)
     act("IO2", "IO0", T.IOTA[:, 2048:3072], T.IOTA[:, 0:1024], F.Identity, bias=2048.0)
+    act("Kd", "rI", T.K[:, W:WD], T.rI[:], F.Silu)
     IOTA = "IO0 IO1 IO2"
     ts("slH", "slI", T.slH[:], T.slI[:], -HO, None, A.add)
-    ts("Q1", "rI colD", T.Q1[:], T.rI[:, 0:144], T.colD[:], None, A.is_equal)
+    ts("colG", "hF pF", T.colG[:], T.hF[:], -2.0, T.pF[:], A.mult, A.add)
     tt("Pm", "slH M0", T.Pm[:], T.slH[:], T.M0[:], A.mult)
     by_lanes("pEQ", "Pm Qh", T.pEQ[:, 0:16], T.Qh, T.Pm, True, True)
-    cp("zA", "slI L1", T.zA[:], T.slI[:].indirect(T.L1[:, 0:32]))
-    ts("cTu0", "pEQ", T.cTu[:, 0:16], T.pEQ[:, 0:16], HO, None, A.add)
-    ts("cf0", "pEQ", T.CC[:, 16:32], T.pEQ[:, 0:16], HO, None, A.add)
-    vtr("zB", "zA", T.zB[:], T.zA[:])
-    act("ZT", "zB LZ", T.ZT[:], T.zB[:].indirect(T.LZ[:, 0:32]))
-    dmas("Y", [(T.Z[j::16, 0:256], T.ZT[j::16, 16 * (5 * j % 16):16 * (5 * j % 16) + 256]) for j in range(16)], "dsh", "Z", "ZT")
-    ts("ID", "rI pF", T.ID[:], T.rI[:, 0:128], T.pF[:], None, A.is_equal)
-    ts("colG", "hF pF", T.colG[:], T.hF[:], -2.0, T.pF[:], A.mult, A.add)
     ts("oI", "pI", T.oI[:], T.pI[:], 1, None, AND)
     ts("gI", "hI", T.gI[:], T.hI[:], 4, None, SH)
     ts("colG", "colG", T.colG[:], T.colG[:], 16.0, None, A.add)
     ts("cI", "xI", T.cI[:], T.xI[:], 1, None, SH)
     ts("dI", "xI", T.dI[:], T.xI[:], 2, None, SH)
     tt("colF", "oI gI", T.colF[:], T.oI[:], T.gI[:], A.not_equal)
-    ts("SW", "rI colG", T.SW[:], T.rI[:, 0:128], T.colG[:], None, A.is_equal)
-    ts("colF", "colF hF", T.colF[:], T.colF[:], 256.0, T.hF[:], A.mult, A.add)
-    ts("oI", "cI", T.oI[:], T.cI[:], 1, None, AND)
-    ts("colE", "cI colF", T.colE[:], T.cI[:], 32.0, T.colF[:], A.mult, A.add)
-    ts("colI", "oI colF", T.colI[:], T.oI[:], 32.0, T.colF[:], A.mult, A.add)
-    ts("LP", "rI colE", T.LP[:, 0:16], T.rI[:, 0:16], T.colE[:], None, A.add)
-    ts("colI", "dI colI", T.colI[:], T.dI[:], 192.0, T.colI[:], A.add, A.add)
-    ts("BO", "rB gF", T.BO[:], T.rB[:, 0:128], T.gF[:], None, A.is_equal)
-    ts("LP2", "rI colI", T.LP[:, 16:20], T.rI[:, 0:4], 4.0, T.colI[:], A.mult, A.add)
-    ts("DB", "rB xF", T.DB[:], T.rB[:], T.xF[:], None, A.is_equal)
-    ts("TIE", "rB", T.TIE[:], T.rB[:], -1.0, 15.0, A.mult, A.add)
-    fill("Rd", T.R[:, W:WD], 0.0)
-    ts("colE", "xF", T.colE[:], T.xF[:], -1.0, 15.0, A.mult, A.add)
-    ts("colI", "xF", T.colI[:], T.xF[:], 2 * BIG, None, A.add)
-    ts("dm", "lane", T.dm[:], T.lane[:], W - BIG, None, A.add)
-    ts("OH", "rI colE", T.OH[:], T.rI[:, 0:16], T.colE[:], None, A.is_equal)
-    ts("CU", "rI xF colI", T.CU[:], T.rI[:, 0:16], T.xF[:], T.colI[:], A.is_equal, A.mult)
-    fill("CZ", T.CZ[:, 0:16], -0.5)
-    fill("CZ2", T.CZ[:, 16:32], -1.875)
-    fill("ON", T.ON[:], 16.0)
-    fill("vv0", T.vv[:, 0:1], 0.0)
-    fill("ntn1", T.ntn[:, 16:17], 1.0)
-    fill("MRK", T.MRK[:], -1.0)
-    ts("colC", "xF", T.colC[:], T.xF[:], 16.0, None, A.mult)
-    tt("colB", "xF hF", T.colB[:], T.xF[:], T.hF[:], A.add)
-    ts("L2", "rH colC", T.L2[:], T.rH[:], T.colC[:], None, A.add)
-    ts("LQ", "rI colB", T.LQ[:], T.rI[:, 0:16], 32.0, T.colB[:], A.mult, A.add)
-    act("IDf", "ID", T.IDf[:], T.ID[:])
-    act("NEG", "ID", T.NEG[:], T.ID[:], scale=-BIG)
-    act("Q16", "Q1", T.Q16[:], T.Q1[:], scale=16.0)
-    act("QF", "Q1", T.QF[:], T.Q1[:], scale=1.0 / 32.0)
-    act("QL", "Q1", T.QL[:], T.Q1[:], scale=1.0 / 16.0)
-    act("DT", "DB", T.DT[:], T.DB[:], F.Identity, bias=-1.0, scale=1.0 + 1.0 / 128.0)
-    for t in range(RO):
-        act("DBt", "DB", T.DBt[:, 256 * t:256 * t + 256], T.DB[:], scale=8.0 + t)
+    ts("colA", "xF hF", T.colA[:], T.xF[:], 32.0, T.hF[:], A.mult, A.add)
+    cp("of0", "xF", T.of0[:, 0:1], T.xF[:])
+    ts("cTu0", "pEQ", T.cTu[:, 0:16], T.pEQ[:, 0:16], HO, None, A.add)
+    cp("cf0", "pEQ", T.CC[:, 16:32], T.pEQ[:, 0:16])
+
+    def round_constants(t):
         act("CC%d" % t, "CU", T.CC[:, 32 * t:32 * t + 16], T.CU[:], F.Identity, bias=16.0 * (t + 1) - 2 * BIG)
+        act("DBt%d" % t, "DB", T.DBt[:, 256 * t:256 * t + 256], T.DB[:], scale=8.0 + t)
+        if t < RO - 1:
+            act("NN%d" % t, "ID Nc", T.NN[:, 128 * t:128 * t + 128], T.ID[:], scale=T.Nc[:, t:t + 1])
+
+    def c_eq():
+        iota("rH", T.rH[:], [[1, 16], [0, 2]])
+        iota("TIE", T.TIE[:], [[-1, 16], [0, 16]], 15, **FL)
+        iota("ON", T.ON[:], [[0, 128]], 16, **FL)
+        iota("MRK", T.MRK[:], [[0, 16]], -2 * int(HO), **FL)
+        ts("BO", "rB gF", T.BO[:], T.rB[:, 0:128], T.gF[:], None, A.is_equal)
+        ts("DB", "rB xF", T.DB[:], T.rB[:], T.xF[:], None, A.is_equal)
+
+    def c_kin():
+        ts("colF", "colF hF", T.colF[:], T.colF[:], 256.0, T.hF[:], A.mult, A.add)
+        ts("oI", "cI", T.oI[:], T.cI[:], 1, None, AND)
+        ts("SW", "rI colG", T.SW[:], T.rI[:, 0:128], T.colG[:], None, A.is_equal)
+        ts("colE", "cI colF", T.colE[:], T.cI[:], 32.0, T.colF[:], A.mult, A.add)
+        ts("colI", "oI colF", T.colI[:], T.oI[:], 32.0, T.colF[:], A.mult, A.add)
+        ts("LZ", "rJ colA", T.LZ[:], T.rJ[:, 0:32], T.colA[:], None, A.add)
+        ts("LP", "rI colE", T.LP[:, 0:16], T.rI[:, 0:16], T.colE[:], None, A.add)
+        ts("colI", "dI colI", T.colI[:], T.dI[:], 192.0, T.colI[:], A.add, A.add)
+        ts("Nc", "rI xF", T.Nc[:], T.rI[:, 0:16], T.xF[:], None, A.not_equal)
+        ts("colC", "xF", T.colC[:], T.xF[:], 2 * BIG, None, A.add)
+        ts("LP2", "rI colI", T.LP[:, 16:20], T.rI[:, 0:4], 4.0, T.colI[:], A.mult, A.add)
+        ts("CU", "rI xF colC", T.CU[:], T.rI[:, 0:16], T.xF[:], T.colC[:], A.is_equal, A.mult)
+        act("IDf", "ID", T.IDf[:], T.ID[:])
+        act("NEGf", "ID", T.NEGf[:], T.ID[:], scale=-1.0)
+        act("NEG", "ID", T.NEG[:], T.ID[:], scale=-BIG)
+        act("Q16", "Q1", T.Q16[:], T.Q1[:], scale=16.0)
+        act("QF", "Q1", T.QF[:], T.Q1[:], scale=1.0 / 32.0)
+        act("DT", "DB", T.DT[:], T.DB[:], F.Identity, bias=1024.0, scale=1.0 / 128.0 - 1024.0)
+        round_constants(0)
+
+    def c_z():
+        ts("L1", "rH xF", T.L1[:], T.rH[:], 16.0, T.xF[:], A.mult, A.add)
+        fill("CZ", T.CZ[:, 0:16], -5.0 / 64.0)
+        fill("CZ2", T.CZ[:, 16:32], 19.0 / 64.0)
+        ts("zA", "slI L1", T.zA[:], T.slI[:].indirect(T.L1[:, 0:32]), -HO, None, A.add)
+        fill("Rd", T.R[:, W:WD], 0.0)
+        vtr("zB", "zA", T.zB[:], T.zA[:])
+        act("ZT", "zB LZ", T.ZT[:], T.zB[:].indirect(T.LZ[:, 0:32]))
+        dmas("Y", [(T.Z[j::16, 0:256], T.ZT[j::16, 16 * (5 * j % 16):16 * (5 * j % 16) + 256]) for j in range(16)], "dsh", "Z", "ZT")
+
+    def c_late():
+        ts("colE", "xF", T.colE[:], T.xF[:], -1.0, 15.0, A.mult, A.add)
+        ts("dm", "lane", T.dm[:], T.lane[:], W - BIG - HO, None, A.add)
+        ts("colC", "xF", T.colC[:], T.xF[:], 16.0, None, A.mult)
+        tt("colB", "xF hF", T.colB[:], T.xF[:], T.hF[:], A.add)
+        fill("mv", T.mv[:, 0:1], 0.0)
+        fill("tn", T.tn[:, 16:17], 0.0)
+        fill("dc", T.dc[:, 0:1], 0.0)
+        ts("QL", "Qh", T.QL[:], T.Qh[:], 1.0 / 16.0, None, A.mult)
+        ts("OH", "rI colE", T.OH[:], T.rI[:, 0:16], T.colE[:], None, A.is_equal)
+        ts("L2", "rH colC", T.L2[:], T.rH[:], T.colC[:], None, A.add)
+        ts("LQ", "rI colB", T.LQ[:], T.rI[:, 0:16], 32.0, T.colB[:], A.mult, A.add)
 
     def remote(dst, out, in_, rs, r):
         eng = topo.engines(core, dst)[::2]
@@ -282,12 +299,13 @@ def rank_program(g, core, T, topo):
     OF = (T.of0, T.of1)
     ident = T.ID[:]
     Rw, Kw, Ww, Iw, Zw = T.R[:, 0:W], T.K[:, 0:W], T.Wt[:], T.IOTA[:], T.Z[:, 0:256]
-    KK = "K0 K1 K2 K3"
+    KK = " ".join("K%d" % i for i in range(W // KP))
 
     for t in range(RO):
         asked = T.cores[(rank + 1 + t % 3) % 4]
         asker = T.cores[(rank - 1 - t % 3) % 4]
         cu, cuk = T.cTu[:, 16 * t:16 * t + 16], "cTu%d" % t
+        qu, quk = T.ql[:, 16 * t:16 * t + 16], "ql%d" % t
         cf, cfk = T.CC[:, 32 * t + 16:32 * t + 32], "cf%d" % t
         of, ofk = OF[t % 2][:, 0:1], "of%d" % (t % 2)
         of2, of2k = OF[(t + 1) % 2][:, 0:1], "of%d" % ((t + 1) % 2)
@@ -332,38 +350,64 @@ def rank_program(g, core, T, topo):
                 tt("X%d" % a, "Wt kTu wc" + (" wcb" if n > 1 else ""), T.X[:, 256 * a:256 * (a + n)], Ww.indirect(T.kTu[:, 16 * a:16 * (a + n)]),
                    T.wc[:, 0:256 * n], A.max)
             elif k == "w+":
-                h = a // 8
-                o = 16 * (a - 8 * h)
+                h, o = (0, 16 * a) if a < 8 else (1, 16 * (a - 8)) if a < WL else (0, 16 * (a - WL))
+                if a == WL:
+                    mm("pS0", "TIE ID", T.pS0[:, 0:16 * n], ident, T.TIE[:, 16 * WL:256], True, False)
                 for j in range(16):
                     mm("pS%d" % h, pieces("X", a, n) + " Q16", (T.pS0, T.pS1)[h][:, o:o + 16 * n], T.Q16[:, 15 - j:143 - j],
-                       T.X[:, 256 * a + j:256 * (a + n):16], False, j == 15 and (a + n) % 8 == 0)
+                       T.X[:, 256 * a + j:256 * (a + n):16], False, j == 15 and a + n in (8, WL, 16))
             else:
                 for b in range(a, a + n):
+                    if k == "K":
+                        ts("K%d" % b, "kinI", T.K[:, KP * b:KP * b + KP], T.kinI[:, KP * b:KP * b + KP], KO, None, A.add)
+                        continue
                     o, w = XB[b], 256 - 16 * b
                     if k == "eq":
-                        ts("EQT%d" % b, "cbu wcol " + cfk, T.EQT[:, o:o + w], T.cbu[:, 16 * b:256], T.CC[:, 32 * t + 16 + b:32 * t + 17 + b],
+                        ts("EQT%d" % b, "cbh wcol " + cfk, T.EQT[:, o:o + w], T.cbh[:, 16 * b:256], T.CC[:, 32 * t + 16 + b:32 * t + 17 + b],
                            T.wcol[:, b:b + 1], A.is_equal, A.mult)
-                    elif k == "eq+":
-                        mm("pEQ", "EQT%d BO" % b, T.pEQ[:, 16 * b:256], T.BO[:], T.EQT[:, o:o + w], b == 0, b == 15)
                     else:
-                        ts("K%d" % b, "kinI%d" % b, T.K[:, 768 * b:768 * b + 768], T.kinI[:, 768 * b:768 * b + 768], KO, None, A.add)
+                        mm("pEQ", "EQT%d BO" % b, T.pEQ[:, 16 * b:256], T.BO[:], T.EQT[:, o:o + w], b == 0, b == 15)
 
         def ask():
-            ne = remote(asked, T.ql[:, 16 * t:16 * t + 16], cu, "qa%d" % t, cuk)
-            lastw["ql%d" % t] = ("qa%d" % t, ne)
+            ne = remote(asked, qu, cu, "qa%d" % t, cuk)
+            lastw[quk] = ("qa%d" % t, ne)
             lastw["rl%d" % t] = ("ra%d" % t, ne)
 
         def answer():
             act("fs%d" % t, "pFS", fs, T.pFS[:, 0:256])
             remote(asker, T.rl[:, 256 * t:256 * t + 256], fs, "ra%d" % t, "fs%d" % t)
 
-        def neighbours():
-            ts("csw0", "cbu", T.csw[:, 0::2], T.cbu[:, 1::2], KO, None, A.add)
-            ts("csw1", "cbu", T.csw[:, 1::2], T.cbu[:, 0::2], KO, None, A.add)
+        def own_kin():
+            if t:
+                act("kcf", KK + " " + cuk, T.kcf[:], Kw.indirect(cu), F.Identity, bias=-(KO + HO))
+            else:
+                ts("kcf", "kinI " + cuk, T.kcf[:], T.kinI[:].indirect(cu), -HO, None, A.add)
+
+        def asker_kin():
+            if t:
+                ts("fku", KK + " " + quk, T.fku[:], Kw.indirect(qu), 0.25 - KO, None, A.add)
+            else:
+                cp("fku", "kinI " + quk, T.fku[:], T.kinI[:].indirect(qu))
 
         def own_wealth():
             act("wc", "Wt " + cuk, T.wc[:, 0:256], Ww.indirect(cu))
             dmas("Y", [(T.wc[:, 256 * i:256 * i + 256], T.wc[:, 0:256]) for i in range(1, 4)], "dwc", "wcb", "wc")
+
+        def own_wealth_v():
+            cp("wc", "Wt " + cuk, T.wc[:, 0:256], Ww.indirect(cu))
+            cp("wcb", "wc", T.wc[:, 256:512], T.wc[:, 0:256])
+            cp("wcb", "wc wcb", T.wc[:, 512:1024], T.wc[:, 0:512])
+
+        def scatter_records(u):
+            tt("R Rd", "Rn SL DBt%d" % u, T.R[:].indirect(T.SL[:]), T.Rn[:], T.DBt[:, 256 * u:256 * u + 256], A.add)
+
+        def new_records():
+            mm("pEQ", "Rc ID", T.pEQ[:, 256:512], ident, T.Rc[:], True, False)
+            mm("pEQ", "DB NEG", T.pEQ[:, 256:512], T.NEG[:], T.DB[:], False, True)
+
+        def best_kin():
+            mm("pEQ", "NEGf " + cfk, T.pEQ[:, 0:16], T.NEGf[:], cf, True, False)
+            by_lanes("pEQ", "Pm Qh", T.pEQ[:, 0:16], T.Qh, T.Pm, False, True)
 
         def starts():
             mm("pZ", "CZ CZ2 ID", T.pZ[:, 0:32], ident, T.CZ[:], True, False)
@@ -380,12 +424,9 @@ def rank_program(g, core, T, topo):
             mm("pL", "rl%d ID" % t, T.pL[:, 0:64], ident, T.rl[:, 256 * t + NA:256 * t + 256], False, False)
 
         def new_kin():
-            act("Kn", "kcf", T.Kn[:], T.kcf[:], F.Identity, bias=KO + HO)
-            dmas("Y", [(T.Kn[t::16, :], T.csw[t::16, :])], "dkn", "Kn", "csw0 csw1")
-
-        def counts():
-            by_lanes("pZ", "cb QF", T.pZ[:, 0:16], T.QF, T.cb, False, False)
-            by_lanes("pZ", "cb QL", T.pZ[:, 16:32], T.QL, T.cb, False, False)
+            mm("pFS", "kcf NN%d" % t, T.pFS[:, 256:512], T.NN[:, 128 * t:128 * t + 128], T.kcf[:], True, False)
+            for h in range(2):
+                mm("pFS", "cbh QL", T.pFS[:, 256 + h:512:2], T.QL[:, 15 - t:143 - t], T.cbh[:, 1 - h::2], False, h == 1)
 
         def installed():
             mm("pX", "a1 NEG", T.pX[:, 16:32], T.NEG[:], T.a1[:], False, last)
@@ -393,72 +434,75 @@ def rank_program(g, core, T, topo):
                 mm("pX", "a1 ON", T.pX[:, 0:16], T.ON[:], T.a1[:], False, True)
 
         def unroll():
-            act("Z2", "Z", T.Z[:, 256:512], T.Z[:, 0:256])
-            dmas("Y", [(T.ZT[j::16, 0:256], T.Z[j::16, 16 * (-5 * j % 16):16 * (-5 * j % 16) + 256]) for j in range(16)], "dun", "ZT", "Z Z2")
+            cut = [16 * (5 * j % 16) for j in range(16)]
+            dmas("Y", [(T.ZT[j::16, cut[j]:256], T.Z[j::16, 0:256 - cut[j]]) for j in range(16)]
+                 + [(T.ZT[j::16, 0:cut[j]], T.Z[j::16, 256 - cut[j]:256]) for j in range(1, 16)], "dun", "ZT", "Z")
 
         def marks():
-            act("MK", "zB LQ", T.MK[:], T.zB[:].indirect(T.LQ[:]), F.Relu, scale=-1.0)
-            act("SN", "zB LQ", T.SN[:], T.zB[:].indirect(T.LQ[:]), F.Relu)
+            act("MK", "zB LQ", T.MK[:], T.zB[:].indirect(T.LQ[:]), F.Relu, scale=-1.0, bias=RND + 1.0 - 2 * HO)
+            act("SN", "zB LQ", T.SN[:], T.zB[:].indirect(T.LQ[:]), F.Abs, bias=HO - RND)
 
         STEP = {
-            "ask": ask, "answer": answer, "starts": starts, "Ec+": own_sum, "rl+": answer_sum, "Kn": new_kin, "cb+": counts,
-            "csw": neighbours, "wc": own_wealth, "a+": installed, "unroll": unroll, "marks": marks,
-            "cbu": lambda: cp("cbu", IOTA + " " + cuk, T.cbu[:], Iw.indirect(cu)),
-            "kcf": lambda: act("kcf", KK + " " + cuk, T.kcf[:], Kw.indirect(cu), F.Identity, bias=-(KO + HO)),
-            "cf": lambda: act(cfk, "Z " + ofk, cf, Zw.indirect(of)),
-            "R": lambda: cp("R Rd", "Rn SL", T.R[:].indirect(T.SL[:]), T.Rn[:]),
+            "c_eq": c_eq, "c_kin": c_kin, "c_z": c_z, "c_late": c_late,
+            "ask": ask, "answer": answer, "starts": starts, "Ec+": own_sum, "rl+": answer_sum, "Kn+": new_kin,
+            "wc": own_wealth, "wcV": own_wealth_v, "next": lambda: round_constants(t + 1), "Rn+": new_records, "Pm+": best_kin,
+            "a+": installed, "unroll": unroll, "marks": marks, "kcf": own_kin, "fku": asker_kin,
+            "cbh": lambda: cp("cbh", IOTA + " " + cuk, T.cbh[:], Iw.indirect(cu)),
+            "cf": lambda: ts(cfk, cuk, cf, cu, -HO, None, A.add),
+            "R": lambda: scatter_records(t), "R0": lambda: scatter_records(t - 1),
+            "Rn": lambda: act("Rn", "pEQ", T.Rn[:], T.pEQ[:, 256:512], F.Relu),
+            "Kn": lambda: act("Kn", "pFS", T.Kn[:], T.pFS[:, 256:512], F.Identity, bias=KO + HO),
             "K": lambda: act(KK + " Kd", "Kn SL", T.K[:].indirect(T.SL[:]), T.Kn[:], F.Silu),
             "kcu": lambda: ts("kcu", "kcf", T.kcu[:, 0:NA], T.kcf[:, 0:NA], HO + 0.25, None, A.add),
             "kTa": lambda: vtr("kTa", "kcf", T.kTr[:, 0:256], T.kcf[:]),
             "SW": lambda: mm("pX", "kTa SW", T.pX[:, 0:256], T.SW[:], T.kTr[:, 0:256], True, True),
             "kTb": lambda: act("kTb", "pX", T.kTr[:, 256:512], T.pX[:, 0:256]),
             "kTu": lambda: ts("kTu", "kTa kTb LP LP2", T.kTu[:], T.kTr[:].indirect(T.LP[:, 0:20]), HO + 0.25, None, A.add),
-            "fku": lambda: ts("fku", KK + " ql%d" % t, T.fku[:], Kw.indirect(T.ql[:, 16 * t:16 * t + 16]), 0.25 - KO, None, A.add),
-            "Ec": lambda: levels("S", T.Ec[:], "Ec", cu, cuk),
-            "Rn": lambda: tt("Rn", "R DBt " + cuk, T.Rn[:], Rw.indirect(cu), T.DBt[:, 256 * t:256 * t + 256], A.max),
+            "Rc": lambda: act("Rc", "R " + cuk, T.Rc[:], Rw.indirect(cu)),
+            "Ec": lambda: ts("Ec", "Rc", T.Ec[:], T.Rc[:], bar, 0.0, A.add, A.max),
             "cb": lambda: tt("cb", "pEQ THR", T.cb[:], T.pEQ[:, 0:256], T.THR[:], A.is_lt),
+            "cb+": lambda: by_lanes("pZ", "cb QF", T.pZ[:, 0:16], T.QF, T.cb, False, False),
             "S1s": lambda: act("S1s", "pS0", T.S1s[:], T.pS0[:, 0:128]),
             "t1": lambda: tt("t1", "pS1 S1s", T.t1[:], T.pS1[:, 0:128], T.S1s[:], A.max),
             "t2": lambda: tt("t2", "t1", T.t2[:], T.t1[:, 0:64], T.t1[:, 64:128], A.max),
             "t3": lambda: tt("t3", "t2", T.t1[:, 0:32], T.t2[:, 0:32], T.t2[:, 32:64], A.max),
-            "t4": lambda: tt("bI", "t3", T.bI[:], T.t1[:, 0:16], T.t1[:, 16:32], A.max),
-            "t5": lambda: ts("bI2", "bI", T.bI2[:], T.bI[:], 15, None, AND),
+            "t4": lambda: tt("t4", "t3", T.t2[:, 0:16], T.t1[:, 0:16], T.t1[:, 16:32], A.max),
+            "t5": lambda: tt("t5", "pS0 t4", T.t2[:, 16:32], T.pS0[:, 0:16], T.t2[:, 0:16], A.max),
+            "t6": lambda: tt("bI", "pS0 t5", T.bI[:], T.pS0[:, 16:32], T.t2[:, 16:32], A.max),
+            "t7": lambda: ts("bI2", "bI", T.bI2[:], T.bI[:], 15, None, AND),
             "mu": lambda: cp("mu", "bI2", T.mu[:], T.bI2[:]),
             "Pm": lambda: tt("Pm", "OH mu kcf", T.Pm[:], T.OH[:].indirect(T.mu[:]), T.kcf[:], A.mult),
-            "Pm+": lambda: by_lanes("pEQ", "Pm Qh", T.pEQ[:, 0:16], T.Qh, T.Pm, True, True),
-            "best": lambda: ts("best", "pEQ", T.best[:], T.pEQ[:, 0:16], HO, None, A.add),
-            "D1": lambda: tt("D1", "best " + cfk, T.D1[:], T.best[:], cf, A.subtract),
-            "D2": lambda: tt("D2", "best " + cfk, T.D2[:, 1:16], T.CC[:, 32 * t + 16:32 * t + 31], T.best[:, 1:16], A.subtract),
-            "X1a": lambda: ts("X1a", "pA", T.XX[:, 0:NA], T.pA[:, 0:NA], 0.75, 1.0 / 64.0, A.is_ge, A.mult),
-            "X2a": lambda: tt("X2a", "pA DT", T.XX[:, 256:256 + NA], T.pA[:, 0:NA], T.DT[:, 0:NA], A.is_lt),
-            "X1b": lambda: ts("X1b", "pL", T.XX[:, NA:256], T.pL[:, 0:64], 0.75, 1.0 / 64.0, A.is_ge, A.mult),
-            "X2b": lambda: tt("X2b", "pL DT", T.XX[:, 256 + NA:512], T.pL[:, 0:64], T.DT[:, NA:256], A.is_lt),
+            "X1a": lambda: ts("X1a", "pA", T.XX[:, 0:NA], T.pA[:, 0:NA], 0.75, -1.0 / 64.0, A.is_ge, A.mult),
+            "X2a": lambda: tt("X2a", "pA DT", T.XX[:, 256:256 + NA], T.pA[:, 0:NA], T.DT[:, 0:NA], A.is_ge),
+            "X1b": lambda: ts("X1b", "pL", T.XX[:, NA:256], T.pL[:, 0:64], 0.75, -1.0 / 64.0, A.is_ge, A.mult),
+            "X2b": lambda: tt("X2b", "pL DT", T.XX[:, 256 + NA:512], T.pL[:, 0:64], T.DT[:, NA:256], A.is_ge),
             "z+": lambda: by_lanes("pZ", "X1a X2a X1b X2b Q1", T.pZ[:, 0:32], T.Q1, T.XX, False, True),
-            "zz": lambda: ts("zz", "pZ", T.zz[:], T.pZ[:, 0:32], 64.0, 1.0, A.mult, A.add),
-            "nb3": lambda: ts("nb3", "pZ", T.nb3[:], T.pZ[:, 0:16], 11.5 / 64.0, None, A.is_lt),
-            "a1": lambda: tt("a1", "zz", T.a1[:], T.zz[:, 0:16], T.zz[:, 16:32], A.is_lt),
+            "zz": lambda: ts("zz", "pZ", T.zz[:], T.pZ[:, 0:32], 64.0, None, A.mult),
+            "a1": lambda: tt("a1", "zz", T.a1[:], T.zz[:, 0:16], T.zz[:, 16:32], A.is_gt),
+            "yy": lambda: ts("yy", "zz", T.yy[:], T.zz[:, 0:16], 4, None, SH),
             "od": lambda: ts("od", "zz", T.od[:], T.zz[:, 0:16], 33, None, AND),
-            "ntn": lambda: tt("ntn", "a1 nb3", T.ntn[:, 0:16], T.nb3[:], T.a1[:], A.subtract),
+            "tn": lambda: tt("tn", "a1 yy", T.tn[:, 0:16], T.yy[:], T.a1[:], A.is_equal),
             "m1": lambda: tt("m1", "pX dm", T.m1[:], T.pX[:, 16:32], T.dm[:], A.min),
-            "SL": lambda: ts("SL", "m1", T.SL[:], T.m1[:], BIG, None, A.add),
+            "SL": lambda: ts("SL", "m1", T.SL[:], T.m1[:], BIG + HO, None, A.add),
             "um": lambda: op("V", lambda: g.vector.tensor_reduce(T.um[:], T.pX[:, 0:16], AxisListType.X, A.max), "um", "pX"),
             "uk": lambda: ts("uk", "um", T.uk[:], T.um[:], 1.0 / 256.0, -127.5 / 256.0, A.mult, A.add),
             "of": lambda: ts(of2k, "uk um", of2, T.uk[:], -256.0, T.um[:], A.mult, A.add),
-            "sn": lambda: tt("sn", "ntn ntn1", T.sn[:], T.ntn[:, 0:16], T.ntn[:, 1:17], A.subtract),
-            "mv": lambda: tt("mv", "od sn", T.mv[:], T.od[:], T.sn[:], A.is_lt),
-            "aa": lambda: tt("aa", "ntn D1", T.aa[:], T.ntn[:, 0:16], T.D1[:], A.mult),
-            "ww": lambda: tt("ww", "mv D1", T.ww[:], T.mv[:], T.D1[:], A.mult),
-            "vv": lambda: tt("vv", "mv D2", T.vv[:, 1:16], T.mv[:, 0:15], T.D2[:, 1:16], A.mult),
-            "ub": lambda: tt("ub", "best aa", T.ub[:], T.best[:], T.aa[:], A.subtract),
-            "sm": lambda: tt("sm", "ww vv vv0", T.sm[:], T.ww[:], T.vv[:], A.add),
+            "dc": lambda: tt("dc", cfk, T.dc[:, 1:16], T.CC[:, 32 * t + 16:32 * t + 31], T.CC[:, 32 * t + 17:32 * t + 32], A.subtract),
+            "sn": lambda: tt("sn", "tn", T.sn[:], T.tn[:, 1:17], T.tn[:, 0:16], A.subtract),
+            "mv": lambda: tt("mv", "od sn", T.mv[:, 1:17], T.od[:], T.sn[:], A.is_lt),
+            "tm": lambda: tt("tm", "tn mv", T.tm[:], T.tn[:, 0:16], T.mv[:, 1:17], A.add),
+            "vv": lambda: tt("vv", "mv dc", T.vv[:], T.mv[:, 0:16], T.dc[:], A.mult),
+            "qq": lambda: tt("qq", "tm mv", T.qq[:], T.tm[:], T.mv[:, 0:16], A.subtract),
+            "ub": lambda: tt("ub", "vv " + cfk, T.ub[:], T.vv[:], cf, A.add),
+            "sm": lambda: tt("sm", "pEQ qq", T.sm[:], T.pEQ[:, 0:16], T.qq[:], A.mult),
             "Z": lambda: tt("Z", "sm ub " + ofk, Zw.indirect(of), T.sm[:], T.ub[:], A.add),
-            "draw": lambda: cp("cTu%d" % (t + 1), "Z " + of2k, T.cTu[:, 16 * t + 16:16 * t + 32], Zw.indirect(of2)),
+            "draw": lambda: ts("cTu%d" % (t + 1), "Z " + of2k, T.cTu[:, 16 * t + 16:16 * t + 32], Zw.indirect(of2), HO + 0.25, None, A.add),
             "mark": lambda: cp("Z", "MRK " + ofk, Zw.indirect(of), T.MRK[:]),
-            "zA": lambda: act("zA", "ZT L2", T.zA[:], T.ZT[:, 0:256].indirect(T.L2[:, 0:32])),
+            "zA": lambda: act("zA", "ZT L2", T.zA[:], T.ZT[:, 0:256].indirect(T.L2[:, 0:32]), F.Identity, bias=RND),
             "zB": lambda: vtr("zB", "zA", T.zB[:], T.zA[:]),
             "yr": lambda: dmas("Y", [(T.yr[:], T.R[:, 0:W])], "dyr", "", "R"),
         }
-        for name in ((LATER if t else FIRST) + FATES).split():
+        for name in (LATER if t else FIRST).split():
             if name[0] in "*-":
                 if last != (name[0] == "*"):
                     continue
@@ -470,10 +514,10 @@ def rank_program(g, core, T, topo):
                 piece(k, int(a), int(n))
 
     tt("aa", "sm ub", T.aa[:], T.sm[:], T.ub[:], A.add)
-    cp("mu", "aa", T.mu[:], T.aa[:])
+    ts("mu", "aa", T.mu[:], T.aa[:], HO + 0.25, None, A.add)
     tt("Kn", IOTA + " mu MK", T.Kn[:], Iw.indirect(T.mu[:]), T.MK[:], A.mult)
-    tt("csw0 csw1", "Kn SN", T.csw[:], T.Kn[:], T.SN[:], A.add)
-    dmas("S", [(T.ys[:], T.csw[:])], "dys", "", "csw0 csw1")
+    tt("kcf", "Kn SN", T.kcf[:], T.Kn[:], T.SN[:], A.add)
+    dmas("S", [(T.ys[:], T.kcf[:])], "dys", "", "kcf")
     for s in cnt:
         if clock["G"].get(s, 0) < cnt[s]:
             g.wait_ge(sem[s], cnt[s])

@@ -15,15 +15,19 @@ BIG = 4096.0
 RND = 1.5 * 2.0 ** 23
 WL = 14
 KP = 512
-FIRST = ("ask c_eq c_kin cbh eq:0:16 c_z eq+:0:16 c_late kcf cb kTa Kn+ SW kcu fku K:0:3 kTb kTu K:3:3 dc starts Rc fS:0:64 fV:176:80 Ec fS:64:112 "
-         "cb+ Rn+ f+:0:64 f+:192:64 f+:64:64 f+:128:64 gS:0:40 wcV w:0:4 answer gS:40:32 w+:0:4 w:4:4 gS:72:56 Ec+ g+:0:64 g+:64:64 w:8:3 gS:128:64 "
-         "w+:4:4 g+:128:64 lS:0:13 rl+ S1s lS:13:3 w+:8:3 l+:0:13 w:11:3 l.:13:3 Kn Rn next X1a X2a X1b X2b w+:11:3 z+ w:14:2 "
-         "t1 zz t2 w+:14:2 a1 yy t3 a+ od tn t4 m1 um t5 SL K sn t6 uk mv t7 of mu tm vv Pm Pm+ qq ub sm Z draw")
-LATER = ("ask R0 kcf cf wc Rc kTa SW kcu cbh gS:0:16 kTb Ec Rn+ gS:16:48 dc eq:0:6 starts eq+:0:6 fku fS:0:80 eq:6:10 fS:80:48 Ec+ kTu -Kn+ "
-         "fV:192:64 *mark eq+:6:10 w:0:2 cb fS:128:64 f+:0:64 w:4:4 g+:0:64 f+:192:64 cb+ gS:64:32 f+:64:64 f+:128:64 w:2:2 w:8:3 w:11:3 answer "
-         "gS:96:32 gS:128:40 gV:168:24 w+:0:4 w+:4:4 w+:8:3 g+:64:64 *unroll w+:11:3 g+:128:64 w:14:1 lS:0:10 S1s rl+ l+:0:6 t1 w:15:1 lS:10:5 "
-         "l+:6:6 t2 lS:15:1 *zA X1a l.:12:4 t3 -next X2a Rn w+:14:2 -Kn t4 X1b X2b z+ t5 t6 t7 mu "
-         "zz a1 a+ yy Pm m1 tn od SL *R *yr sn -um -K mv -uk tm Pm+ -of vv qq ub *zB *marks sm -Z -draw")
+FIRST = ("ask numbers by_gpsimd for_fates K:0:2 for_sums K:2:2 kcf fku kTa kcu fV:168:88 kT+ cbh kTu eq:0:16 wc fS:0:72 Rc eq+:0:16 fS:72:96 Kn+ "
+         "f+:0:64 f+:192:64 Ec f+:64:64 f+:128:64 gS:0:16 cb gS:136:56 gS:104:32 w:0:1 w:3:1 starts w:1:1 w:2:1 w:15:1 answer Rn+ K:4:1 gS:16:88 "
+         "w:14:1 w:4:4 w+:0:4 Ec+ g+:128:64 lS:0:13 lS:13:3 cb+ w+:4:4 S1s g+:64:64 Kn g+:0:64 Rn rl+ w:8:3 w+:8:3 l+:0:13 next l.:13:3 w:11:3 "
+         "X1a w+:11:3 X2a X1b X2b K:5:1 t1 t2 z+ zz dc t3 yy zn t4 na w+:14:2 od t5 tn pm t6 a+ um Kd m1 t7 mv uk SL mu vv of Pm R K ub Pm+ q+ D "
+         "sm Z for_results draw")
+LATER = ("ask Rc kcf Rn+ cf kcu wc gS:48:16 cbh kTa kT+ Kn+ gS:112:32 Ec Ec+ eq:0:6 eq:6:10 gS:0:48 g+:0:64 fku fS:0:56 kTu fV:184:72 eq+:0:6 starts "
+         "f+:192:64 eq+:6:10 fS:56:72 fS:128:56 w:0:2 f+:0:64 gS:144:32 w:2:2 w:8:3 f+:64:64 f+:128:64 answer gS:64:48 w:4:4 w+:8:3 cb w+:0:4 w:11:3 "
+         "lS:4:9 w+:4:4 cb+ gV:176:16 w:14:1 S1s g+:64:64 lS:0:4 w+:11:3 g+:128:64 l+:6:6 lS:13:3 rl+ l+:0:6 t1 w:15:1 t2 X2a l.:12:4 t3 w+:14:2 "
+         "X1a X2b X1b t4 dc t5 t6 t7 z+ zz zn mu next yy od na Pm a+ tn Rn Pm+ pm m1 Kn um mv D SL uk q+ vv R sm ub K of Z draw")
+LAST = ("ask kcf mark Rc wc cf kcu gS:0:32 gS:32:24 Ec cbh gV:184:8 kTa gS:56:24 eq:0:6 fku kT+ Rn+ eq:6:10 kTu unroll fS:0:72 Ec+ fV:184:72 eq+:0:6 "
+        "fS:88:96 g+:0:64 f+:192:64 starts eq+:6:10 fS:72:16 w:4:4 f+:0:64 f+:64:64 f+:128:64 gS:80:48 cb w:0:2 w:2:2 cb+ lV:10:6 g+:64:64 w:8:3 "
+        "answer lS:5:5 w+:0:4 w+:4:4 l+:6:6 w+:8:3 gS:128:56 w:11:3 g+:128:64 rl+ w:15:1 lS:0:5 l+:0:6 l.:12:4 X1a X2a X2b X1b w+:11:3 w:14:1 Rn "
+        "z+ S1s t1 t2 zz zn t3 w+:14:2 na a+ t4 t5 m1 yy t6 SL od t7 R yr mu Pm zA pm tn dc mv zB vv ub Pm+ D marks q+ sm")
 
 SCRATCH = {}
 
@@ -40,39 +44,39 @@ _bufs("sbuf", WD, "bfloat16", "R")
 _bufs("sbuf", WD, "float32", "K")
 _bufs("sbuf", 4096, "bfloat16", "GE FE X")
 _bufs("sbuf", XB[16], "bfloat16", "EQT")
-_bufs("sbuf", 512, "float32", "Z ZT zA zB kTr")
+_bufs("sbuf", 512, "float32", "zA zB")
 _bufs("sbuf", 256, "int32", "slI rJ rB")
 _bufs("sbuf", 256, "uint16", "kcu fku")
 _bufs("sbuf", 320, "uint16", "kTu")
-_bufs("sbuf", 256, "float32", "kcf Kn THR DT rI SN MK")
-_bufs("sbuf", 256, "float16", "Pm slH M0 cbh")
+_bufs("sbuf", 256, "float32", "Z ZT Kn THR DT rI SN MK")
+_bufs("sbuf", 256, "float16", "Pm slH M0 cbh kcf kTr")
 _bufs("sbuf", 1024, "bfloat16", "wc")
-_bufs("sbuf", 512, "bfloat16", "XX")
+_bufs("sbuf", 512, "bfloat16", "XX MV")
 _bufs("sbuf", 256 * RO, "bfloat16", "DBt")
-_bufs("sbuf", 128, "float32", "S1s t1 IDf NEGf SW")
-_bufs("sbuf", 128 * (RO - 1), "float32", "NN")
+_bufs("sbuf", 128, "float32", "S1s t1 IDf NEGf")
+_bufs("sbuf", 128 * (RO - 1), "bfloat16", "NN")
 _bufs("sbuf", 256, "bfloat16", "Ec Rc Rn TIE cb DB")
-_bufs("sbuf", 16, "int32", "bI bI2 od yy")
+_bufs("sbuf", 16, "int32", "bI bI2 od yy zn")
 _bufs("sbuf", 32, "int32", "zz rH")
 _bufs("sbuf", 16, "uint16", "mu SL LQ")
-_bufs("sbuf", 16, "float32", "m1 sn tm qq aa ub vv sm dc lane dm wcol OH MRK CU Nc")
-_bufs("sbuf", 32, "float32", "tn mv")
-_bufs("sbuf", 16, "bfloat16", "a1")
+_bufs("sbuf", 16, "float32", "m1 pm D aa ub vv sm dc lane dm wcol OH MRK CU Nc")
+_bufs("sbuf", 32, "bfloat16", "tn mv")
+_bufs("sbuf", 16, "bfloat16", "na")
 _bufs("sbuf", 32, "bfloat16", "CZ")
-_bufs("sbuf", 32, "uint16", "L1 L2 LZ LP")
+_bufs("sbuf", 32, "uint16", "L2")
 _bufs("sbuf", 64, "float32", "t2")
 _bufs("sbuf", 32 * RO, "float32", "CC")
-_bufs("sbuf", 128, "bfloat16", "BO ID ON NEG")
-_bufs("sbuf", 144, "bfloat16", "Q16 Q1 QF")
-_bufs("sbuf", 144, "float16", "Qh QL")
-_bufs("sbuf", 1, "int32", "pI xI gI hI oI uk cI dI")
-_bufs("sbuf", 1, "float32", "pF xF gF hF um colA colB colC colD colE colF colG colH colI")
+_bufs("sbuf", 128, "bfloat16", "BO ID ON NEG POS SW")
+_bufs("sbuf", 144, "bfloat16", "Q16 Q1 QF QL")
+_bufs("sbuf", 1, "int32", "pI xI gI hI uk cI dI")
+_bufs("sbuf", 1, "float32", "pF xF gF hF um colB colC colD colE colG colH")
+_bufs("sbuf", 2, "float32", "colF")
 _bufs("sbuf", 2, "uint16", "of0 of1")
 _bufs("psum", 512, "float32", "pA pL pFS pEQ pS0 pS1 pZ pX")
 _bufs("sbuf", 16 * RO, "uint16", "cTu ql")
 _bufs("sbuf", 256 * RO, "bfloat16", "fs rl")
 SEMAPHORES = ["sv", "ss", "sp", "sg", "ls", "dsl", "dsh", "dun", "dys", "dyr", "dw", "dr", "dk", "dwc"] \
-    + ["qa%d" % t for t in range(RO)] + ["ra%d" % t for t in range(RO)]
+    + [s % t for s in ("qa%d", "ra%d") for t in range(RO)]
 
 
 def rank_program(g, core, T, topo):
@@ -187,7 +191,6 @@ def rank_program(g, core, T, topo):
     iota("pI", T.pI[:], [[0, 1]], 0, 1)
     iota("rI", T.rI[:], [[1, 256]], **FL)
     iota("rJ", T.rJ[:], [[0, 16], [1, 16]])
-    iota("IO0", T.IOTA[:, 0:1024], [[1, 1024]], -int(HO), **FL)
     iota("rB", T.rB[:], [[1, 16], [0, 16]])
     ts("xI", "pI", T.xI[:], T.pI[:], 15, None, AND)
     ts("gI", "pI", T.gI[:], T.pI[:], 4, None, SH)
@@ -201,104 +204,103 @@ def rank_program(g, core, T, topo):
     cp("gF", "gI", T.gF[:], T.gI[:])
     cp("colH", "dI", T.colH[:], T.dI[:])
     ts("lane", "rI xF", T.lane[:], T.rI[:, 0:16], 16.0, T.xF[:], A.mult, A.add)
-    ts("Qh", "rI colD", T.Qh[:], T.rI[:, 0:144], T.colD[:], None, A.is_equal)
     ts("ID", "rI pF", T.ID[:], T.rI[:, 0:128], T.pF[:], None, A.is_equal)
     ts("Q1", "rI colD", T.Q1[:], T.rI[:, 0:144], T.colD[:], None, A.is_equal)
     ts("M0", "rJ colH", T.M0[:], T.rJ[:], T.colH[:], None, A.is_equal)
     LB = math.log(BASE)
     act("wcol", "lane", T.wcol[:], T.lane[:], F.Exp, bias=71.0, scale=-LB)
     act("THR", "rI", T.THR[:], T.rI[:], F.Exp, bias=71.0 + math.log(2.53), scale=-LB)
-    act("IO1", "IO0", T.IOTA[:, 1024:2048], T.IOTA[:, 0:1024], F.Identity, bias=1024.0)
-    act("IO2", "IO0", T.IOTA[:, 2048:3072], T.IOTA[:, 0:1024], F.Identity, bias=2048.0)
-    act("Kd", "rI", T.K[:, W:WD], T.rI[:], F.Silu)
     IOTA = "IO0 IO1 IO2"
-    ts("slH", "slI", T.slH[:], T.slI[:], -HO, None, A.add)
     ts("colG", "hF pF", T.colG[:], T.hF[:], -2.0, T.pF[:], A.mult, A.add)
-    tt("Pm", "slH M0", T.Pm[:], T.slH[:], T.M0[:], A.mult)
-    by_lanes("pEQ", "Pm Qh", T.pEQ[:, 0:16], T.Qh, T.Pm, True, True)
-    ts("oI", "pI", T.oI[:], T.pI[:], 1, None, AND)
-    ts("gI", "hI", T.gI[:], T.hI[:], 4, None, SH)
-    ts("colG", "colG", T.colG[:], T.colG[:], 16.0, None, A.add)
-    ts("cI", "xI", T.cI[:], T.xI[:], 1, None, SH)
-    ts("dI", "xI", T.dI[:], T.xI[:], 2, None, SH)
-    tt("colF", "oI gI", T.colF[:], T.oI[:], T.gI[:], A.not_equal)
-    ts("colA", "xF hF", T.colA[:], T.xF[:], 32.0, T.hF[:], A.mult, A.add)
+    ts("colF", "rI hF", T.colF[:], T.rI[:, 0:32:16], T.hF[:], None, A.is_equal)
     cp("of0", "xF", T.of0[:, 0:1], T.xF[:])
+    ts("colG", "colG", T.colG[:], T.colG[:], 16.0, None, A.add)
+    ts("Nc", "rI xF", T.Nc[:], T.rI[:, 0:16], T.xF[:], None, A.not_equal)
+    ts("colC", "xF", T.colC[:], T.xF[:], 2 * BIG, None, A.add)
+    ts("SW", "rI colG", T.SW[:], T.rI[:, 0:128], T.colG[:], None, A.is_equal)
+    for x in range(2):
+        for y in range(2):
+            act("MV%d" % (2 * x + y), "ID SW colF", T.MV[:, 256 * x + 128 * y:256 * x + 128 * y + 128], (T.ID if x == y else T.SW)[:], scale=T.colF[:, x:x + 1])
+    ts("CU", "rI xF colC", T.CU[:], T.rI[:, 0:16], T.xF[:], T.colC[:], A.is_equal, A.mult)
+    ts("slH", "slI", T.slH[:], T.slI[:], -HO, None, A.add)
+    ts("BO", "rB gF", T.BO[:], T.rB[:, 0:128], T.gF[:], None, A.is_equal)
+    tt("Pm", "slH M0", T.Pm[:], T.slH[:], T.M0[:], A.mult)
+    by_lanes("pEQ", "Pm Q1", T.pEQ[:, 0:16], T.Q1, T.Pm, True, True)
+    vtr("kTa", "slH", T.kTr[:], T.slH[:])
+    ts("DB", "rB xF", T.DB[:], T.rB[:], T.xF[:], None, A.is_equal)
     ts("cTu0", "pEQ", T.cTu[:, 0:16], T.pEQ[:, 0:16], HO, None, A.add)
     cp("cf0", "pEQ", T.CC[:, 16:32], T.pEQ[:, 0:16])
 
+    def by_places(more):
+        for b, out in [(b, T.pX[:, b:256:16]) for b in range(16)] + [(b, T.pX[:, 244 + b:320:4]) for b in range(12, 12 + more)]:
+            for y in range(2):
+                o, a = 256 * (b & 1) + 128 * y, 32 * (b >> 1) + 16 * y
+                mm("pX", "kTa MV0 MV1 MV2 MV3", out, T.MV[:, o:o + 128], T.kTr[:, a:a + 16], y == 0, y == 1)
+
+    def rolls(a, b):
+        cut = [16 * (5 * j % 16) for j in range(16)]
+        return [(a[j::16, 0:256 - cut[j]], b[j::16, cut[j]:256]) for j in range(16)] + [(a[j::16, 256 - cut[j]:256], b[j::16, 0:cut[j]]) for j in range(1, 16)]
+
+    by_places(0)
+    act("ZT", "pX", T.ZT[:], T.pX[:, 0:256])
+    dmas("Y", rolls(T.Z, T.ZT), "dsh", "Z", "ZT")
+
     def round_constants(t):
-        act("CC%d" % t, "CU", T.CC[:, 32 * t:32 * t + 16], T.CU[:], F.Identity, bias=16.0 * (t + 1) - 2 * BIG)
+        act("CC%d" % t, "CU", T.CC[:, 32 * t:32 * t + 16], T.CU[:], F.Identity, bias=16.0 * (128 + t + 1) - 2 * BIG)
         act("DBt%d" % t, "DB", T.DBt[:, 256 * t:256 * t + 256], T.DB[:], scale=8.0 + t)
         if t < RO - 1:
             act("NN%d" % t, "ID Nc", T.NN[:, 128 * t:128 * t + 128], T.ID[:], scale=T.Nc[:, t:t + 1])
 
-    def c_eq():
-        iota("rH", T.rH[:], [[1, 16], [0, 2]])
+    def numbers():
+        iota("IO0", T.IOTA[:, 0:1024], [[1, 1024]], -int(HO), **FL)
+        act("IO1", "IO0", T.IOTA[:, 1024:2048], T.IOTA[:, 0:1024], F.Identity, bias=1024.0)
+        iota("IO2", T.IOTA[:, 2048:3072], [[1, 1024]], 2048 - int(HO), **FL)
+
+    def by_gpsimd():
         iota("TIE", T.TIE[:], [[-1, 16], [0, 16]], 15, **FL)
-        iota("ON", T.ON[:], [[0, 128]], 16, **FL)
+        iota("ON", T.ON[:], [[0, 128]], -16, **FL)
         iota("MRK", T.MRK[:], [[0, 16]], -2 * int(HO), **FL)
-        ts("BO", "rB gF", T.BO[:], T.rB[:, 0:128], T.gF[:], None, A.is_equal)
-        ts("DB", "rB xF", T.DB[:], T.rB[:], T.xF[:], None, A.is_equal)
+        iota("rH", T.rH[:], [[1, 16], [0, 2]])
+        iota("Rd", T.R[:, W:WD], [[0, 256]], **FL)
+        iota("mv", T.mv[:, 0:1], [[0, 1]], **FL)
+        iota("tn", T.tn[:, 16:17], [[0, 1]], **FL)
+        iota("dc", T.dc[:, 0:1], [[0, 1]], **FL)
 
-    def c_kin():
-        ts("colF", "colF hF", T.colF[:], T.colF[:], 256.0, T.hF[:], A.mult, A.add)
-        ts("oI", "cI", T.oI[:], T.cI[:], 1, None, AND)
-        ts("SW", "rI colG", T.SW[:], T.rI[:, 0:128], T.colG[:], None, A.is_equal)
-        ts("colE", "cI colF", T.colE[:], T.cI[:], 32.0, T.colF[:], A.mult, A.add)
-        ts("colI", "oI colF", T.colI[:], T.oI[:], 32.0, T.colF[:], A.mult, A.add)
-        ts("LZ", "rJ colA", T.LZ[:], T.rJ[:, 0:32], T.colA[:], None, A.add)
-        ts("LP", "rI colE", T.LP[:, 0:16], T.rI[:, 0:16], T.colE[:], None, A.add)
-        ts("colI", "dI colI", T.colI[:], T.dI[:], 192.0, T.colI[:], A.add, A.add)
-        ts("Nc", "rI xF", T.Nc[:], T.rI[:, 0:16], T.xF[:], None, A.not_equal)
-        ts("colC", "xF", T.colC[:], T.xF[:], 2 * BIG, None, A.add)
-        ts("LP2", "rI colI", T.LP[:, 16:20], T.rI[:, 0:4], 4.0, T.colI[:], A.mult, A.add)
-        ts("CU", "rI xF colC", T.CU[:], T.rI[:, 0:16], T.xF[:], T.colC[:], A.is_equal, A.mult)
+    def for_sums():
         act("IDf", "ID", T.IDf[:], T.ID[:])
-        act("NEGf", "ID", T.NEGf[:], T.ID[:], scale=-1.0)
         act("NEG", "ID", T.NEG[:], T.ID[:], scale=-BIG)
-        act("Q16", "Q1", T.Q16[:], T.Q1[:], scale=16.0)
-        act("QF", "Q1", T.QF[:], T.Q1[:], scale=1.0 / 32.0)
-        act("DT", "DB", T.DT[:], T.DB[:], F.Identity, bias=1024.0, scale=1.0 / 128.0 - 1024.0)
+        act("QL", "Q1", T.QL[:], T.Q1[:], scale=1.0 / 16.0)
         round_constants(0)
+        fill("CZ", T.CZ[:, 0:16], 84.0 / 64.0)
+        fill("CZ2", T.CZ[:, 16:32], -36.0 / 64.0)
 
-    def c_z():
-        ts("L1", "rH xF", T.L1[:], T.rH[:], 16.0, T.xF[:], A.mult, A.add)
-        fill("CZ", T.CZ[:, 0:16], -5.0 / 64.0)
-        fill("CZ2", T.CZ[:, 16:32], 19.0 / 64.0)
-        ts("zA", "slI L1", T.zA[:], T.slI[:].indirect(T.L1[:, 0:32]), -HO, None, A.add)
-        fill("Rd", T.R[:, W:WD], 0.0)
-        vtr("zB", "zA", T.zB[:], T.zA[:])
-        act("ZT", "zB LZ", T.ZT[:], T.zB[:].indirect(T.LZ[:, 0:32]))
-        dmas("Y", [(T.Z[j::16, 0:256], T.ZT[j::16, 16 * (5 * j % 16):16 * (5 * j % 16) + 256]) for j in range(16)], "dsh", "Z", "ZT")
-
-    def c_late():
+    def for_fates():
+        act("Q16", "Q1", T.Q16[:], T.Q1[:], scale=16.0)
+        act("QF", "Q1", T.QF[:], T.Q1[:], scale=-1.0 / 16.0)
+        act("DT", "DB", T.DT[:], T.DB[:], F.Identity, bias=-1.0, scale=1.0 + 1.0 / 128.0)
+        act("POS", "ID", T.POS[:], T.ID[:], scale=BIG)
+        act("NEGf", "ID", T.NEGf[:], T.ID[:], scale=-1.0)
         ts("colE", "xF", T.colE[:], T.xF[:], -1.0, 15.0, A.mult, A.add)
-        ts("dm", "lane", T.dm[:], T.lane[:], W - BIG - HO, None, A.add)
+        ts("dm", "lane", T.dm[:], T.lane[:], W - HO, None, A.add)
+        ts("OH", "rI colE", T.OH[:], T.rI[:, 0:16], T.colE[:], None, A.is_equal)
+
+    def for_results():
         ts("colC", "xF", T.colC[:], T.xF[:], 16.0, None, A.mult)
         tt("colB", "xF hF", T.colB[:], T.xF[:], T.hF[:], A.add)
-        fill("mv", T.mv[:, 0:1], 0.0)
-        fill("tn", T.tn[:, 16:17], 0.0)
-        fill("dc", T.dc[:, 0:1], 0.0)
-        ts("QL", "Qh", T.QL[:], T.Qh[:], 1.0 / 16.0, None, A.mult)
-        ts("OH", "rI colE", T.OH[:], T.rI[:, 0:16], T.colE[:], None, A.is_equal)
         ts("L2", "rH colC", T.L2[:], T.rH[:], T.colC[:], None, A.add)
         ts("LQ", "rI colB", T.LQ[:], T.rI[:, 0:16], 32.0, T.colB[:], A.mult, A.add)
 
     def remote(dst, out, in_, rs, r):
-        eng = topo.engines(core, dst)[::2]
-        m = 0
-        for e in eng:
-            m |= 1 << e
+        eng = topo.engines(core, dst)
         rid, pid, _ = topo.addr(dst)
         dep("G", r.split(), [])
-        g.remote_dma(out, in_, sem[rs], sem.ls, pid, rid, m)
+        g.remote_dma(out, in_, sem[rs], sem.ls, pid, rid, topo.mask(core, dst))
         cnt["ls"] = cnt.get("ls", 0) + len(eng)
         return len(eng)
 
     OF = (T.of0, T.of1)
     ident = T.ID[:]
-    Rw, Kw, Ww, Iw, Zw = T.R[:, 0:W], T.K[:, 0:W], T.Wt[:], T.IOTA[:], T.Z[:, 0:256]
+    Rw, Kw, Ww, Iw, Zw = T.R[:, 0:W], T.K[:, 0:W], T.Wt[:], T.IOTA[:], T.Z[:]
     KK = " ".join("K%d" % i for i in range(W // KP))
 
     for t in range(RO):
@@ -309,7 +311,6 @@ def rank_program(g, core, T, topo):
         cf, cfk = T.CC[:, 32 * t + 16:32 * t + 32], "cf%d" % t
         of, ofk = OF[t % 2][:, 0:1], "of%d" % (t % 2)
         of2, of2k = OF[(t + 1) % 2][:, 0:1], "of%d" % ((t + 1) % 2)
-        fs = T.fs[:, 256 * t:256 * t + 256]
         last = t == RO - 1
         bar = -(8.0 + t - 3) + 1.0 / 64.0
         done = {}
@@ -374,12 +375,17 @@ def rank_program(g, core, T, topo):
             lastw["rl%d" % t] = ("ra%d" % t, ne)
 
         def answer():
+            fs = T.fs[:, 256 * t:256 * t + 256]
             act("fs%d" % t, "pFS", fs, T.pFS[:, 0:256])
             remote(asker, T.rl[:, 256 * t:256 * t + 256], fs, "ra%d" % t, "fs%d" % t)
 
+        def answer_sum():
+            mm("pA", "rl%d ID" % t, T.pA[:, 0:NA], ident, T.rl[:, 256 * t:256 * t + NA], False, True)
+            mm("pL", "rl%d ID" % t, T.pL[:, 0:64], ident, T.rl[:, 256 * t + NA:256 * t + 256], False, False)
+
         def own_kin():
             if t:
-                act("kcf", KK + " " + cuk, T.kcf[:], Kw.indirect(cu), F.Identity, bias=-(KO + HO))
+                ts("kcf", KK + " " + cuk, T.kcf[:], Kw.indirect(cu), -(KO + HO), None, A.add)
             else:
                 ts("kcf", "kinI " + cuk, T.kcf[:], T.kinI[:].indirect(cu), -HO, None, A.add)
 
@@ -390,13 +396,8 @@ def rank_program(g, core, T, topo):
                 cp("fku", "kinI " + quk, T.fku[:], T.kinI[:].indirect(qu))
 
         def own_wealth():
-            act("wc", "Wt " + cuk, T.wc[:, 0:256], Ww.indirect(cu))
+            (act if t else cp)("wc", "Wt " + cuk, T.wc[:, 0:256], Ww.indirect(cu))
             dmas("Y", [(T.wc[:, 256 * i:256 * i + 256], T.wc[:, 0:256]) for i in range(1, 4)], "dwc", "wcb", "wc")
-
-        def own_wealth_v():
-            cp("wc", "Wt " + cuk, T.wc[:, 0:256], Ww.indirect(cu))
-            cp("wcb", "wc", T.wc[:, 256:512], T.wc[:, 0:256])
-            cp("wcb", "wc wcb", T.wc[:, 512:1024], T.wc[:, 0:512])
 
         def scatter_records(u):
             tt("R Rd", "Rn SL DBt%d" % u, T.R[:].indirect(T.SL[:]), T.Rn[:], T.DBt[:, 256 * u:256 * u + 256], A.add)
@@ -407,7 +408,7 @@ def rank_program(g, core, T, topo):
 
         def best_kin():
             mm("pEQ", "NEGf " + cfk, T.pEQ[:, 0:16], T.NEGf[:], cf, True, False)
-            by_lanes("pEQ", "Pm Qh", T.pEQ[:, 0:16], T.Qh, T.Pm, False, True)
+            by_lanes("pEQ", "Pm Q1", T.pEQ[:, 0:16], T.Q1, T.Pm, False, True)
 
         def starts():
             mm("pZ", "CZ CZ2 ID", T.pZ[:, 0:32], ident, T.CZ[:], True, False)
@@ -419,34 +420,34 @@ def rank_program(g, core, T, topo):
             mm("pA", "Ec ID", T.pA[:, 0:NA], ident, T.Ec[:, 0:NA], True, False)
             mm("pL", "Ec ID", T.pL[:, 0:64], ident, T.Ec[:, NA:256], True, False)
 
-        def answer_sum():
-            mm("pA", "rl%d ID" % t, T.pA[:, 0:NA], ident, T.rl[:, 256 * t:256 * t + NA], False, True)
-            mm("pL", "rl%d ID" % t, T.pL[:, 0:64], ident, T.rl[:, 256 * t + NA:256 * t + 256], False, False)
-
         def new_kin():
             mm("pFS", "kcf NN%d" % t, T.pFS[:, 256:512], T.NN[:, 128 * t:128 * t + 128], T.kcf[:], True, False)
             for h in range(2):
                 mm("pFS", "cbh QL", T.pFS[:, 256 + h:512:2], T.QL[:, 15 - t:143 - t], T.cbh[:, 1 - h::2], False, h == 1)
 
         def installed():
-            mm("pX", "a1 NEG", T.pX[:, 16:32], T.NEG[:], T.a1[:], False, last)
+            mm("pX", "na POS", T.pX[:, 16:32], T.POS[:], T.na[:], False, last)
             if not last:
-                mm("pX", "a1 ON", T.pX[:, 0:16], T.ON[:], T.a1[:], False, True)
+                mm("pX", "na ON", T.pX[:, 0:16], T.ON[:], T.na[:], False, True)
+
+        def takes_best():
+            mm("pZ", "tn POS", T.pZ[:, 0:16], T.POS[:], T.tn[:, 0:16], True, False)
+            mm("pZ", "mv POS", T.pZ[:, 0:16], T.POS[:], T.mv[:, 1:17], False, False)
+            mm("pZ", "mv NEG", T.pZ[:, 0:16], T.NEG[:], T.mv[:, 0:16], False, True)
 
         def unroll():
-            cut = [16 * (5 * j % 16) for j in range(16)]
-            dmas("Y", [(T.ZT[j::16, cut[j]:256], T.Z[j::16, 0:256 - cut[j]]) for j in range(16)]
-                 + [(T.ZT[j::16, 0:cut[j]], T.Z[j::16, 256 - cut[j]:256]) for j in range(1, 16)], "dun", "ZT", "Z")
+            dmas("Y", [(b, a) for a, b in rolls(T.Z, T.ZT)], "dun", "ZT", "Z")
 
         def marks():
             act("MK", "zB LQ", T.MK[:], T.zB[:].indirect(T.LQ[:]), F.Relu, scale=-1.0, bias=RND + 1.0 - 2 * HO)
             act("SN", "zB LQ", T.SN[:], T.zB[:].indirect(T.LQ[:]), F.Abs, bias=HO - RND)
 
         STEP = {
-            "c_eq": c_eq, "c_kin": c_kin, "c_z": c_z, "c_late": c_late,
+            "numbers": numbers, "by_gpsimd": by_gpsimd, "for_sums": for_sums, "for_fates": for_fates, "for_results": for_results,
+            "Kd": lambda: act("Kd", "rI", T.K[:, W:WD], T.rI[:], F.Silu),
             "ask": ask, "answer": answer, "starts": starts, "Ec+": own_sum, "rl+": answer_sum, "Kn+": new_kin,
-            "wc": own_wealth, "wcV": own_wealth_v, "next": lambda: round_constants(t + 1), "Rn+": new_records, "Pm+": best_kin,
-            "a+": installed, "unroll": unroll, "marks": marks, "kcf": own_kin, "fku": asker_kin,
+            "wc": own_wealth, "next": lambda: round_constants(t + 1), "Rn+": new_records, "Pm+": best_kin,
+            "a+": installed, "q+": takes_best, "unroll": unroll, "marks": marks, "kcf": own_kin, "fku": asker_kin,
             "cbh": lambda: cp("cbh", IOTA + " " + cuk, T.cbh[:], Iw.indirect(cu)),
             "cf": lambda: ts(cfk, cuk, cf, cu, -HO, None, A.add),
             "R": lambda: scatter_records(t), "R0": lambda: scatter_records(t - 1),
@@ -454,10 +455,9 @@ def rank_program(g, core, T, topo):
             "Kn": lambda: act("Kn", "pFS", T.Kn[:], T.pFS[:, 256:512], F.Identity, bias=KO + HO),
             "K": lambda: act(KK + " Kd", "Kn SL", T.K[:].indirect(T.SL[:]), T.Kn[:], F.Silu),
             "kcu": lambda: ts("kcu", "kcf", T.kcu[:, 0:NA], T.kcf[:, 0:NA], HO + 0.25, None, A.add),
-            "kTa": lambda: vtr("kTa", "kcf", T.kTr[:, 0:256], T.kcf[:]),
-            "SW": lambda: mm("pX", "kTa SW", T.pX[:, 0:256], T.SW[:], T.kTr[:, 0:256], True, True),
-            "kTb": lambda: act("kTb", "pX", T.kTr[:, 256:512], T.pX[:, 0:256]),
-            "kTu": lambda: ts("kTu", "kTa kTb LP LP2", T.kTu[:], T.kTr[:].indirect(T.LP[:, 0:20]), HO + 0.25, None, A.add),
+            "kTa": lambda: vtr("kTa", "kcf", T.kTr[:], T.kcf[:]),
+            "kT+": lambda: by_places(4),
+            "kTu": lambda: ts("kTu", "pX", T.kTu[:], T.pX[:, 0:320], HO + 0.25, None, A.add),
             "Rc": lambda: act("Rc", "R " + cuk, T.Rc[:], Rw.indirect(cu)),
             "Ec": lambda: ts("Ec", "Rc", T.Ec[:], T.Rc[:], bar, 0.0, A.add, A.max),
             "cb": lambda: tt("cb", "pEQ THR", T.cb[:], T.pEQ[:, 0:256], T.THR[:], A.is_lt),
@@ -467,34 +467,36 @@ def rank_program(g, core, T, topo):
             "t2": lambda: tt("t2", "t1", T.t2[:], T.t1[:, 0:64], T.t1[:, 64:128], A.max),
             "t3": lambda: tt("t3", "t2", T.t1[:, 0:32], T.t2[:, 0:32], T.t2[:, 32:64], A.max),
             "t4": lambda: tt("t4", "t3", T.t2[:, 0:16], T.t1[:, 0:16], T.t1[:, 16:32], A.max),
-            "t5": lambda: tt("t5", "pS0 t4", T.t2[:, 16:32], T.pS0[:, 0:16], T.t2[:, 0:16], A.max),
-            "t6": lambda: tt("bI", "pS0 t5", T.bI[:], T.pS0[:, 16:32], T.t2[:, 16:32], A.max),
+            "t5": lambda: tt("t5", "pS0 t4", T.t2[:, 16:32], T.pS0[:, 16:32], T.t2[:, 0:16], A.max),
+            "t6": lambda: tt("bI", "pS0 t4 t5", T.bI[:], T.pS0[:, 0:16], T.t2[:, 0:16] if WL == 15 else T.t2[:, 16:32], A.max),
             "t7": lambda: ts("bI2", "bI", T.bI2[:], T.bI[:], 15, None, AND),
             "mu": lambda: cp("mu", "bI2", T.mu[:], T.bI2[:]),
             "Pm": lambda: tt("Pm", "OH mu kcf", T.Pm[:], T.OH[:].indirect(T.mu[:]), T.kcf[:], A.mult),
-            "X1a": lambda: ts("X1a", "pA", T.XX[:, 0:NA], T.pA[:, 0:NA], 0.75, -1.0 / 64.0, A.is_ge, A.mult),
-            "X2a": lambda: tt("X2a", "pA DT", T.XX[:, 256:256 + NA], T.pA[:, 0:NA], T.DT[:, 0:NA], A.is_ge),
-            "X1b": lambda: ts("X1b", "pL", T.XX[:, NA:256], T.pL[:, 0:64], 0.75, -1.0 / 64.0, A.is_ge, A.mult),
-            "X2b": lambda: tt("X2b", "pL DT", T.XX[:, 256 + NA:512], T.pL[:, 0:64], T.DT[:, NA:256], A.is_ge),
+            "X1a": lambda: ts("X1a", "pA", T.XX[:, 0:NA], T.pA[:, 0:NA], 0.75, 1.0 / 64.0, A.is_ge, A.mult),
+            "X2a": lambda: tt("X2a", "pA DT", T.XX[:, 256:256 + NA], T.pA[:, 0:NA], T.DT[:, 0:NA], A.is_lt),
+            "X1b": lambda: ts("X1b", "pL", T.XX[:, NA:256], T.pL[:, 0:64], 0.75, 1.0 / 64.0, A.is_ge, A.mult),
+            "X2b": lambda: tt("X2b", "pL DT", T.XX[:, 256 + NA:512], T.pL[:, 0:64], T.DT[:, NA:256], A.is_lt),
             "z+": lambda: by_lanes("pZ", "X1a X2a X1b X2b Q1", T.pZ[:, 0:32], T.Q1, T.XX, False, True),
             "zz": lambda: ts("zz", "pZ", T.zz[:], T.pZ[:, 0:32], 64.0, None, A.mult),
-            "a1": lambda: tt("a1", "zz", T.a1[:], T.zz[:, 0:16], T.zz[:, 16:32], A.is_gt),
-            "yy": lambda: ts("yy", "zz", T.yy[:], T.zz[:, 0:16], 4, None, SH),
-            "od": lambda: ts("od", "zz", T.od[:], T.zz[:, 0:16], 33, None, AND),
-            "tn": lambda: tt("tn", "a1 yy", T.tn[:, 0:16], T.yy[:], T.a1[:], A.is_equal),
+            "zn": lambda: ts("zn", "pZ", T.zn[:], T.pZ[:, 0:16], -64.0, 31.0, A.mult, A.add),
+            "na": lambda: tt("na", "zz", T.na[:], T.zz[:, 0:16], T.zz[:, 16:32], A.is_ge),
+            "yy": lambda: ts("yy", "zz", T.yy[:], T.zz[:, 0:16], 5, None, SH),
+            "od": lambda: ts("od", "zn", T.od[:], T.zn[:], 129, None, AND),
+            "tn": lambda: tt("tn", "na yy", T.tn[:, 0:16], T.yy[:], T.na[:], A.is_equal),
+            "pm": lambda: tt("pm", "na od", T.pm[:], T.od[:], T.na[:], A.is_lt),
             "m1": lambda: tt("m1", "pX dm", T.m1[:], T.pX[:, 16:32], T.dm[:], A.min),
-            "SL": lambda: ts("SL", "m1", T.SL[:], T.m1[:], BIG + HO, None, A.add),
+            "SL": lambda: ts("SL", "m1", T.SL[:], T.m1[:], HO, None, A.add),
             "um": lambda: op("V", lambda: g.vector.tensor_reduce(T.um[:], T.pX[:, 0:16], AxisListType.X, A.max), "um", "pX"),
             "uk": lambda: ts("uk", "um", T.uk[:], T.um[:], 1.0 / 256.0, -127.5 / 256.0, A.mult, A.add),
             "of": lambda: ts(of2k, "uk um", of2, T.uk[:], -256.0, T.um[:], A.mult, A.add),
             "dc": lambda: tt("dc", cfk, T.dc[:, 1:16], T.CC[:, 32 * t + 16:32 * t + 31], T.CC[:, 32 * t + 17:32 * t + 32], A.subtract),
-            "sn": lambda: tt("sn", "tn", T.sn[:], T.tn[:, 1:17], T.tn[:, 0:16], A.subtract),
-            "mv": lambda: tt("mv", "od sn", T.mv[:, 1:17], T.od[:], T.sn[:], A.is_lt),
-            "tm": lambda: tt("tm", "tn mv", T.tm[:], T.tn[:, 0:16], T.mv[:, 1:17], A.add),
+            "mv": lambda: tt("mv", "pm tn", T.mv[:, 1:17], T.pm[:], T.tn[:, 1:17], A.mult),
             "vv": lambda: tt("vv", "mv dc", T.vv[:], T.mv[:, 0:16], T.dc[:], A.mult),
-            "qq": lambda: tt("qq", "tm mv", T.qq[:], T.tm[:], T.mv[:, 0:16], A.subtract),
+            "D": lambda: act("D", "pEQ", T.D[:], T.pEQ[:, 0:16], scale=1.0 / BIG),
             "ub": lambda: tt("ub", "vv " + cfk, T.ub[:], T.vv[:], cf, A.add),
-            "sm": lambda: tt("sm", "pEQ qq", T.sm[:], T.pEQ[:, 0:16], T.qq[:], A.mult),
+            "sm": lambda: tt("sm", "pZ D", T.sm[:], T.pZ[:, 0:16], T.D[:], A.mult),
+            "Q": lambda: act("D", "pZ", T.D[:], T.pZ[:, 0:16], scale=1.0 / BIG),
+            "sq": lambda: tt("sm", "pEQ D", T.sm[:], T.pEQ[:, 0:16], T.D[:], A.mult),
             "Z": lambda: tt("Z", "sm ub " + ofk, Zw.indirect(of), T.sm[:], T.ub[:], A.add),
             "draw": lambda: ts("cTu%d" % (t + 1), "Z " + of2k, T.cTu[:, 16 * t + 16:16 * t + 32], Zw.indirect(of2), HO + 0.25, None, A.add),
             "mark": lambda: cp("Z", "MRK " + ofk, Zw.indirect(of), T.MRK[:]),
@@ -502,11 +504,7 @@ def rank_program(g, core, T, topo):
             "zB": lambda: vtr("zB", "zA", T.zB[:], T.zA[:]),
             "yr": lambda: dmas("Y", [(T.yr[:], T.R[:, 0:W])], "dyr", "", "R"),
         }
-        for name in (LATER if t else FIRST).split():
-            if name[0] in "*-":
-                if last != (name[0] == "*"):
-                    continue
-                name = name[1:]
+        for name in (LAST if last else LATER if t else FIRST).split():
             if name in STEP:
                 STEP[name]()
             else:
@@ -516,8 +514,8 @@ def rank_program(g, core, T, topo):
     tt("aa", "sm ub", T.aa[:], T.sm[:], T.ub[:], A.add)
     ts("mu", "aa", T.mu[:], T.aa[:], HO + 0.25, None, A.add)
     tt("Kn", IOTA + " mu MK", T.Kn[:], Iw.indirect(T.mu[:]), T.MK[:], A.mult)
-    tt("kcf", "Kn SN", T.kcf[:], T.Kn[:], T.SN[:], A.add)
-    dmas("S", [(T.ys[:], T.kcf[:])], "dys", "", "kcf")
+    tt("SN", "Kn SN", T.SN[:], T.Kn[:], T.SN[:], A.add)
+    dmas("S", [(T.ys[:], T.SN[:])], "dys", "", "SN")
     for s in cnt:
         if clock["G"].get(s, 0) < cnt[s]:
             g.wait_ge(sem[s], cnt[s])

import math
from concourse.mybir import AluOpType as A
from concourse.mybir import ActivationFunctionType as F
from concourse.mybir import AxisListType

RO = 6
W = 3072
WD = W + 256
NA = 192
BASE = 1.75
XB = [256 * b - 8 * b * (b - 1) for b in range(17)]
KO = 64.0
HO = 1536.0
BIG = 4096.0
RND = 1.5 * 2.0 ** 23
WL = 14
KP = 512
FIRST = ("ask numbers by_gpsimd for_fates K:0:2 for_sums K:2:2 kcf fku kTa kcu fV:168:88 kT+ cbh kTu eq:0:16 wc fS:0:72 Rc eq+:0:16 fS:72:96 Kn+ "
         "f+:0:64 f+:192:64 Ec f+:64:64 f+:128:64 gS:0:16 cb gS:136:56 gS:104:32 w:0:1 w:3:1 starts w:1:1 w:2:1 w:15:1 answer Rn+ K:4:1 gS:16:88 "
         "w:14:1 w:4:4 w+:0:4 Ec+ g+:128:64 lS:0:13 lS:13:3 cb+ w+:4:4 S1s g+:64:64 Kn g+:0:64 Rn rl+ w:8:3 w+:8:3 l+:0:13 next l.:13:3 w:11:3 "
         "X1a w+:11:3 X2a X1b X2b K:5:1 t1 t2 z+ zz dc t3 yy zn t4 na w+:14:2 od t5 tn pm t6 a+ um Kd m1 t7 mv uk SL mu vv of Pm R K ub Pm+ q+ D "
         "sm Z for_results draw")
LATER = ("ask Rc kcf Rn+ cf kcu wc gS:48:16 cbh kTa kT+ Kn+ gS:112:32 Ec Ec+ eq:0:6 eq:6:10 gS:0:48 g+:0:64 fku fS:0:56 kTu fV:184:72 eq+:0:6 starts "
         "f+:192:64 eq+:6:10 fS:56:72 fS:128:56 w:0:2 f+:0:64 gS:144:32 w:2:2 w:8:3 f+:64:64 f+:128:64 answer gS:64:48 w:4:4 w+:8:3 cb w+:0:4 w:11:3 "
         "lS:4:9 w+:4:4 cb+ gV:176:16 w:14:1 S1s g+:64:64 lS:0:4 w+:11:3 g+:128:64 l+:6:6 lS:13:3 rl+ l+:0:6 t1 w:15:1 t2 X2a l.:12:4 t3 w+:14:2 "
         "X1a X2b X1b t4 dc t5 t6 t7 z+ zz zn mu next yy od na Pm a+ tn Rn Pm+ pm m1 Kn um mv D SL uk q+ vv R sm ub K of Z draw")
LAST = ("ask kcf mark Rc wc cf kcu gS:0:32 gS:32:24 Ec cbh gV:184:8 kTa gS:56:24 eq:0:6 fku kT+ Rn+ eq:6:10 kTu unroll fS:0:72 Ec+ fV:184:72 eq+:0:6 "
        "fS:88:96 g+:0:64 f+:192:64 starts eq+:6:10 fS:72:16 w:4:4 f+:0:64 f+:64:64 f+:128:64 gS:80:48 cb w:0:2 w:2:2 cb+ lV:10:6 g+:64:64 w:8:3 "
        "answer lS:5:5 w+:0:4 w+:4:4 l+:6:6 w+:8:3 gS:128:56 w:11:3 g+:128:64 rl+ w:15:1 lS:0:5 l+:0:6 l.:12:4 X1a X2a X2b X1b w+:11:3 w:14:1 Rn "
        "z+ S1s t1 t2 zz zn t3 w+:14:2 na a+ t4 t5 m1 yy t6 SL od t7 R yr mu Pm zA pm tn dc mv zB vv ub Pm+ D marks q+ sm")

SCRATCH = {}


def _bufs(where, n, dtype, names):
    for k in names.split():
        SCRATCH[k] = (where, [128, n], dtype)


_bufs("sbuf", W, "bfloat16", "Wt")
_bufs("sbuf", W, "int32", "kinI")
_bufs("sbuf", W, "float32", "IOTA")
_bufs("sbuf", WD, "bfloat16", "R")
_bufs("sbuf", WD, "float32", "K")
_bufs("sbuf", 4096, "bfloat16", "GE FE X")
_bufs("sbuf", XB[16], "bfloat16", "EQT")
_bufs("sbuf", 512, "float32", "zA zB")
_bufs("sbuf", 256, "int32", "slI rJ rB")
_bufs("sbuf", 256, "uint16", "kcu fku")
_bufs("sbuf", 320, "uint16", "kTu")
_bufs("sbuf", 256, "float32", "Z ZT Kn THR DT rI SN MK")
_bufs("sbuf", 256, "float16", "Pm slH M0 cbh kcf kTr")
_bufs("sbuf", 1024, "bfloat16", "wc")
_bufs("sbuf", 512, "bfloat16", "XX MV")
_bufs("sbuf", 256 * RO, "bfloat16", "DBt")
_bufs("sbuf", 128, "float32", "S1s t1 IDf NEGf")
_bufs("sbuf", 128 * (RO - 1), "bfloat16", "NN")
_bufs("sbuf", 256, "bfloat16", "Ec Rc Rn TIE cb DB")
_bufs("sbuf", 16, "int32", "bI bI2 od yy zn")
_bufs("sbuf", 32, "int32", "zz rH")
_bufs("sbuf", 16, "uint16", "mu SL LQ")
_bufs("sbuf", 16, "float32", "m1 pm D aa ub vv sm dc lane dm wcol OH MRK CU Nc")
_bufs("sbuf", 32, "bfloat16", "tn mv")
_bufs("sbuf", 16, "bfloat16", "na")
_bufs("sbuf", 32, "bfloat16", "CZ")
_bufs("sbuf", 32, "uint16", "L2")
_bufs("sbuf", 64, "float32", "t2")
_bufs("sbuf", 32 * RO, "float32", "CC")
_bufs("sbuf", 128, "bfloat16", "BO ID ON NEG POS SW")
_bufs("sbuf", 144, "bfloat16", "Q16 Q1 QF QL")
_bufs("sbuf", 1, "int32", "pI xI gI hI uk cI dI")
_bufs("sbuf", 1, "float32", "pF xF gF hF um colB colC colD colE colG colH")
_bufs("sbuf", 2, "float32", "colF")
_bufs("sbuf", 2, "uint16", "of0 of1")
_bufs("psum", 512, "float32", "pA pL pFS pEQ pS0 pS1 pZ pX")
_bufs("sbuf", 16 * RO, "uint16", "cTu ql")
_bufs("sbuf", 256 * RO, "bfloat16", "fs rl")
SEMAPHORES = ["sv", "ss", "sp", "sg", "ls", "dsl", "dsh", "dun", "dys", "dyr", "dw", "dr", "dk", "dwc"] \
    + [s % t for s in ("qa%d", "ra%d") for t in range(RO)]


def rank_program(g, core, T, topo):
    rank = T.rank_of(core)
    if rank is None:
        return
    sem = T.sem
    ENG = {"V": g.vector, "S": g.scalar, "P": g.tensor, "G": g, "Y": g.sync}
    SEM = {"V": "sv", "S": "ss", "P": "sp", "G": "sg"}
    BANKS = [k for k in SCRATCH if SCRATCH[k][0] == "psum"]
    cnt = {}
    clock = {"V": {}, "S": {}, "P": {}, "G": {}, "Y": {}}
    snap = {}
    lastw = {}
    lastr = {}

    def dep(q, r, w):
        need = {}

        def add(tok, war):
            s, n = tok
            if war and q == "P" and s == "sp":
                return
            if need.get(s, 0) < n:
                need[s] = n
        for k in r:
            if k in lastw:
                add(lastw[k], False)
            if k in BANKS:
                for s, n in lastr.get(k, {}).items():
                    if s != SEM[q]:
                        add((s, n), False)
        for k in w:
            if k in lastw:
                add(lastw[k], True)
            for s, n in lastr.get(k, {}).items():
                add((s, n), True)
        ck = clock[q]
        for s in sorted(need, key=lambda s: -len(snap.get((s, need[s]), {}))):
            n = need[s]
            if ck.get(s, 0) < n:
                ENG[q].wait_ge(sem[s], n)
                ck[s] = n
                for s2, n2 in snap.get((s, n), {}).items():
                    if ck.get(s2, 0) < n2:
                        ck[s2] = n2

    def mark(q, tok, r, w):
        snap[tok] = dict(clock[q])
        for k in w:
            lastw[k] = tok
            lastr[k] = {}
        for k in r:
            d = lastr.setdefault(k, {})
            if d.get(tok[0], 0) < tok[1]:
                d[tok[0]] = tok[1]

    def op(q, fn, w, r):
        w, r = w.split(), r.split()
        dep(q, r, w)
        s = SEM[q]
        fn().then_inc(sem[s], 1)
        cnt[s] = cnt.get(s, 0) + 1
        mark(q, (s, cnt[s]), r, w)

    def dmas(q, pairs, s, w, r):
        w, r = w.split(), r.split()
        dep(q, r, w)
        for o, i in pairs:
            ENG[q].dma_start(o, i).then_inc(sem[s], 16)
            cnt[s] = cnt.get(s, 0) + 16
        mark(q, (s, cnt[s]), r, w)

    def ts(w, r, out, in0, s1, s2, op0, op1=None):
        if op1 is None:
            op("V", lambda: g.vector.tensor_scalar(out, in0, s1, None, op0), w, r)
        else:
            op("V", lambda: g.vector.tensor_scalar(out, in0, s1, s2, op0, op1), w, r)

    def tt(w, r, out, a, b, o):
        op("V", lambda: g.vector.tensor_tensor(out, a, b, o), w, r)

    def cp(w, r, out, in_):
        op("V", lambda: g.vector.tensor_copy(out, in_), w, r)

    def fill(w, ap, v):
        op("V", lambda: g.vector.memset(ap, v), w, "")

    def vtr(w, r, out, in_):
        op("V", lambda: g.vector.transpose(out, in_), w, r)

    def act(w, r, out, in_, f=F.Copy, **k):
        op("S", lambda: g.scalar.activation(out, in_, f, **k), w, r)

    def mm(w, r, out, l, x, st, sp):
        op("P", lambda: g.tensor.matmul(out, l, x, st, sp), w, r)

    def iota(w, out, pat, base=0, cm=0, **k):
        op("G", lambda: g.iota(out, pat, base, cm, **k), w, "")

    def by_lanes(w, r, out, sel, x, st, sp):
        for j in range(16):
            mm(w, r, out, sel[:, 15 - j:143 - j], x[:, j::16], st and j == 0, sp and j == 15)

    dmas("Y", [(T.slI[:], T.slips[:])], "dsl", "slI", "")
    dmas("Y", [(T.kinI[:], T.kin[:])], "dk", "kinI", "")
    dmas("Y", [(T.R[:, 0:W], T.rec[:])], "dr", "R", "")
    dmas("Y", [(T.Wt[:], T.wealth[:])], "dw", "Wt", "")

    SH, AND = A.arith_shift_right, A.bitwise_and
    FL = dict(allow_small_or_imprecise_dtypes=True)
    iota("pI", T.pI[:], [[0, 1]], 0, 1)
    iota("rI", T.rI[:], [[1, 256]], **FL)
    iota("rJ", T.rJ[:], [[0, 16], [1, 16]])
    iota("rB", T.rB[:], [[1, 16], [0, 16]])
    ts("xI", "pI", T.xI[:], T.pI[:], 15, None, AND)
    ts("gI", "pI", T.gI[:], T.pI[:], 4, None, SH)
    ts("cI", "pI", T.cI[:], T.pI[:], 13.0, None, A.mult)
    ts("hI", "pI", T.hI[:], T.pI[:], 16, None, AND)
    cp("xF", "xI", T.xF[:], T.xI[:])
    ts("colD", "gI", T.colD[:], T.gI[:], 16.0, 15.0, A.mult, A.add)
    ts("dI", "cI", T.dI[:], T.cI[:], 15, None, AND)
    cp("hF", "hI", T.hF[:], T.hI[:])
    cp("pF", "pI", T.pF[:], T.pI[:])
    cp("gF", "gI", T.gF[:], T.gI[:])
    cp("colH", "dI", T.colH[:], T.dI[:])
    ts("lane", "rI xF", T.lane[:], T.rI[:, 0:16], 16.0, T.xF[:], A.mult, A.add)
    ts("ID", "rI pF", T.ID[:], T.rI[:, 0:128], T.pF[:], None, A.is_equal)
    ts("Q1", "rI colD", T.Q1[:], T.rI[:, 0:144], T.colD[:], None, A.is_equal)
    ts("M0", "rJ colH", T.M0[:], T.rJ[:], T.colH[:], None, A.is_equal)
    LB = math.log(BASE)
    act("wcol", "lane", T.wcol[:], T.lane[:], F.Exp, bias=71.0, scale=-LB)
    act("THR", "rI", T.THR[:], T.rI[:], F.Exp, bias=71.0 + math.log(2.53), scale=-LB)
    IOTA = "IO0 IO1 IO2"
    ts("colG", "hF pF", T.colG[:], T.hF[:], -2.0, T.pF[:], A.mult, A.add)
    ts("colF", "rI hF", T.colF[:], T.rI[:, 0:32:16], T.hF[:], None, A.is_equal)
    cp("of0", "xF", T.of0[:, 0:1], T.xF[:])
    ts("colG", "colG", T.colG[:], T.colG[:], 16.0, None, A.add)
    ts("Nc", "rI xF", T.Nc[:], T.rI[:, 0:16], T.xF[:], None, A.not_equal)
    ts("colC", "xF", T.colC[:], T.xF[:], 2 * BIG, None, A.add)
    ts("SW", "rI colG", T.SW[:], T.rI[:, 0:128], T.colG[:], None, A.is_equal)
    for x in range(2):
        for y in range(2):
            act("MV%d" % (2 * x + y), "ID SW colF", T.MV[:, 256 * x + 128 * y:256 * x + 128 * y + 128], (T.ID if x == y else T.SW)[:], scale=T.colF[:, x:x + 1])
    ts("CU", "rI xF colC", T.CU[:], T.rI[:, 0:16], T.xF[:], T.colC[:], A.is_equal, A.mult)
    ts("slH", "slI", T.slH[:], T.slI[:], -HO, None, A.add)
    ts("BO", "rB gF", T.BO[:], T.rB[:, 0:128], T.gF[:], None, A.is_equal)
    tt("Pm", "slH M0", T.Pm[:], T.slH[:], T.M0[:], A.mult)
    by_lanes("pEQ", "Pm Q1", T.pEQ[:, 0:16], T.Q1, T.Pm, True, True)
    vtr("kTa", "slH", T.kTr[:], T.slH[:])
    ts("DB", "rB xF", T.DB[:], T.rB[:], T.xF[:], None, A.is_equal)
    ts("cTu0", "pEQ", T.cTu[:, 0:16], T.pEQ[:, 0:16], HO, None, A.add)
    cp("cf0", "pEQ", T.CC[:, 16:32], T.pEQ[:, 0:16])

    def by_places(more):
        for b, out in [(b, T.pX[:, b:256:16]) for b in range(16)] + [(b, T.pX[:, 244 + b:320:4]) for b in range(12, 12 + more)]:
            for y in range(2):
                o, a = 256 * (b & 1) + 128 * y, 32 * (b >> 1) + 16 * y
                mm("pX", "kTa MV0 MV1 MV2 MV3", out, T.MV[:, o:o + 128], T.kTr[:, a:a + 16], y == 0, y == 1)

    def rolls(a, b):
        cut = [16 * (5 * j % 16) for j in range(16)]
        return [(a[j::16, 0:256 - cut[j]], b[j::16, cut[j]:256]) for j in range(16)] + [(a[j::16, 256 - cut[j]:256], b[j::16, 0:cut[j]]) for j in range(1, 16)]

    by_places(0)
    act("ZT", "pX", T.ZT[:], T.pX[:, 0:256])
    dmas("Y", rolls(T.Z, T.ZT), "dsh", "Z", "ZT")

    def round_constants(t):
        act("CC%d" % t, "CU", T.CC[:, 32 * t:32 * t + 16], T.CU[:], F.Identity, bias=16.0 * (128 + t + 1) - 2 * BIG)
        act("DBt%d" % t, "DB", T.DBt[:, 256 * t:256 * t + 256], T.DB[:], scale=8.0 + t)
        if t < RO - 1:
            act("NN%d" % t, "ID Nc", T.NN[:, 128 * t:128 * t + 128], T.ID[:], scale=T.Nc[:, t:t + 1])

    def numbers():
        iota("IO0", T.IOTA[:, 0:1024], [[1, 1024]], -int(HO), **FL)
        act("IO1", "IO0", T.IOTA[:, 1024:2048], T.IOTA[:, 0:1024], F.Identity, bias=1024.0)
        iota("IO2", T.IOTA[:, 2048:3072], [[1, 1024]], 2048 - int(HO), **FL)

    def by_gpsimd():
        iota("TIE", T.TIE[:], [[-1, 16], [0, 16]], 15, **FL)
        iota("ON", T.ON[:], [[0, 128]], -16, **FL)
        iota("MRK", T.MRK[:], [[0, 16]], -2 * int(HO), **FL)
        iota("rH", T.rH[:], [[1, 16], [0, 2]])
        iota("Rd", T.R[:, W:WD], [[0, 256]], **FL)
        iota("mv", T.mv[:, 0:1], [[0, 1]], **FL)
        iota("tn", T.tn[:, 16:17], [[0, 1]], **FL)
        iota("dc", T.dc[:, 0:1], [[0, 1]], **FL)

    def for_sums():
        act("IDf", "ID", T.IDf[:], T.ID[:])
        act("NEG", "ID", T.NEG[:], T.ID[:], scale=-BIG)
        act("QL", "Q1", T.QL[:], T.Q1[:], scale=1.0 / 16.0)
        round_constants(0)
        fill("CZ", T.CZ[:, 0:16], 84.0 / 64.0)
        fill("CZ2", T.CZ[:, 16:32], -36.0 / 64.0)

    def for_fates():
        act("Q16", "Q1", T.Q16[:], T.Q1[:], scale=16.0)
        act("QF", "Q1", T.QF[:], T.Q1[:], scale=-1.0 / 16.0)
        act("DT", "DB", T.DT[:], T.DB[:], F.Identity, bias=-1.0, scale=1.0 + 1.0 / 128.0)
        act("POS", "ID", T.POS[:], T.ID[:], scale=BIG)
        act("NEGf", "ID", T.NEGf[:], T.ID[:], scale=-1.0)
        ts("colE", "xF", T.colE[:], T.xF[:], -1.0, 15.0, A.mult, A.add)
        ts("dm", "lane", T.dm[:], T.lane[:], W - HO, None, A.add)
        ts("OH", "rI colE", T.OH[:], T.rI[:, 0:16], T.colE[:], None, A.is_equal)

    def for_results():
        ts("colC", "xF", T.colC[:], T.xF[:], 16.0, None, A.mult)
        tt("colB", "xF hF", T.colB[:], T.xF[:], T.hF[:], A.add)
        ts("L2", "rH colC", T.L2[:], T.rH[:], T.colC[:], None, A.add)
        ts("LQ", "rI colB", T.LQ[:], T.rI[:, 0:16], 32.0, T.colB[:], A.mult, A.add)

    def remote(dst, out, in_, rs, r):
        eng = topo.engines(core, dst)
        rid, pid, _ = topo.addr(dst)
        dep("G", r.split(), [])
        g.remote_dma(out, in_, sem[rs], sem.ls, pid, rid, topo.mask(core, dst))
        cnt["ls"] = cnt.get("ls", 0) + len(eng)
        return len(eng)

    OF = (T.of0, T.of1)
    ident = T.ID[:]
    Rw, Kw, Ww, Iw, Zw = T.R[:, 0:W], T.K[:, 0:W], T.Wt[:], T.IOTA[:], T.Z[:]
    KK = " ".join("K%d" % i for i in range(W // KP))

    for t in range(RO):
        asked = T.cores[(rank + 1 + t % 3) % 4]
        asker = T.cores[(rank - 1 - t % 3) % 4]
        cu, cuk = T.cTu[:, 16 * t:16 * t + 16], "cTu%d" % t
        qu, quk = T.ql[:, 16 * t:16 * t + 16], "ql%d" % t
        cf, cfk = T.CC[:, 32 * t + 16:32 * t + 32], "cf%d" % t
        of, ofk = OF[t % 2][:, 0:1], "of%d" % (t % 2)
        of2, of2k = OF[(t + 1) % 2][:, 0:1], "of%d" % ((t + 1) % 2)
        last = t == RO - 1
        bar = -(8.0 + t - 3) + 1.0 / 64.0
        done = {}

        def pieces(pre, a, n):
            return " ".join(k for k, (x, y) in done.items() if k.startswith(pre) and x < a + n and y > a)

        def levels(eng, out, key, lst, lk):
            if eng == "S":
                act(key, "R " + lk, out, Rw.indirect(lst), F.Relu, bias=bar)
            else:
                ts(key, "R " + lk, out, Rw.indirect(lst), bar, 0.0, A.add, A.max)

        def sum_kin(ps, pk, src, keys, a, n, whole):
            for m in range(16):
                mm(pk, keys + " ID", ps[:, a:a + n], ident, src[:, 16 * a + m:16 * (a + n):16], whole and m == 0, whole and m == 15)

        def piece(k, a, n):
            if k[0] in "gfl" and k[1] in "SV":
                key = "%sE%d" % (k[0], a)
                done[key] = (a, a + n)
                if k[0] == "g":
                    levels(k[1], T.GE[:, 16 * a:16 * (a + n)], key, T.kcu[:, a:a + n], "kcu")
                elif k[0] == "f":
                    levels(k[1], T.FE[:, 16 * a:16 * (a + n)], key, T.fku[:, a:a + n], "fku")
                else:
                    levels(k[1], T.GE[:, 16 * NA + 64 * a:16 * NA + 64 * (a + n)], key, T.kTu[:, 256 + 4 * a:256 + 4 * (a + n)], "kTu")
            elif k == "g+":
                sum_kin(T.pA, "pA", T.GE, pieces("gE", a, n), a, n, False)
            elif k == "f+":
                sum_kin(T.pFS, "pFS", T.FE, pieces("fE", a, n), a, n, True)
            elif k in ("l+", "l."):
                for m in range(a, a + n):
                    o = 16 * NA + 64 * m
                    mm("pL", pieces("lE", m, 1) + " ID", T.pL[:, 0:64], ident, T.GE[:, o:o + 64], False, k == "l." and m == a + n - 1)
            elif k == "w":
                done["X%d" % a] = (a, a + n)
                tt("X%d" % a, "Wt kTu wc" + (" wcb" if n > 1 else ""), T.X[:, 256 * a:256 * (a + n)], Ww.indirect(T.kTu[:, 16 * a:16 * (a + n)]),
                   T.wc[:, 0:256 * n], A.max)
            elif k == "w+":
                h, o = (0, 16 * a) if a < 8 else (1, 16 * (a - 8)) if a < WL else (0, 16 * (a - WL))
                if a == WL:
                    mm("pS0", "TIE ID", T.pS0[:, 0:16 * n], ident, T.TIE[:, 16 * WL:256], True, False)
                for j in range(16):
                    mm("pS%d" % h, pieces("X", a, n) + " Q16", (T.pS0, T.pS1)[h][:, o:o + 16 * n], T.Q16[:, 15 - j:143 - j],
                       T.X[:, 256 * a + j:256 * (a + n):16], False, j == 15 and a + n in (8, WL, 16))
            else:
                for b in range(a, a + n):
                    if k == "K":
                        ts("K%d" % b, "kinI", T.K[:, KP * b:KP * b + KP], T.kinI[:, KP * b:KP * b + KP], KO, None, A.add)
                        continue
                    o, w = XB[b], 256 - 16 * b
                    if k == "eq":
                        ts("EQT%d" % b, "cbh wcol " + cfk, T.EQT[:, o:o + w], T.cbh[:, 16 * b:256], T.CC[:, 32 * t + 16 + b:32 * t + 17 + b],
                           T.wcol[:, b:b + 1], A.is_equal, A.mult)
                    else:
                        mm("pEQ", "EQT%d BO" % b, T.pEQ[:, 16 * b:256], T.BO[:], T.EQT[:, o:o + w], b == 0, b == 15)

        def ask():
            ne = remote(asked, qu, cu, "qa%d" % t, cuk)
            lastw[quk] = ("qa%d" % t, ne)
            lastw["rl%d" % t] = ("ra%d" % t, ne)

        def answer():
            fs = T.fs[:, 256 * t:256 * t + 256]
            act("fs%d" % t, "pFS", fs, T.pFS[:, 0:256])
            remote(asker, T.rl[:, 256 * t:256 * t + 256], fs, "ra%d" % t, "fs%d" % t)

        def answer_sum():
            mm("pA", "rl%d ID" % t, T.pA[:, 0:NA], ident, T.rl[:, 256 * t:256 * t + NA], False, True)
            mm("pL", "rl%d ID" % t, T.pL[:, 0:64], ident, T.rl[:, 256 * t + NA:256 * t + 256], False, False)

        def own_kin():
            if t:
                ts("kcf", KK + " " + cuk, T.kcf[:], Kw.indirect(cu), -(KO + HO), None, A.add)
            else:
                ts("kcf", "kinI " + cuk, T.kcf[:], T.kinI[:].indirect(cu), -HO, None, A.add)

        def asker_kin():
            if t:
                ts("fku", KK + " " + quk, T.fku[:], Kw.indirect(qu), 0.25 - KO, None, A.add)
            else:
                cp("fku", "kinI " + quk, T.fku[:], T.kinI[:].indirect(qu))

        def own_wealth():
            (act if t else cp)("wc", "Wt " + cuk, T.wc[:, 0:256], Ww.indirect(cu))
            dmas("Y", [(T.wc[:, 256 * i:256 * i + 256], T.wc[:, 0:256]) for i in range(1, 4)], "dwc", "wcb", "wc")

        def scatter_records(u):
            tt("R Rd", "Rn SL DBt%d" % u, T.R[:].indirect(T.SL[:]), T.Rn[:], T.DBt[:, 256 * u:256 * u + 256], A.add)

        def new_records():
            mm("pEQ", "Rc ID", T.pEQ[:, 256:512], ident, T.Rc[:], True, False)
            mm("pEQ", "DB NEG", T.pEQ[:, 256:512], T.NEG[:], T.DB[:], False, True)

        def best_kin():
            mm("pEQ", "NEGf " + cfk, T.pEQ[:, 0:16], T.NEGf[:], cf, True, False)
            by_lanes("pEQ", "Pm Q1", T.pEQ[:, 0:16], T.Q1, T.Pm, False, True)

        def starts():
            mm("pZ", "CZ CZ2 ID", T.pZ[:, 0:32], ident, T.CZ[:], True, False)
            mm("pX", "CC%d IDf %s" % (t, cfk), T.pX[:, 0:32], T.IDf[:], T.CC[:, 32 * t:32 * t + 32], True, False)
            for h in range(2):
                mm("pS%d" % h, "TIE ID", (T.pS0, T.pS1)[h][:, 0:128], ident, T.TIE[:, 128 * h:128 * h + 128], True, False)

        def own_sum():
            mm("pA", "Ec ID", T.pA[:, 0:NA], ident, T.Ec[:, 0:NA], True, False)
            mm("pL", "Ec ID", T.pL[:, 0:64], ident, T.Ec[:, NA:256], True, False)

        def new_kin():
            mm("pFS", "kcf NN%d" % t, T.pFS[:, 256:512], T.NN[:, 128 * t:128 * t + 128], T.kcf[:], True, False)
            for h in range(2):
                mm("pFS", "cbh QL", T.pFS[:, 256 + h:512:2], T.QL[:, 15 - t:143 - t], T.cbh[:, 1 - h::2], False, h == 1)

        def installed():
            mm("pX", "na POS", T.pX[:, 16:32], T.POS[:], T.na[:], False, last)
            if not last:
                mm("pX", "na ON", T.pX[:, 0:16], T.ON[:], T.na[:], False, True)

        def takes_best():
            mm("pZ", "tn POS", T.pZ[:, 0:16], T.POS[:], T.tn[:, 0:16], True, False)
            mm("pZ", "mv POS", T.pZ[:, 0:16], T.POS[:], T.mv[:, 1:17], False, False)
            mm("pZ", "mv NEG", T.pZ[:, 0:16], T.NEG[:], T.mv[:, 0:16], False, True)

        def unroll():
            dmas("Y", [(b, a) for a, b in rolls(T.Z, T.ZT)], "dun", "ZT", "Z")

        def marks():
            act("MK", "zB LQ", T.MK[:], T.zB[:].indirect(T.LQ[:]), F.Relu, scale=-1.0, bias=RND + 1.0 - 2 * HO)
            act("SN", "zB LQ", T.SN[:], T.zB[:].indirect(T.LQ[:]), F.Abs, bias=HO - RND)

        STEP = {
            "numbers": numbers, "by_gpsimd": by_gpsimd, "for_sums": for_sums, "for_fates": for_fates, "for_results": for_results,
            "Kd": lambda: act("Kd", "rI", T.K[:, W:WD], T.rI[:], F.Silu),
            "ask": ask, "answer": answer, "starts": starts, "Ec+": own_sum, "rl+": answer_sum, "Kn+": new_kin,
            "wc": own_wealth, "next": lambda: round_constants(t + 1), "Rn+": new_records, "Pm+": best_kin,
            "a+": installed, "q+": takes_best, "unroll": unroll, "marks": marks, "kcf": own_kin, "fku": asker_kin,
            "cbh": lambda: cp("cbh", IOTA + " " + cuk, T.cbh[:], Iw.indirect(cu)),
            "cf": lambda: ts(cfk, cuk, cf, cu, -HO, None, A.add),
            "R": lambda: scatter_records(t), "R0": lambda: scatter_records(t - 1),
            "Rn": lambda: act("Rn", "pEQ", T.Rn[:], T.pEQ[:, 256:512], F.Relu),
            "Kn": lambda: act("Kn", "pFS", T.Kn[:], T.pFS[:, 256:512], F.Identity, bias=KO + HO),
            "K": lambda: act(KK + " Kd", "Kn SL", T.K[:].indirect(T.SL[:]), T.Kn[:], F.Silu),
            "kcu": lambda: ts("kcu", "kcf", T.kcu[:, 0:NA], T.kcf[:, 0:NA], HO + 0.25, None, A.add),
            "kTa": lambda: vtr("kTa", "kcf", T.kTr[:], T.kcf[:]),
            "kT+": lambda: by_places(4),
            "kTu": lambda: ts("kTu", "pX", T.kTu[:], T.pX[:, 0:320], HO + 0.25, None, A.add),
            "Rc": lambda: act("Rc", "R " + cuk, T.Rc[:], Rw.indirect(cu)),
            "Ec": lambda: ts("Ec", "Rc", T.Ec[:], T.Rc[:], bar, 0.0, A.add, A.max),
            "cb": lambda: tt("cb", "pEQ THR", T.cb[:], T.pEQ[:, 0:256], T.THR[:], A.is_lt),
            "cb+": lambda: by_lanes("pZ", "cb QF", T.pZ[:, 0:16], T.QF, T.cb, False, False),
            "S1s": lambda: act("S1s", "pS0", T.S1s[:], T.pS0[:, 0:128]),
            "t1": lambda: tt("t1", "pS1 S1s", T.t1[:], T.pS1[:, 0:128], T.S1s[:], A.max),
            "t2": lambda: tt("t2", "t1", T.t2[:], T.t1[:, 0:64], T.t1[:, 64:128], A.max),
            "t3": lambda: tt("t3", "t2", T.t1[:, 0:32], T.t2[:, 0:32], T.t2[:, 32:64], A.max),
            "t4": lambda: tt("t4", "t3", T.t2[:, 0:16], T.t1[:, 0:16], T.t1[:, 16:32], A.max),
            "t5": lambda: tt("t5", "pS0 t4", T.t2[:, 16:32], T.pS0[:, 16:32], T.t2[:, 0:16], A.max),
            "t6": lambda: tt("bI", "pS0 t4 t5", T.bI[:], T.pS0[:, 0:16], T.t2[:, 0:16] if WL == 15 else T.t2[:, 16:32], A.max),
            "t7": lambda: ts("bI2", "bI", T.bI2[:], T.bI[:], 15, None, AND),
            "mu": lambda: cp("mu", "bI2", T.mu[:], T.bI2[:]),
            "Pm": lambda: tt("Pm", "OH mu kcf", T.Pm[:], T.OH[:].indirect(T.mu[:]), T.kcf[:], A.mult),
            "X1a": lambda: ts("X1a", "pA", T.XX[:, 0:NA], T.pA[:, 0:NA], 0.75, 1.0 / 64.0, A.is_ge, A.mult),
            "X2a": lambda: tt("X2a", "pA DT", T.XX[:, 256:256 + NA], T.pA[:, 0:NA], T.DT[:, 0:NA], A.is_lt),
            "X1b": lambda: ts("X1b", "pL", T.XX[:, NA:256], T.pL[:, 0:64], 0.75, 1.0 / 64.0, A.is_ge, A.mult),
            "X2b": lambda: tt("X2b", "pL DT", T.XX[:, 256 + NA:512], T.pL[:, 0:64], T.DT[:, NA:256], A.is_lt),
            "z+": lambda: by_lanes("pZ", "X1a X2a X1b X2b Q1", T.pZ[:, 0:32], T.Q1, T.XX, False, True),
            "zz": lambda: ts("zz", "pZ", T.zz[:], T.pZ[:, 0:32], 64.0, None, A.mult),
            "zn": lambda: ts("zn", "pZ", T.zn[:], T.pZ[:, 0:16], -64.0, 31.0, A.mult, A.add),
            "na": lambda: tt("na", "zz", T.na[:], T.zz[:, 0:16], T.zz[:, 16:32], A.is_ge),
            "yy": lambda: ts("yy", "zz", T.yy[:], T.zz[:, 0:16], 5, None, SH),
            "od": lambda: ts("od", "zn", T.od[:], T.zn[:], 129, None, AND),
            "tn": lambda: tt("tn", "na yy", T.tn[:, 0:16], T.yy[:], T.na[:], A.is_equal),
            "pm": lambda: tt("pm", "na od", T.pm[:], T.od[:], T.na[:], A.is_lt),
            "m1": lambda: tt("m1", "pX dm", T.m1[:], T.pX[:, 16:32], T.dm[:], A.min),
            "SL": lambda: ts("SL", "m1", T.SL[:], T.m1[:], HO, None, A.add),
            "um": lambda: op("V", lambda: g.vector.tensor_reduce(T.um[:], T.pX[:, 0:16], AxisListType.X, A.max), "um", "pX"),
            "uk": lambda: ts("uk", "um", T.uk[:], T.um[:], 1.0 / 256.0, -127.5 / 256.0, A.mult, A.add),
            "of": lambda: ts(of2k, "uk um", of2, T.uk[:], -256.0, T.um[:], A.mult, A.add),
            "dc": lambda: tt("dc", cfk, T.dc[:, 1:16], T.CC[:, 32 * t + 16:32 * t + 31], T.CC[:, 32 * t + 17:32 * t + 32], A.subtract),
            "mv": lambda: tt("mv", "pm tn", T.mv[:, 1:17], T.pm[:], T.tn[:, 1:17], A.mult),
            "vv": lambda: tt("vv", "mv dc", T.vv[:], T.mv[:, 0:16], T.dc[:], A.mult),
            "D": lambda: act("D", "pEQ", T.D[:], T.pEQ[:, 0:16], scale=1.0 / BIG),
            "ub": lambda: tt("ub", "vv " + cfk, T.ub[:], T.vv[:], cf, A.add),
            "sm": lambda: tt("sm", "pZ D", T.sm[:], T.pZ[:, 0:16], T.D[:], A.mult),
            "Q": lambda: act("D", "pZ", T.D[:], T.pZ[:, 0:16], scale=1.0 / BIG),
            "sq": lambda: tt("sm", "pEQ D", T.sm[:], T.pEQ[:, 0:16], T.D[:], A.mult),
            "Z": lambda: tt("Z", "sm ub " + ofk, Zw.indirect(of), T.sm[:], T.ub[:], A.add),
            "draw": lambda: ts("cTu%d" % (t + 1), "Z " + of2k, T.cTu[:, 16 * t + 16:16 * t + 32], Zw.indirect(of2), HO + 0.25, None, A.add),
            "mark": lambda: cp("Z", "MRK " + ofk, Zw.indirect(of), T.MRK[:]),
            "zA": lambda: act("zA", "ZT L2", T.zA[:], T.ZT[:, 0:256].indirect(T.L2[:, 0:32]), F.Identity, bias=RND),
            "zB": lambda: vtr("zB", "zA", T.zB[:], T.zA[:]),
            "yr": lambda: dmas("Y", [(T.yr[:], T.R[:, 0:W])], "dyr", "", "R"),
        }
        for name in (LAST if last else LATER if t else FIRST).split():
            if name in STEP:
                STEP[name]()
            else:
                k, a, n = name.split(":")
                piece(k, int(a), int(n))

    tt("aa", "sm ub", T.aa[:], T.sm[:], T.ub[:], A.add)
    ts("mu", "aa", T.mu[:], T.aa[:], HO + 0.25, None, A.add)
    tt("Kn", IOTA + " mu MK", T.Kn[:], Iw.indirect(T.mu[:]), T.MK[:], A.mult)
    tt("SN", "Kn SN", T.SN[:], T.Kn[:], T.SN[:], A.add)
    dmas("S", [(T.ys[:], T.SN[:])], "dys", "", "SN")
    for s in cnt:
        if clock["G"].get(s, 0) < cnt[s]:
            g.wait_ge(sem[s], cnt[s])
